import numpy as np, ml_dtypes
CORES = [9,25,41,57]
N = 4
import mx_ref
BF = ml_dtypes.bfloat16
def entries(a):
    return np.ascontiguousarray(a.T).reshape(-1)
def table(e):
    return np.ascontiguousarray(np.reshape(e, (-1, 16)).T).astype(np.int32)
def pick(q, e):
    c = np.concatenate([q[0].reshape(128, -1, 4), np.zeros((128, 1, 4), np.uint8)], axis=1); s = np.concatenate([q[1], np.ones((16, 1), np.uint8)], axis=1)
    return (np.ascontiguousarray(c[:, e].reshape(128, -1)), np.ascontiguousarray(s[:, e]))
def join(*qs):
    return (np.concatenate([q[0] for q in qs], axis=1), np.concatenate([q[1] for q in qs], axis=1))
def put(q, e, v):
    c, s = q[0].reshape(128, -1, 4).copy(), q[1].copy(); c[:, e] = v[0].reshape(128, -1, 4); s[:, e] = v[1]
    return (c.reshape(128, -1), s)
def pk(c, s):
    return (np.ascontiguousarray(c), mx_ref.live(s))
def emit(q):
    return q[0], q[1]
def decode(q):
    o = []
    for b in range(4):
        e = np.zeros((128, 128, 4), np.float32); e[np.arange(128), np.arange(128), b] = 1
        o.append(mx_ref.matmul(mx_ref.quantize(e.reshape(128, 512).astype(BF)), q))
    return np.stack(o, axis=2).reshape(128, -1)
def cut(t, i, w=512):
    return t[:, w * i:w * i + w]
def f(rng, *shape):
    return mx_ref.flush((rng.standard_normal(shape, dtype=np.float32) * np.exp2(rng.integers(-2, 3, shape[:-1] + (1,)))).astype(BF))
def wide(rng, *shape, cols=0):
    v = rng.standard_normal(shape, dtype=np.float32) * np.exp2(rng.integers(-12, 13, shape)).astype(np.float32)
    if cols: v *= np.repeat(np.exp2(rng.integers(-cols, cols + 1, shape[:-2] + (1, shape[-1] // 4))) * (rng.random(shape[:-2] + (1, shape[-1] // 4)) > 0.0625), 4, axis=-1).astype(np.float32)
    return mx_ref.flush(v.astype(BF))
V, E, PAIR, CAP, R, O = 48, 192, 48, 16, 3, 3
def lift(v):
    v = np.array(v, np.float32)
    v[np.abs(v) < np.float32(2.0 ** -12)] = 0
    return v.astype(BF)
def lay(back):
    return np.stack([table(back[E * r:E * r + E]) for r in range(N)])
def links(rng):
    back = np.zeros(N * E, int)
    part = [rng.permutation(E).reshape(N, PAIR) + E * r for r in range(N)]
    for r in range(N):
        for h in range(r, N):
            a, c = part[r][h], part[h][r]
            if h == r: a, c = a[:PAIR // 2], a[PAIR // 2:]
            back[a] = c
            back[c] = a
    return lay(back)
def setup_inputs(rng):
    return {"b": lift(f(rng, N, 128, 4 * V)), "m": lift(f(rng, N, 128, 4 * E)), "u": f(rng, N, 128, 512), "w": f(rng, N, 128, 512 * O), "rev": links(rng)}
def setup_inputs_ties(rng):
    d = setup_inputs(rng)
    x = rng.integers(4, 8, (128, 1, 4)) * np.exp2(rng.integers(-2, 1, (128, 1, 4))) * rng.choice([-1.0, 1.0], (128, 1, 4))
    double = rng.permutation(N) < N // 2
    d["b"] = np.stack([np.repeat(x * (1 + double[r]), V, axis=1).reshape(128, 4 * V) for r in range(N)]).astype(np.float32).astype(BF)
    d["m"] = np.stack([np.repeat(x, E, axis=1).reshape(128, 4 * E) for r in range(N)]).astype(np.float32).astype(BF)
    return d
def setup_inputs_near(rng):
    d = setup_inputs(rng)
    p = 8 * rng.permutation(16)[:3] + rng.integers(0, 8, 3)
    t = rng.integers(0, 4, 3)
    i = np.arange(V)
    rows = [np.full(V, 32), 4 * (i % 8), 4 * (i // 8)]
    g = 1.0 - 2 * rng.integers(0, 2, N)
    b, m, u = np.array(d["b"]).reshape(N, 128, V, 4), np.array(d["m"]).reshape(N, 128, E, 4), np.array(d["u"])
    u[:, :, :4] = 0
    for k in range(3):
        b[:, p[k], :, t[k]] = np.broadcast_to(rows[k], (N, V)).astype(np.float32).astype(BF)
        m[:, p[k], :, t[k]] = 0
        u[:, p[k], t[k]] = (g * 2.0 ** (0, -19, -16)[k]).astype(np.float32).astype(BF)
    d["b"], d["m"], d["u"] = b.reshape(N, 128, 4 * V), m.reshape(N, 128, 4 * E), u
    return d
def setup_inputs_huge_order(rng):
    d = setup_inputs(rng)
    for k, n in (("b", V), ("m", E)):
        sign = np.repeat(1 - 2 * rng.integers(0, 2, (N, 1, n)), 4, axis=2)
        d[k] = ((1 + rng.random((N, 128, 4 * n))) * 2.0 ** 27 * sign).astype(np.float32).astype(BF)
    u = np.array(d["u"])
    u[:, :, :4] = ((1 + rng.random((N, 128, 4))) * 2.0 ** 29 * (1 - 2 * rng.integers(0, 2, (N, 1, 1)))).astype(np.float32).astype(BF)
    d["u"] = u
    for g in rng.permutation(16)[:2]:
        x = rng.integers(4, 8, (8, 1, 4)) * 2.0 ** 25 * rng.choice([-1.0, 1.0], (8, 1, 4))
        kind = rng.integers(-1, 2, (N, 1, E, 1))
        small = rng.integers(1, 8, (N, 8, E, 4)) * 0.25 * rng.choice([-1.0, 1.0], (N, 8, E, 4))
        nodes = x * (1 - 2 * rng.integers(0, 2, (N, 1, V, 1)))
        d["b"][:, 8 * g:8 * g + 8] = nodes.reshape(N, 8, 4 * V).astype(np.float32).astype(BF)
        d["m"][:, 8 * g:8 * g + 8] = np.where(kind == 0, small, x * kind).reshape(N, 8, 4 * E).astype(np.float32).astype(BF)
    return d
def setup_inputs_blocks(rng):
    d = setup_inputs(rng)
    spots = [np.arange(V).reshape(N, PAIR // 4)[rng.permutation(N)] + V * r for r in range(N)]
    back, keep, four = np.zeros(N * E, int), np.zeros(N * V, bool), np.arange(4)
    for r in range(N):
        for h in range(r, N):
            a, c = spots[r][h], rng.permutation(spots[h][r])
            if h == r: c = a
            for k in range(PAIR // 4):
                q = rng.permutation(4)
                if h == r:
                    back[4 * a[k] + q] = 4 * a[k] + q[[1, 0, 3, 2]]
                else:
                    back[4 * a[k] + four] = 4 * c[k] + q
                    back[4 * c[k] + q] = 4 * a[k] + four
            on = rng.integers(0, PAIR // 4)
            if (r + h) % 2 == 0:
                keep[a[on]] = True
                keep[c[on]] = True
            else:
                keep[a] = True
                keep[c] = True
    d["b"] = np.where(np.repeat(keep.reshape(N, 1, V), 4, axis=2), d["b"], np.zeros_like(d["b"]))
    d["m"] = np.where(np.repeat(keep.reshape(N, 1, V), 16, axis=2), d["m"], np.zeros_like(d["m"]))
    d["rev"] = lay(back)
    return d
def setup_inputs_spread(rng):
    d = {**setup_inputs(rng), "b": lift(wide(rng, N, 128, 4 * V, cols=6)), "m": lift(wide(rng, N, 128, 4 * E, cols=6))}
    u = np.array(d["u"])
    u[int(rng.integers(0, N)), :, :4] = 0
    return {**d, "u": u}
def check_inputs(d):
    bad = []
    for k, low, high in (("b", -12, 28), ("m", -12, 28), ("u", -30, 30), ("w", -30, 30)):
        v = np.abs(d[k].astype(np.float32))
        if not (np.isfinite(v).all() and ((v == 0) | (v >= 2.0 ** low) & (v <= 2.0 ** high)).all()): bad.append("a value of " + k)
    back = np.concatenate([entries(d["rev"][r]) for r in range(N)])
    if back.min() < 0 or back.max() >= N * E:
        bad.append("rev is out of range")
        return bad
    e = np.arange(N * E)
    if (back[back] != e).any() or (back == e).any(): bad.append("rev isn't made of pairs of different edges")
    if (np.bincount(e // E * N + back // E, minlength=N * N) != PAIR).any(): bad.append("edges of a pair of ranks")
    return bad
def reference(b, m, u, w, rev):
    y, up = np.zeros((N, 128, R * O * E), np.float32), np.zeros((N, 1, E), np.float32)
    oc, osc = np.zeros((N, 128, 4 * E), np.uint8), np.zeros((N, 16, E), np.uint8)
    back = np.concatenate([entries(rev[r]) for r in range(N)])
    e = np.arange(N * E)
    head = back // E
    others = np.array([[k for k in range(4) if k != j] for j in range(4)])
    come = back[4 * (e // 4)[:, None] + others[e % 4]]
    msg = mx_ref.quantize(np.concatenate([m[r] for r in range(N)], axis=1))
    dm = decode(msg).reshape(128, N * E, 4)
    db = decode(mx_ref.quantize(np.concatenate([b[r] for r in range(N)], axis=1))).reshape(128, N * V, 4)
    qu = [mx_ref.quantize(np.ascontiguousarray(u[r])) for r in range(N)]
    qw = [[mx_ref.quantize(np.ascontiguousarray(cut(w[r], o))) for o in range(O)] for r in range(N)]
    for t in range(R):
        z = db[:, e // 4]
        for j in range(3): z = z + dm[:, come[:, j]]
        z = z * np.float32(0.25)
        cand = mx_ref.quantize(np.ascontiguousarray(z.reshape(128, -1).astype(BF)))
        dc = decode(cand).reshape(128, N * E, 4)
        change = mx_ref.quantize(np.ascontiguousarray((dc - dm).reshape(128, -1).astype(BF)))
        taken = []
        for r in range(N):
            s = np.abs(mx_ref.matmul(qu[r], pick(change, np.arange(E * r, E * r + E)))[0]) + np.float32(0)
            for h in range(N):
                k = np.flatnonzero(head[E * r:E * r + E] == h)
                k = k[np.argsort(-s[k], kind="stable")[:CAP]]
                up[r, 0, k] += 1
                taken.append(E * r + k)
        taken = np.concatenate(taken)
        msg = put(msg, taken, pick(cand, taken))
        dm[:, taken] = dc[:, taken]
        for r in range(N):
            new = np.arange(E * r, E * r + E) if t == 0 else taken[N * CAP * r:N * CAP * r + N * CAP]
            now = pick(msg, new)
            for o in range(O):
                i = (t * O + o) * E
                if t > 0: y[r, :, i:i + E] = y[r, :, i - O * E:i - O * E + E]
                y[r][:, i + new - E * r] = mx_ref.matmul(qw[r][o], now)
    for r in range(N): oc[r], osc[r] = emit(pick(msg, np.arange(E * r, E * r + E)))
    return {"y": y, "oc": oc, "osc": osc, "up": up}

@@ -1,0 +1,401 @@
+from concourse.bass import DstId, RemoteDMATransfer
+from concourse.mybir import dt, AluOpType, AxisListType, ActivationFunctionType
+
+N, V, E, PAIR, CAP, R, O = 4, 48, 192, 48, 16, 3, 3
+X4, U8, BF, F32, I32, U16 = "float8_e4m3fn_x4", "uint8", "bfloat16", "float32", "int32", "uint16"
+MS, HR, CA, LA, XW = 0, 192, 384, 576, 720
+STEP = CA - MS
+KEYW = 256 * 3 + E
+SHIFT = 80
+NT = 21
+
+SCRATCH = {}
+
+
+def _sb(name, n, d):
+    SCRATCH[name] = ("sbuf", [128, n], d)
+
+
+def _mx(name, n):
+    _sb(name, n, X4)
+    _sb(name + "s", n, U8)
+
+
+for _n, _w, _d in (
+        ("rt", 12, I32), ("mb", 960, BF), ("ut", 512, BF), ("wt", 1536, BF),
+        ("ones", 516, BF), ("ez", 516, BF), ("ezn", 516, BF), ("seg", E, BF), ("irow", E, BF), ("erow", E, BF),
+        ("diag", E, BF), ("latch", E, BF), ("pcol", 1, I32), ("pi", 4, I32), ("pf", 4, F32), ("etab", 12, F32),
+        ("cj0", 4, F32), ("cj", 4, F32), ("rfo", 36, U16), ("occ", KEYW, BF), ("cum", KEYW, BF), ("occ2", 768, BF),
+        ("cum2", 768, BF), ("k1", 12, F32), ("k2", 12, I32), ("k3", 12, F32), ("ko", 12, U16), ("ro", 12, U16),
+        ("gm", E, BF), ("gs", E, BF), ("so", 12, U16), ("invb", E, BF), ("invs", E, BF), ("iof", 12, U16),
+        ("b1", 12, F32), ("b2", 12, I32), ("bo", 12, U16), ("rb", E, BF), ("rf", 3 * E, BF), ("am", 3 * E, BF),
+        ("asc", 3 * E, BF), ("ao", 36, U16), ("ub", 512, BF), ("sel", 512, BF), ("xt", 512, BF), ("th", E, BF),
+        ("krow", NT, F32), ("kk", 2 * NT, F32), ("wc", LA, BF), ("acc", E, F32), ("upo", E, F32),
+        ("zt", 4 * E, BF), ("yt", 4 * E, BF), ("dd", E, F32), ("nc", 2, F32), ("sg", E, BF), ("gt", E, BF),
+        ("cnt", 2, F32)):
+    _sb(_n, _w, _d)
+for _n, _w in (("qm", 240), ("qe", 512), ("qn", 512), ("qu", 128), ("qw", 384), ("qs", 128), ("qb", E), ("qy", E),
+               ("qx", 128), ("x0", XW), ("x1", XW), ("x2", LA), ("x3", E)):
+    _mx(_n, _w)
+for _t in range(R):
+    _mx("qa%d" % _t, 3 * E)
+    _mx("qo%d" % _t, E)
+    _sb("yb%d" % _t, O * E, F32)
+    _sb("off%d" % _t, 24, U16)
+for _t in range(R - 1):
+    _sb("lo%d" % _t, 16, U16)
+SCRATCH["pz"] = ("psum", [128, 2048], F32)
+SCRATCH["py"] = ("psum", [128, 2048], F32)
+
+SEMAPHORES = ["cv", "cs", "cp", "cg", "ldr", "ldm", "ldu", "ldw", "st", "sent", "ad0", "ad1", "ad2", "af0", "af1"]
+
+
+def rank_program(g, core, T, topo):
+    r = T.rank_of(core)
+    if r is None:
+        return
+    A, ACT = AluOpType, ActivationFunctionType
+    Q = {"v": g.vector, "s": g.scalar, "p": g.tensor, "g": g, "y": g.sync}
+    SEM = {"v": "cv", "s": "cs", "p": "cp", "g": "cg"}
+    count = {"cv": 0, "cs": 0, "cp": 0, "cg": 0, "st": 0, "sent": 0}
+    known = {q: {} for q in Q}
+    wrote, readers = {}, {}
+
+    def settle(q, reads, writes):
+        need = []
+        for k in reads:
+            if k in wrote:
+                need.append(wrote[k])
+        for k in writes:
+            bank = k[:2] in ("pz", "py")
+            for tok in ([wrote[k]] if k in wrote else []) + readers.get(k, []):
+                if not (bank and q == "p" and tok[0] == "cp"):
+                    need.append(tok)
+        need = [t for t in need if known[q].get(t[0], 0) < t[1]]
+        top = {}
+        for t in need:
+            if t[0] not in top or top[t[0]][1] < t[1]:
+                top[t[0]] = t
+        for s in sorted(top):
+            t = top[s]
+            if any(o[2].get(s, 0) >= t[1] for o in top.values() if o is not t):
+                continue
+            Q[q].wait_ge(T.sem[s], t[1])
+        for t in top.values():
+            for s, c in list(t[2].items()) + [(t[0], t[1])]:
+                if known[q].get(s, 0) < c:
+                    known[q][s] = c
+
+    def note(tok, reads, writes):
+        for k in reads:
+            readers.setdefault(k, []).append(tok)
+        for k in writes:
+            wrote[k] = tok
+            readers[k] = []
+
+    def op(q, reads, writes, call):
+        writes = list(writes) + [k for k in reads if k[:2] in ("pz", "py")]
+        settle(q, reads, writes)
+        s = SEM[q]
+        count[s] += 1
+        call().then_inc(T.sem[s], 1)
+        note((s, count[s], dict(known[q])), reads, writes)
+
+    def load(q, sem, out, in_):
+        Q[q].dma_start(out, in_).then_inc(T.sem[sem], 16)
+
+    def store(q, reads, out, in_):
+        settle(q, reads, [])
+        count["st"] += 16
+        Q[q].dma_start(out, in_).then_inc(T.sem.st, 16)
+
+    vec, sca, pe = g.vector, g.scalar, g.tensor
+
+    def ts(out, in0, s1, s2, op0, op1=None):
+        if op1 is None:
+            return lambda: vec.tensor_scalar(out, in0, s1, None, op0)
+        return lambda: vec.tensor_scalar(out, in0, s1, s2, op0, op1)
+
+    def act(out, in_, func=None, **kw):
+        return lambda: sca.activation(out, in_, ACT.Copy if func is None else func, **kw)
+
+    def scan(out, d0, d1, first, op0, op1):
+        return lambda: vec.tensor_tensor_scan(out, d0, d1, first, op0, op1)
+
+    def iota(out, pattern, base):
+        return lambda: g.iota(out, pattern, base, 0, allow_small_or_imprecise_dtypes=True)
+
+    def quant(name, a, b, tile, reads, key):
+        op("v", reads, [key, key + "s"], lambda: vec.quantize_mx(T[name][:, a:b], T[name + "s"][:, a:b], tile))
+
+    def pick_codes(dst, c, d, dkey, src, a, b, skeys, off, okeys):
+        op("v", skeys + okeys, [dkey], lambda: vec.tensor_copy(
+            T[dst][:, c:d].bitcast(dt.uint32), T[src][:, a:b].bitcast(dt.uint32).indirect(off)))
+
+    def pick_scales(dst, c, d, dkey, src, a, b, skeys, off, okeys):
+        op("s", [k + "s" for k in skeys] + okeys, [dkey + "s"], act(T[dst + "s"][:, c:d], T[src + "s"][:, a:b].indirect(off)))
+
+    def pick(*a):
+        pick_codes(*a)
+        pick_scales(*a)
+
+    def mm(bank, b, n, lname, la, lkey, rname, ra, rkey, start, stop):
+        op("p", [lkey, lkey + "s", rkey, rkey + "s"], ["%s%d" % (bank, b)], lambda: pe.matmul_mx(
+            T[bank][:, 512 * b:512 * b + n], T[lname][:, la:la + 128], T[lname + "s"][:, la:la + 128],
+            T[rname][:, ra:ra + n], T[rname + "s"][:, ra:ra + n], start, stop))
+
+    others = [(r + d) % N for d in range(1, N)]
+
+    def blk(src, dst):
+        return src if src < dst else src - 1
+
+    def dest(h):
+        rid, pid, _ = topo.addr(T.cores[h])
+        return DstId(rid=rid, pnc=pid)
+
+    def masks(src, first):
+        out = []
+        for i in range(N - 1):
+            eng = topo.engines(T.cores[src], T.cores[(src + 1 + i) % N])
+            n = len(eng)
+            part = [eng[:n // 2], eng[n // 2:3 * n // 4], eng[3 * n // 4:]] if first else \
+                   [eng[n // 2:], eng[:n // 4], eng[n // 4:n // 2]]
+            out.append(part[i])
+        return out
+
+    def send(reads, sem, first, pairs):
+        settle("g", reads, [])
+        ms = masks(r, first)
+        count["sent"] += sum(len(m) for m in ms)
+        g.remote_dma_fused([RemoteDMATransfer(dst_ids=[dest(h)], dma_engine_mask=sum(1 << e for e in ms[i]),
+                                              remote_sem=T.sem[sem], src=pairs[i][0], dst=pairs[i][1])
+                            for i, h in enumerate(others)], local_sem=T.sem.sent)
+
+    def arriving(firsts):
+        return sum(len(masks(s, f)[(r - s - 1) % N]) for s in others for f in firsts)
+
+    def send_block(name, a, z, key, sem):
+        c, s = T[name], T[name + "s"]
+        at = [(a + PAIR * h, z + PAIR * blk(r, h)) for h in others]
+        send([key], sem, True, [(c[:, i:i + PAIR].bitcast(dt.uint8), c[:, j:j + PAIR].bitcast(dt.uint8)) for i, j in at])
+        send([key + "s"], sem, False, [(s[:, i:i + PAIR], s[:, j:j + PAIR]) for i, j in at])
+
+    def landed(keys, sem, n):
+        for k in keys:
+            wrote[k] = (sem, n, {})
+
+    for k in range(4):
+        load("y", "ldr", T.rt[32 * k:32 * k + 16, :], T.rev[:])
+        load("s", "ldr", T.rt[32 * k + 16:32 * k + 32, :], T.rev[:])
+    load("y", "ldm", T.mb[:, 0:4 * E], T.m[:])
+    load("s", "ldm", T.mb[:, 4 * E:4 * E + 4 * V], T.b[:])
+    load("y", "ldu", T.ut[:], T.u[:])
+    load("y", "ldw", T.wt[:], T.w[:])
+    landed(["rt"], "ldr", 128)
+    landed(["mb"], "ldm", 32)
+    landed(["ut"], "ldu", 16)
+    landed(["wt"], "ldw", 16)
+
+    ones = T.ones
+    op("g", [], ["pcol"], lambda: g.iota(T.pcol[:], [[0, 1]], 0, 1))
+    op("v", [], ["ones"], lambda: vec.memset(ones[:], 1.0))
+    op("v", [], ["seg"], lambda: vec.memset(T.seg[:], 1.0))
+    op("g", ["ones"], ["ez"], lambda: g.affine_select(T.ez[:], ones[:], [[1, 516]], A.is_equal, 0.0, -3, -4))
+    op("s", ["ones"], ["occa"], act(T.occ[:, 0:480], ones[:, 0:480], scale=0.0))
+    op("s", ["ones"], ["occb"], act(T.occ[:, 480:960], ones[:, 0:480], scale=0.0))
+    op("s", ["ones"], ["xt0", "xt1", "xtc"], act(T.xt[:], ones[:, 0:512], scale=0.0))
+    op("s", ["ones"], ["invb"], act(T.invb[:], ones[:, 0:E]))
+    op("s", ["ones"], ["occ2a"], act(T.occ2[:, 0:384], ones[:, 0:384], scale=0.0))
+    op("s", ["ones"], ["occ2b"], act(T.occ2[:, 384:768], ones[:, 0:384], scale=0.0))
+    op("s", ["ones"], ["th"], act(T.th[:], ones[:, 0:E], scale=0.5))
+    for i, (s1, o) in enumerate(((15, A.bitwise_and), (3, A.bitwise_and), (12, A.bitwise_and), (4, A.arith_shift_right))):
+        op("v", ["pcol"], ["pi%d" % i], ts(T.pi[:, i:i + 1], T.pcol[:], s1, None, o))
+    op("v", [], ["seg"], lambda: vec.memset(T.seg[:, 0:E:16], 0.0))
+    op("v", ["ones"], ["erow"], scan(T.erow[:], ones[:, 0:E], ones[:, 0:E], -1.0, A.mult, A.add))
+    op("v", ["pi0", "pi1", "pi2", "pi3"], ["pf"], lambda: vec.tensor_copy(T.pf[:], T.pi[:]))
+    op("v", ["seg"], ["irow"], scan(T.irow[:], T.seg[:], T.seg[:], 0.0, A.mult, A.add))
+    q16, a4, q12, g16 = T.pf[:, 0:1], T.pf[:, 1:2], T.pf[:, 2:3], T.pf[:, 3:4]
+    op("v", ["erow", "pf"], ["etab"], ts(T.etab[:], T.erow[:, 0:E:16], q16, 1.0 / 256, A.add, A.mult))
+    op("v", ["erow", "pf"], ["cj0"], ts(T.cj0[:], T.erow[:, 0:4], a4, q12, A.is_ge, A.add))
+    op("v", ["irow", "pf"], ["diag"], ts(T.diag[:], T.irow[:], q16, None, A.is_equal))
+    op("v", ["irow", "pf"], ["latch"], ts(T.latch[:], T.irow[:], q16, 256.0, A.is_equal, A.mult))
+    op("v", ["cj0", "erow"], ["cj"], lambda: vec.tensor_tensor(T.cj[:], T.cj0[:], T.erow[:, 0:4], A.add))
+    op("s", ["ez"], ["ezn"], act(T.ezn[:], T.ez[:], scale=-1.0))
+    for t in range(2):
+        op("s", ["diag"], ["sel%d" % t], act(T.sel[:, t:512:4], T.diag[:, 0:128], scale=float(STEP)))
+    op("s", ["irow"], ["sel2"], act(T.sel[:, 2:512:4], T.irow[:, 0:128]))
+    op("s", ["ones"], ["sel3"], act(T.sel[:, 3:512:4], ones[:, 0:128]))
+    op("g", [], ["krow"], iota(T.krow[:, 0:12], [[1, 12]], 0))
+    op("g", ["xtc"], ["xtc3"], iota(T.xt[0:1, 2:4 * NT:4], [[0, NT]], 1))
+    op("g", ["xtc"], ["xtc4"], iota(T.xt[0:1, 3:48:4], [[16, 12]], 0))
+    for i, h in enumerate(others):
+        op("g", [], ["krow%d" % i], iota(T.krow[:, 12 + 3 * i:15 + 3 * i], [[1, 3]], 3 * h))
+        op("g", ["xtc"], ["xtc%d" % i], iota(T.xt[0:1, 51 + 12 * i:60 + 12 * i:4], [[16, 3]], PAIR * blk(r, h)))
+
+    op("v", ["rt"], ["k1"], ts(T.k1[:], T.rt[:], -(E - 1) / 2.0, 1.0 / E, A.add, A.mult))
+    op("v", ["rt"], ["ro"], lambda: vec.tensor_copy(T.ro[:], T.rt[:]))
+    op("v", ["k1"], ["k2"], lambda: vec.tensor_copy(T.k2[:], T.k1[:]))
+    op("v", ["k2", "etab"], ["k3"], lambda: vec.tensor_tensor(T.k3[:], T.k2[:], T.etab[:], A.add))
+    op("v", ["k3"], ["ko"], ts(T.ko[:], T.k3[:], 256.0, None, A.mult))
+    op("v", ["ko", "ones"], ["occa", "occb"], lambda: vec.tensor_copy(T.occ[:, 0:KEYW].indirect(T.ko[:, 0:12]), ones[:, 0:E]))
+    op("v", ["occa", "occb"], ["cum"], scan(T.cum[:], T.occ[:], T.occ[:], 0.0, A.add, A.max))
+    op("v", ["cum", "ko", "diag"], ["gm"], lambda: vec.tensor_tensor(T.gm[:], T.cum[:, 0:KEYW].indirect(T.ko[:, 0:12]), T.diag[:], A.mult))
+    op("v", ["gm", "seg"], ["gs"], scan(T.gs[:], T.seg[:], T.gm[:], 0.0, A.mult, A.add))
+    op("v", ["gs"], ["so"], ts(T.so[:], T.gs[:, 15:E:16], -1.0, None, A.add))
+    op("v", ["so", "erow"], ["invb"], lambda: vec.tensor_copy(T.invb[:, 0:E].indirect(T.so[:, 0:12]), T.erow[:]))
+    quant("qm", 0, 240, T.mb[:], ["mb"], "qm")
+    op("v", ["invb", "latch"], ["invs"], scan(T.invs[:], T.latch[:], T.invb[:], 0.0, A.max, A.min))
+    op("v", ["invs"], ["iof"], lambda: vec.tensor_copy(T.iof[:], T.invs[:, 15:E:16]))
+    pick("x0", MS, MS + E, "x0m", "qm", 0, 240, ["qm"], T.iof[:, 0:12], ["iof"])
+    send_block("x0", MS, HR, "x0m", "ad0")
+    landed(["x0h", "x0hs"], "ad0", arriving((True, False)))
+
+    op("v", ["ro", "ones"], ["occ2a", "occ2b"], lambda: vec.tensor_copy(T.occ2[:, 0:768].indirect(T.ro[:, 0:12]), ones[:, 0:E]))
+    for j in range(3):
+        op("v", ["erow", "cj"], ["rfo%d" % j], ts(T.rfo[:, 12 * j:12 * j + 12], T.erow[:, 0:E:16], T.cj[:, j:j + 1], None, A.add))
+    for h in range(N):
+        first = (MS + PAIR * h if h == r else HR + PAIR * blk(h, r)) - SHIFT - 1
+        op("v", ["occ2a", "occ2b", "ones"], ["cum2%d" % h],
+           scan(T.cum2[:, E * h:E * h + E], ones[:, 0:E], T.occ2[:, E * h:E * h + E], float(first), A.mult, A.add))
+    op("s", ["cum2%d" % h for h in range(N)] + ["ro"], ["rb"], act(T.rb[:], T.cum2[:, 0:768].indirect(T.ro[:, 0:12])))
+    for j in range(3):
+        op("s", ["rb", "rfo%d" % j], ["rf%d" % j], act(T.rf[:, E * j:E * j + E], T.rb[:, 0:E].indirect(T.rfo[:, 12 * j:12 * j + 12])))
+    op("v", ["invs"], ["b1"], ts(T.b1[:], T.invs[:, 15:E:16], 0.25, E - 0.375, A.mult, A.add))
+    quant("qe", 0, 128, T.ez[:, 3:515], ["ez"], "qe0")
+    op("v", ["b1"], ["b2"], lambda: vec.tensor_copy(T.b2[:], T.b1[:]))
+    quant("qe", 128, 256, T.ez[:, 2:514], ["ez"], "qe1")
+    op("v", ["b2"], ["bo"], lambda: vec.tensor_copy(T.bo[:], T.b2[:]))
+    quant("qe", 256, 384, T.ez[:, 1:513], ["ez"], "qe2")
+    nodes = ("qb", 0, E, "qb", "qm", 0, 240, ["qm"], T.bo[:, 0:12], ["bo"])
+    pick_codes(*nodes)
+    for j in range(3):
+        op("v", ["rf%d" % j, "iof", "diag"], ["am%d" % j], lambda j=j: vec.tensor_tensor(
+            T.am[:, E * j:E * j + E], T.rf[:, E * j:E * j + E].indirect(T.iof[:, 0:12]), T.diag[:], A.mult))
+    pick_scales(*nodes)
+    for j in range(3):
+        op("v", ["am%d" % j, "seg"], ["asc%d" % j], scan(T.asc[:, E * j:E * j + E], T.seg[:], T.am[:, E * j:E * j + E], 0.0, A.mult, A.add))
+    quant("qe", 384, 512, T.ez[:, 0:512], ["ez"], "qe3")
+    op("v", ["asc0", "asc1", "asc2"], ["ao"], ts(T.ao[:], T.asc[:, 15:3 * E:16], float(SHIFT), None, A.add))
+    for t in range(4):
+        op("s", ["ut", "ones"], ["ub%d" % t], act(T.ub[:, t:512:4], ones[:, 0:128], ACT.Identity, bias=T.ut[:, t:t + 1], scale=0.0))
+
+    def select(a, n, step, fill, base, mult):
+        op("g", ["th"], ["th"], lambda: g.affine_select(T.th[:, a:a + n], T.th[:, a:a + n], [[step, n]], A.is_ge, fill, base, mult))
+
+    for t in range(2):
+        c0, p0 = 96 * t, 64 * t
+        select(c0, 96, 1, -0.5, c0 - p0, -1)
+        select(c0, PAIR, 0, 2.0, c0 + PAIR - 1 - p0, -1)
+        select(c0 + PAIR, PAIR, 0, 2.0, p0 - c0 - PAIR, 1)
+
+    def node_terms():
+        for b in range(4):
+            mm("pz", b, E, "qe", 128 * b, "qe%d" % b, "qb", 0, "qb", True, False)
+
+    def minus_held(t):
+        for b in range(4):
+            mm("py", b, E, "qn", 128 * b, "qn%d" % b, "x%d" % t, MS, "x%dm" % t, True, False)
+
+    def to_tile(tile, bank, scale):
+        for b in range(4):
+            src, dst = T[bank][:, 512 * b:512 * b + E], T[tile][:, b:4 * E:4]
+            if b % 2 == 0:
+                op("s", ["%s%d" % (bank, b)], ["%s%d" % (tile, b)], act(dst, src, scale=scale))
+            else:
+                op("v", ["%s%d" % (bank, b)], ["%s%d" % (tile, b)], ts(dst, src, scale, None, A.mult))
+
+    node_terms()
+    for t in range(R):
+        x, nx, qa, qo, yb, off = "x%d" % t, "x%d" % (t + 1), "qa%d" % t, "qo%d" % t, "yb%d" % t, T["off%d" % t]
+        last = t == R - 1
+        if t > 0:
+            px = "x%d" % (t - 1)
+            pick(x, HR, HR + 3 * PAIR, x + "h", px, HR, XW, [px + "h", px + "c", px + "l"], T["lo%d" % (t - 1)][:, 0:9], ["lo%d" % (t - 1)])
+        for j in range(3):
+            pick(qa, E * j, E * j + E, "%s_%d" % (qa, j), x, 0, HR + 3 * PAIR, [x + "m", x + "h"], T.ao[:, 12 * j:12 * j + 12], ["ao"])
+            for b in range(4):
+                mm("pz", b, E, "qe", 128 * b, "qe%d" % b, qa, E * j, "%s_%d" % (qa, j), False, j == 2)
+        if t == 0:
+            for b in range(4):
+                quant("qn", 128 * b, 128 * b + 128, T.ezn[:, 3 - b:515 - b], ["ezn"], "qn%d" % b)
+            minus_held(0)
+        to_tile("zt", "pz", 0.25)
+        quant(x, CA, CA + E, T.zt[:], ["zt0", "zt1", "zt2", "zt3"], x + "c")
+        if not last:
+            send_block(x, CA, LA, x + "c", "ad%d" % (t + 1))
+            landed([x + "l", x + "ls"], "ad%d" % (t + 1), arriving((True, False)))
+        for b in range(4):
+            mm("py", b, E, "qe", 128 * b, "qe%d" % b, x, CA, x + "c", False, True)
+        if t == 0:
+            quant("qu", 0, 128, T.ub[:], ["ub0", "ub1", "ub2", "ub3"], "qu")
+            for s in range(2):
+                op("v", ["krow", "krow0", "krow1", "krow2", "pf"], ["kk%d" % s],
+                   ts(T.kk[:, NT * s:NT * s + NT], T.krow[:], -4.0 * s, g16, A.add, A.is_equal))
+        to_tile("yt", "py", 1.0)
+        quant("qy", 0, E, T.yt[:], ["yt0", "yt1", "yt2", "yt3"], "qy")
+        mm("pz", 0, E, "qu", 0, "qu", "qy", 0, "qy", True, True)
+        mm("pz", 1, 128, "qy", 0, "qy", "qu", 0, "qu", True, True)
+        mm("pz", 2, 128, "qy", 64, "qy", "qu", 0, "qu", True, True)
+        if t == 0:
+            op("v", [], ["kk0"], lambda: vec.memset(T.kk[96:128, 0:NT], 0.0))
+            op("v", [], ["kk1"], lambda: vec.memset(T.kk[0:32, NT:2 * NT], 0.0))
+        for s in range(2):
+            op("v", ["pz%d" % (1 + s)], ["nc%d" % s], lambda s=s: vec.tensor_reduce(
+                T.nc[:, s:s + 1], T.pz[:, 512 * (1 + s):512 * (1 + s) + 1], AxisListType.X, A.max, negate=True, apply_absolute_value=True))
+        if t == 0:
+            quant("qs", 0, 128, T.sel[:], ["sel0", "sel1", "sel2", "sel3"], "qs")
+        for s in range(2):
+            a = slice(96 * s, 96 * s + 96)
+            op("s", ["pz0"], ["dd%d" % s], act(T.dd[:, a], T.pz[:, a], ACT.Abs))
+            op("s", ["dd%d" % s, "nc%d" % s], ["sg%d" % s], act(T.sg[:, a], T.dd[:, a], ACT.Sign, bias=T.nc[:, s:s + 1]))
+        for s in range(2):
+            a = slice(96 * s, 96 * s + 96)
+            op("v", ["sg%d" % s, "th"], ["gt%d" % s], lambda a=a: vec.tensor_tensor(T.gt[:, a], T.sg[:, a], T.th[:, a], A.is_gt))
+        op("s", ["gt0"], ["cnt0", "sg0"], act(T.sg[:, 0:96], T.gt[:, 0:96], accum_out=T.cnt[:, 0:1]))
+        op("v", ["gt1"], ["cnt1"], lambda: vec.tensor_reduce(T.cnt[:, 1:2], T.gt[:, 96:E], AxisListType.X, A.add))
+        for s in range(2):
+            op("v", ["cnt%d" % s, "kk%d" % s], ["xt%d" % s],
+               ts(T.xt[:, s:4 * NT:4], T.kk[:, NT * s:NT * s + NT], float(CAP), T.cnt[:, s:s + 1], A.mult, A.is_gt))
+        quant("qx", 0, 128, T.xt[:], ["xt0", "xt1", "xtc", "xtc0", "xtc1", "xtc2", "xtc3", "xtc4"], "qx")
+        mm("pz", 3, 128, "qs", 0, "qs", "qx", 0, "qx", True, True)
+        op("v", ["pz3"], ["off%d" % t], lambda off=off: vec.tensor_copy(off[:, 0:NT], T.pz[:, 1536:1536 + NT]))
+        if not last:
+            lo = T["lo%d" % t]
+            send(["off%d" % t], "af%d" % t, True,
+                 [(off[:, 12 + 3 * i:15 + 3 * i], lo[:, 3 * blk(r, h):3 * blk(r, h) + 3]) for i, h in enumerate(others)])
+            landed(["lo%d" % t], "af%d" % t, arriving((True,)))
+            node_terms()
+        pick(nx, MS, MS + E, nx + "m", x, 0, LA, [x + "m", x + "h", x + "c"], off[:, 0:12], ["off%d" % t])
+        pick(qo, 0, E, qo, nx, MS, MS + E, [nx + "m"], T.so[:, 0:12], ["so"])
+        if t == 0:
+            quant("qw", 0, 128 * O, T.wt[:], ["wt"], "qw")
+            op("s", ["ones"], ["wca"], act(T.wc[:, 0:CA], ones[:, 0:CA], scale=0.0))
+            op("s", ["ones"], ["wcb"], act(T.wc[:, CA:LA], ones[:, 0:E]))
+        for o in range(O):
+            mm("py", o, E, "qw", 128 * o, "qw", qo, 0, qo, True, True)
+        if last:
+            store("y", [qo], T.oc[:], T[qo][:, 0:E].bitcast(dt.uint8))
+            for k in range(4):
+                store("y", [qo + "s"], T.osc[4 * k:4 * k + 4, :], T[qo + "s"][32 * k:32 * k + 4, :])
+        flags = T.wc[:, 0:LA].indirect(off[:, 0:12])
+        if t > 0:
+            op("v", ["wca", "wcb", "off%d" % t, "acc"], ["acc"], lambda flags=flags: vec.tensor_tensor(T.acc[:], flags, T.acc[:], A.add))
+        for o in range(O):
+            src, dst = T.py[:, 512 * o:512 * o + E], T[yb][:, E * o:E * o + E]
+            if o == 1 and t != 1:
+                op("v", ["py%d" % o], ["%s_%d" % (yb, o)], lambda src=src, dst=dst: vec.tensor_copy(dst, src))
+            else:
+                op("s", ["py%d" % o], ["%s_%d" % (yb, o)], act(dst, src))
+            if last:
+                store("y", ["%s_%d" % (yb, o)], T.y[:, (t * O + o) * E:(t * O + o + 1) * E], dst)
+        if t == 0:
+            op("v", ["wca", "wcb", "off0"], ["acc"], lambda flags=flags: vec.tensor_copy(T.acc[:], flags))
+        if last:
+            op("v", ["acc", "so"], ["upo"], lambda: vec.tensor_copy(T.upo[:], T.acc[:, 0:E].indirect(T.so[:, 0:12])))
+            store("s", ["upo"], T.up[:], T.upo[0:1, :])
+        else:
+            store("y", ["%s_%d" % (yb, o) for o in range(O)] + ["lo%d" % t], T.y[:, t * O * E:(t + 1) * O * E], T[yb][:])
+            minus_held(t + 1)
+
+    for s in ("cv", "cs", "cp", "cg", "sent", "st"):
+        g.wait_ge(T.sem[s], count[s])

@@ -5,7 +5,9 @@ N, V, E, PAIR, CAP, R, O = 4, 48, 192, 48, 16, 3, 3
 X4, U8, BF, F32, I32, U16 = "float8_e4m3fn_x4", "uint8", "bfloat16", "float32", "int32", "uint16"
 MS, HR, CA, LA, XW = 0, 192, 384, 576, 720
 STEP = CA - MS
-KEYW = 256 * 3 + E
+BASE = 64
+YW = E + 32
+OFFK = 64.0
 SHIFT = 80
 NT = 21
 
@@ -22,24 +24,25 @@ def _mx(name, n):
 
 
 for _n, _w, _d in (
-        ("rt", 12, I32), ("mb", 960, BF), ("ut", 512, BF), ("wt", 1536, BF),
+        ("rt", 12, I32), ("mb", 1024, BF), ("ut", 512, BF), ("wt", 1536, BF),
         ("ones", 516, BF), ("ez", 516, BF), ("ezn", 516, BF), ("seg", E, BF), ("irow", E, BF), ("erow", E, BF),
-        ("diag", E, BF), ("latch", E, BF), ("pcol", 1, I32), ("pi", 4, I32), ("pf", 4, F32), ("etab", 12, F32),
-        ("cj0", 4, F32), ("cj", 4, F32), ("rfo", 36, U16), ("occ", KEYW, BF), ("cum", KEYW, BF), ("occ2", 768, BF),
-        ("cum2", 768, BF), ("k1", 12, F32), ("k2", 12, I32), ("k3", 12, F32), ("ko", 12, U16), ("ro", 12, U16),
-        ("gm", E, BF), ("gs", E, BF), ("so", 12, U16), ("invb", E, BF), ("invs", E, BF), ("iof", 12, U16),
-        ("b1", 12, F32), ("b2", 12, I32), ("bo", 12, U16), ("rb", E, BF), ("rf", 3 * E, BF), ("am", 3 * E, BF),
-        ("asc", 3 * E, BF), ("ao", 36, U16), ("ub", 512, BF), ("sel", 512, BF), ("xt", 512, BF), ("th", E, BF),
-        ("krow", NT, F32), ("kk", 2 * NT, F32), ("wc", LA, BF), ("acc", E, F32), ("upo", E, F32),
-        ("zt", 4 * E, BF), ("yt", 4 * E, BF), ("dd", E, F32), ("nc", 2, F32), ("sg", E, BF), ("gt", E, BF),
-        ("cnt", 2, F32)):
+        ("diag", E, BF), ("latch", E, BF), ("pcol", 1, I32), ("pi", 4, I32), ("pf", 4, F32), ("gk", 36, F32),
+        ("cj0", 4, F32), ("cj", 4, F32), ("rfo", 36, U16), ("wtab", N * E, BF), ("cum", E, F32), ("occ2", 768, BF),
+        ("cum2", 768, BF), ("k2", 12, I32), ("w12", 12, F32), ("winv", 24, F32), ("ro", 12, U16),
+        ("wrow", E, BF), ("lat", E, F32), ("nh", 24, I32), ("b48", 12, F32), ("f1", 24, F32), ("f2", 12, F32),
+        ("so", 12, U16), ("invb", E, BF), ("invs", E, BF), ("iof", 12, U16),
+        ("b2", 12, I32), ("bo", 12, U16), ("rb", E, BF), ("rf", 3 * E, BF), ("am", 3 * E, BF),
+        ("asc", 3 * E, BF), ("ao", 36, U16), ("ub", 704, BF), ("sel", 512, BF), ("xt", 512, BF), ("flip", PAIR, BF),
+        ("krow", NT, F32), ("k01", 2 * NT, F32), ("kk", 2 * NT, F32), ("wc", LA, BF), ("acc", E, F32), ("upo", E, F32),
+        ("zt", 4 * E, BF), ("yt", 4 * YW, BF), ("dd", 144, F32), ("nc", 2, F32), ("sg", 96, BF), ("eq", 96, BF),
+        ("tie", 96, F32), ("cnt", 2, F32), ("hrow", E, BF), ("lh", 2 * E, BF), ("lhd", 2 * E, BF), ("lhc", 4, F32),
+        ("sele", 512, BF), ("k01e", 24, F32), ("kke", 24, F32), ("upe", E, F32)):
     _sb(_n, _w, _d)
-for _n, _w in (("qm", 240), ("qe", 512), ("qn", 512), ("qu", 128), ("qw", 384), ("qs", 128), ("qb", E), ("qy", E),
-               ("qx", 128), ("x0", XW), ("x1", XW), ("x2", LA), ("x3", E)):
+for _n, _w in (("qm", 256), ("qe", 512), ("qn", 512), ("qu", 176), ("qw", 384), ("qs", 128), ("qb", E), ("qy", YW),
+               ("qx", 128), ("x0", XW), ("x1", XW), ("x2", LA), ("qo0", E), ("qo1", LA), ("qo2", E), ("qse", 128)):
     _mx(_n, _w)
 for _t in range(R):
     _mx("qa%d" % _t, 3 * E)
-    _mx("qo%d" % _t, E)
     _sb("yb%d" % _t, O * E, F32)
     _sb("off%d" % _t, 24, U16)
 for _t in range(R - 1):
@@ -115,6 +118,9 @@ def rank_program(g, core, T, topo):
         if op1 is None:
             return lambda: vec.tensor_scalar(out, in0, s1, None, op0)
         return lambda: vec.tensor_scalar(out, in0, s1, s2, op0, op1)
+
+    def tt(out, in0, in1, o):
+        return lambda: vec.tensor_tensor(out, in0, in1, o)
 
     def act(out, in_, func=None, **kw):
         return lambda: sca.activation(out, in_, ACT.Copy if func is None else func, **kw)
@@ -201,13 +207,9 @@ def rank_program(g, core, T, topo):
     op("v", [], ["ones"], lambda: vec.memset(ones[:], 1.0))
     op("v", [], ["seg"], lambda: vec.memset(T.seg[:], 1.0))
     op("g", ["ones"], ["ez"], lambda: g.affine_select(T.ez[:], ones[:], [[1, 516]], A.is_equal, 0.0, -3, -4))
-    op("s", ["ones"], ["occa"], act(T.occ[:, 0:480], ones[:, 0:480], scale=0.0))
-    op("s", ["ones"], ["occb"], act(T.occ[:, 480:960], ones[:, 0:480], scale=0.0))
-    op("s", ["ones"], ["xt0", "xt1", "xtc"], act(T.xt[:], ones[:, 0:512], scale=0.0))
+    for h in range(N):
+        op("s", ["ones"], ["wtab%d" % h], act(T.wtab[:, E * h:E * h + E], ones[:, 0:E], scale=float(BASE ** h)))
     op("s", ["ones"], ["invb"], act(T.invb[:], ones[:, 0:E]))
-    op("s", ["ones"], ["occ2a"], act(T.occ2[:, 0:384], ones[:, 0:384], scale=0.0))
-    op("s", ["ones"], ["occ2b"], act(T.occ2[:, 384:768], ones[:, 0:384], scale=0.0))
-    op("s", ["ones"], ["th"], act(T.th[:], ones[:, 0:E], scale=0.5))
     for i, (s1, o) in enumerate(((15, A.bitwise_and), (3, A.bitwise_and), (12, A.bitwise_and), (4, A.arith_shift_right))):
         op("v", ["pcol"], ["pi%d" % i], ts(T.pi[:, i:i + 1], T.pcol[:], s1, None, o))
     op("v", [], ["seg"], lambda: vec.memset(T.seg[:, 0:E:16], 0.0))
@@ -215,78 +217,111 @@ def rank_program(g, core, T, topo):
     op("v", ["pi0", "pi1", "pi2", "pi3"], ["pf"], lambda: vec.tensor_copy(T.pf[:], T.pi[:]))
     op("v", ["seg"], ["irow"], scan(T.irow[:], T.seg[:], T.seg[:], 0.0, A.mult, A.add))
     q16, a4, q12, g16 = T.pf[:, 0:1], T.pf[:, 1:2], T.pf[:, 2:3], T.pf[:, 3:4]
-    op("v", ["erow", "pf"], ["etab"], ts(T.etab[:], T.erow[:, 0:E:16], q16, 1.0 / 256, A.add, A.mult))
     op("v", ["erow", "pf"], ["cj0"], ts(T.cj0[:], T.erow[:, 0:4], a4, q12, A.is_ge, A.add))
     op("v", ["irow", "pf"], ["diag"], ts(T.diag[:], T.irow[:], q16, None, A.is_equal))
-    op("v", ["irow", "pf"], ["latch"], ts(T.latch[:], T.irow[:], q16, 256.0, A.is_equal, A.mult))
-    op("v", ["cj0", "erow"], ["cj"], lambda: vec.tensor_tensor(T.cj[:], T.cj0[:], T.erow[:, 0:4], A.add))
+    op("v", ["cj0", "erow"], ["cj"], tt(T.cj[:], T.cj0[:], T.erow[:, 0:4], A.add))
+    op("v", ["diag"], ["latch"], ts(T.latch[:], T.diag[:], 2.0 ** 27, -2.0 ** 26, A.mult, A.add))
+
+    op("v", ["rt"], ["ro"], lambda: vec.tensor_copy(T.ro[:], T.rt[:]))
+    op("s", ["ro"] + ["wtab%d" % h for h in range(N)], ["wrow"], act(T.wrow[:], T.wtab[:, 0:N * E].indirect(T.ro[:, 0:12])))
+
+    op("s", ["ones"], ["mbp"], act(T.mb[:, 4 * (E + V):1024], ones[:, 0:1024 - 4 * (E + V)], scale=0.0))
+    op("s", ["ones"], ["xt0", "xt1", "xtc"], act(T.xt[:], ones[:, 0:512], scale=0.0))
+    op("s", ["ones"], ["occ2a"], act(T.occ2[:, 0:384], ones[:, 0:384], scale=0.0))
+    op("s", ["ones"], ["occ2b"], act(T.occ2[:, 384:768], ones[:, 0:384], scale=0.0))
     op("s", ["ez"], ["ezn"], act(T.ezn[:], T.ez[:], scale=-1.0))
     for t in range(2):
         op("s", ["diag"], ["sel%d" % t], act(T.sel[:, t:512:4], T.diag[:, 0:128], scale=float(STEP)))
-    op("s", ["irow"], ["sel2"], act(T.sel[:, 2:512:4], T.irow[:, 0:128]))
-    op("s", ["ones"], ["sel3"], act(T.sel[:, 3:512:4], ones[:, 0:128]))
+
+    def table_rows(name):
+        op("s", ["irow"], [name + "2"], act(T[name][:, 2:512:4], T.irow[:, 0:128]))
+        op("s", ["ones"], [name + "3"], act(T[name][:, 3:512:4], ones[:, 0:128]))
+
+    table_rows("sel")
     op("g", [], ["krow"], iota(T.krow[:, 0:12], [[1, 12]], 0))
+    for i, h in enumerate(others):
+        op("g", [], ["krow%d" % i], iota(T.krow[:, 12 + 3 * i:15 + 3 * i], [[1, 3]], 3 * h))
+    op("g", [], ["hrow"], iota(T.hrow[:], [[1, 12], [0, 16]], 0))
     op("g", ["xtc"], ["xtc3"], iota(T.xt[0:1, 2:4 * NT:4], [[0, NT]], 1))
     op("g", ["xtc"], ["xtc4"], iota(T.xt[0:1, 3:48:4], [[16, 12]], 0))
     for i, h in enumerate(others):
-        op("g", [], ["krow%d" % i], iota(T.krow[:, 12 + 3 * i:15 + 3 * i], [[1, 3]], 3 * h))
         op("g", ["xtc"], ["xtc%d" % i], iota(T.xt[0:1, 51 + 12 * i:60 + 12 * i:4], [[16, 3]], PAIR * blk(r, h)))
 
-    op("v", ["rt"], ["k1"], ts(T.k1[:], T.rt[:], -(E - 1) / 2.0, 1.0 / E, A.add, A.mult))
-    op("v", ["rt"], ["ro"], lambda: vec.tensor_copy(T.ro[:], T.rt[:]))
-    op("v", ["k1"], ["k2"], lambda: vec.tensor_copy(T.k2[:], T.k1[:]))
-    op("v", ["k2", "etab"], ["k3"], lambda: vec.tensor_tensor(T.k3[:], T.k2[:], T.etab[:], A.add))
-    op("v", ["k3"], ["ko"], ts(T.ko[:], T.k3[:], 256.0, None, A.mult))
-    op("v", ["ko", "ones"], ["occa", "occb"], lambda: vec.tensor_copy(T.occ[:, 0:KEYW].indirect(T.ko[:, 0:12]), ones[:, 0:E]))
-    op("v", ["occa", "occb"], ["cum"], scan(T.cum[:], T.occ[:], T.occ[:], 0.0, A.add, A.max))
-    op("v", ["cum", "ko", "diag"], ["gm"], lambda: vec.tensor_tensor(T.gm[:], T.cum[:, 0:KEYW].indirect(T.ko[:, 0:12]), T.diag[:], A.mult))
-    op("v", ["gm", "seg"], ["gs"], scan(T.gs[:], T.seg[:], T.gm[:], 0.0, A.mult, A.add))
-    op("v", ["gs"], ["so"], ts(T.so[:], T.gs[:, 15:E:16], -1.0, None, A.add))
+    for k in range(3):
+        op("v", ["rt"], ["gk%d" % k], ts(T.gk[:, 12 * k:12 * k + 12], T.rt[:], float(E * (k + 1)), 1.0 / BASE, A.is_lt, A.max))
+    op("v", ["rt"], ["k2"], ts(T.k2[:], T.rt[:], -(E - 1) / 2.0, 1.0 / E, A.add, A.mult))
+    op("v", ["gk0", "gk1"], ["w12"], tt(T.w12[:], T.gk[:, 0:12], T.gk[:, 12:24], A.mult))
+    op("v", ["k2"], ["b48"], ts(T.b48[:], T.k2[:], float(PAIR), PAIR / 2.0 - 1, A.mult, A.add))
+    op("v", ["w12", "gk2"], ["winv0"], tt(T.winv[:, 0:12], T.w12[:], T.gk[:, 24:36], A.mult))
+    op("v", ["wrow", "ones"], ["cum"], scan(T.cum[:], ones[:, 0:E], T.wrow[:], -PAIR / 2.0 * sum(BASE ** h for h in range(N)), A.mult, A.add))
+    op("v", ["winv0"], ["winv1"], ts(T.winv[:, 12:24], T.winv[:, 0:12], 1.0 / BASE, None, A.mult))
+    op("v", ["cum", "latch"], ["lat"], scan(T.lat[:], T.latch[:], T.cum[:], 0.0, A.max, A.min))
+
+    def rfo(j):
+        op("v", ["erow", "cj"], ["rfo%d" % j], ts(T.rfo[:, 12 * j:12 * j + 12], T.erow[:, 0:E:16], T.cj[:, j:j + 1], None, A.add))
+
+    def k01(s):
+        op("v", ["krow", "krow0", "krow1", "krow2", "pf"], ["k01%d" % s],
+           ts(T.k01[:, NT * s:NT * s + NT], T.krow[:], -6.0 * s, g16, A.add, A.is_equal))
+
+    rfo(0)
+    for i in range(2):
+        op("v", ["lat", "winv%d" % i], ["nh%d" % i], tt(T.nh[:, 12 * i:12 * i + 12], T.lat[:, 15:E:16], T.winv[:, 12 * i:12 * i + 12], A.mult))
+    op("v", ["nh0", "b48"], ["f10"], tt(T.f1[:, 0:12], T.nh[:, 0:12], T.b48[:], A.add))
+    op("v", ["nh1"], ["f11"], ts(T.f1[:, 12:24], T.nh[:, 12:24], -float(BASE), None, A.mult))
+    rfo(1)
+    op("v", ["f10", "f11"], ["f2"], tt(T.f2[:], T.f1[:, 0:12], T.f1[:, 12:24], A.add))
+    rfo(2)
+    op("v", ["f2"], ["so"], lambda: vec.tensor_copy(T.so[:], T.f2[:]))
+    quant("qm", 0, 128, T.mb[:, 0:512], ["mb"], "qm0")
     op("v", ["so", "erow"], ["invb"], lambda: vec.tensor_copy(T.invb[:, 0:E].indirect(T.so[:, 0:12]), T.erow[:]))
-    quant("qm", 0, 240, T.mb[:], ["mb"], "qm")
+    quant("qm", 128, 256, T.mb[:, 512:1024], ["mb", "mbp"], "qm1")
     op("v", ["invb", "latch"], ["invs"], scan(T.invs[:], T.latch[:], T.invb[:], 0.0, A.max, A.min))
+    k01(0)
     op("v", ["invs"], ["iof"], lambda: vec.tensor_copy(T.iof[:], T.invs[:, 15:E:16]))
-    pick("x0", MS, MS + E, "x0m", "qm", 0, 240, ["qm"], T.iof[:, 0:12], ["iof"])
+    op("v", ["invs"], ["b2"], ts(T.b2[:], T.invs[:, 15:E:16], 0.25, E - 0.375, A.mult, A.add))
+    pick("x0", MS, MS + E, "x0m", "qm", 0, 256, ["qm0", "qm1"], T.iof[:, 0:12], ["iof"])
     send_block("x0", MS, HR, "x0m", "ad0")
     landed(["x0h", "x0hs"], "ad0", arriving((True, False)))
 
     op("v", ["ro", "ones"], ["occ2a", "occ2b"], lambda: vec.tensor_copy(T.occ2[:, 0:768].indirect(T.ro[:, 0:12]), ones[:, 0:E]))
-    for j in range(3):
-        op("v", ["erow", "cj"], ["rfo%d" % j], ts(T.rfo[:, 12 * j:12 * j + 12], T.erow[:, 0:E:16], T.cj[:, j:j + 1], None, A.add))
+    op("v", ["b2"], ["bo"], lambda: vec.tensor_copy(T.bo[:], T.b2[:]))
+    k01(1)
+    op("v", ["k010"], ["k010"], lambda: vec.memset(T.k01[96:128, 0:NT], 0.0))
     for h in range(N):
         first = (MS + PAIR * h if h == r else HR + PAIR * blk(h, r)) - SHIFT - 1
         op("v", ["occ2a", "occ2b", "ones"], ["cum2%d" % h],
            scan(T.cum2[:, E * h:E * h + E], ones[:, 0:E], T.occ2[:, E * h:E * h + E], float(first), A.mult, A.add))
+    for i, row in enumerate(("irow", "hrow")):
+        op("s", [row, "iof"], ["lh%d" % i], act(T.lh[:, E * i:E * i + E], T[row][:, 0:E].indirect(T.iof[:, 0:12])))
+        for s in range(2):
+            a = slice(E * i + 96 * s, E * i + 96 * s + 96)
+            op("g", ["lh%d" % i], ["lhd%d%d" % (i, s)], lambda a=a: g.affine_select(T.lhd[:, a], T.lh[:, a], [[1, 96]], A.is_equal, 0.0, 0, -1))
+    nodes = ("qb", 0, E, "qb", "qm", 0, 256, ["qm0", "qm1"], T.bo[:, 0:12], ["bo"])
+    pick_scales(*nodes)
     op("s", ["cum2%d" % h for h in range(N)] + ["ro"], ["rb"], act(T.rb[:], T.cum2[:, 0:768].indirect(T.ro[:, 0:12])))
     for j in range(3):
         op("s", ["rb", "rfo%d" % j], ["rf%d" % j], act(T.rf[:, E * j:E * j + E], T.rb[:, 0:E].indirect(T.rfo[:, 12 * j:12 * j + 12])))
-    op("v", ["invs"], ["b1"], ts(T.b1[:], T.invs[:, 15:E:16], 0.25, E - 0.375, A.mult, A.add))
-    quant("qe", 0, 128, T.ez[:, 3:515], ["ez"], "qe0")
-    op("v", ["b1"], ["b2"], lambda: vec.tensor_copy(T.b2[:], T.b1[:]))
-    quant("qe", 128, 256, T.ez[:, 2:514], ["ez"], "qe1")
-    op("v", ["b2"], ["bo"], lambda: vec.tensor_copy(T.bo[:], T.b2[:]))
-    quant("qe", 256, 384, T.ez[:, 1:513], ["ez"], "qe2")
-    nodes = ("qb", 0, E, "qb", "qm", 0, 240, ["qm"], T.bo[:, 0:12], ["bo"])
+    op("s", ["k010", "k011"], ["kk"], act(T.kk[:], T.k01[:], ACT.Identity, bias=OFFK, scale=CAP - OFFK))
+    op("s", ["ones"], ["ytp"], act(T.yt[:, 4 * E:4 * YW], ones[:, 0:4 * (YW - E)], scale=0.0))
+    op("s", ["ones"], ["uba"], act(T.ub[:, 0:192], ones[:, 0:192], scale=0.0))
+    op("s", ["ones"], ["ubb"], act(T.ub[:, 384:704], ones[:, 0:320], scale=0.0))
+    for t in range(4):
+        op("s", ["ut", "ones"], ["ub%d" % t], act(T.ub[:, 192 + t:384:4], ones[:, 0:PAIR], ACT.Identity, bias=T.ut[:, t:t + 1], scale=0.0))
+    op("g", ["ones"], ["flip"], lambda: g.affine_select(T.flip[:], ones[:, 0:PAIR], [[1, PAIR]], A.not_equal, -1.0, 0, -1))
+    op("g", ["flip"], ["flip"], lambda: g.affine_select(T.flip[:], T.flip[:], [[1, PAIR]], A.not_equal, -1.0, PAIR, -1))
+    op("g", [], ["wc"], iota(T.wc[:], [[1, 2], [0, LA // 2]], 0))
     pick_codes(*nodes)
+    for b in range(4):
+        quant("qe", 128 * b, 128 * b + 128, T.ez[:, 3 - b:515 - b], ["ez"], "qe%d" % b)
     for j in range(3):
-        op("v", ["rf%d" % j, "iof", "diag"], ["am%d" % j], lambda j=j: vec.tensor_tensor(
-            T.am[:, E * j:E * j + E], T.rf[:, E * j:E * j + E].indirect(T.iof[:, 0:12]), T.diag[:], A.mult))
-    pick_scales(*nodes)
+        op("v", ["rf%d" % j, "iof", "diag"], ["am%d" % j],
+           tt(T.am[:, E * j:E * j + E], T.rf[:, E * j:E * j + E].indirect(T.iof[:, 0:12]), T.diag[:], A.mult))
     for j in range(3):
         op("v", ["am%d" % j, "seg"], ["asc%d" % j], scan(T.asc[:, E * j:E * j + E], T.seg[:], T.am[:, E * j:E * j + E], 0.0, A.mult, A.add))
-    quant("qe", 384, 512, T.ez[:, 0:512], ["ez"], "qe3")
+    quant("qn", 0, 128, T.ezn[:, 3:515], ["ezn"], "qn0")
     op("v", ["asc0", "asc1", "asc2"], ["ao"], ts(T.ao[:], T.asc[:, 15:3 * E:16], float(SHIFT), None, A.add))
-    for t in range(4):
-        op("s", ["ut", "ones"], ["ub%d" % t], act(T.ub[:, t:512:4], ones[:, 0:128], ACT.Identity, bias=T.ut[:, t:t + 1], scale=0.0))
-
-    def select(a, n, step, fill, base, mult):
-        op("g", ["th"], ["th"], lambda: g.affine_select(T.th[:, a:a + n], T.th[:, a:a + n], [[step, n]], A.is_ge, fill, base, mult))
-
-    for t in range(2):
-        c0, p0 = 96 * t, 64 * t
-        select(c0, 96, 1, -0.5, c0 - p0, -1)
-        select(c0, PAIR, 0, 2.0, c0 + PAIR - 1 - p0, -1)
-        select(c0 + PAIR, PAIR, 0, 2.0, p0 - c0 - PAIR, 1)
+    quant("qn", 128, 256, T.ezn[:, 2:514], ["ezn"], "qn1")
 
     def node_terms():
         for b in range(4):
@@ -304,9 +339,44 @@ def rank_program(g, core, T, topo):
             else:
                 op("v", ["%s%d" % (bank, b)], ["%s%d" % (tile, b)], ts(dst, src, scale, None, A.mult))
 
+    def products(t):
+        for o in range(O):
+            mm("pz", o, E, "qw", 128 * o, "qw", "qo%d" % t, 0, "qo%d" % t, True, True)
+
+    def results(t, o, q):
+        src, dst = T.pz[:, 512 * o:512 * o + E], T["yb%d" % t][:, E * o:E * o + E]
+        op(q, ["pz%d" % o], ["yb%d_%d" % (t, o)], act(dst, src) if q == "s" else (lambda: vec.tensor_copy(dst, src)))
+
+    def store_results(t, after):
+        store("y", ["yb%d_%d" % (t, o) for o in range(O)] + after, T.y[:, t * O * E:(t + 1) * O * E], T["yb%d" % t][:])
+
+    def tally(t):
+        flags = T.wc[:, 0:LA].indirect(T["off%d" % t][:, 0:12])
+        if t == 0:
+            op("v", ["wc", "off0"], ["acc"], lambda: vec.tensor_copy(T.acc[:], flags))
+        elif t < R - 1:
+            op("v", ["wc", "off%d" % t, "acc"], ["acc"], tt(T.acc[:], flags, T.acc[:], A.add))
+        else:
+            op("v", ["wc", "off%d" % t, "upe"], ["upo"], tt(T.upo[:], flags, T.upe[:], A.add))
+
+    def edge_columns():
+        for i in range(2):
+            for s in range(2):
+                a = slice(E * i + 96 * s, E * i + 96 * s + 96)
+                op("s", ["lhd%d%d" % (i, s)], ["lhd%d%d" % (i, s), "lhc%d%d" % (i, s)],
+                   act(T.lhd[:, a], T.lhd[:, a], accum_out=T.lhc[:, 2 * i + s:2 * i + s + 1]))
+
+    def edge_tiles():
+        for s in range(2):
+            op("v", ["irow", "lhc0%d" % s], ["sele%d" % s], ts(T.sele[:, s:512:4], T.irow[:, 0:128], T.lhc[:, s:s + 1], float(STEP), A.is_equal, A.mult))
+        for s in range(2):
+            op("v", ["krow", "lhc1%d" % s], ["k01e%d" % s], ts(T.k01e[:, 12 * s:12 * s + 12], T.krow[:, 0:12], T.lhc[:, 2 + s:3 + s], None, A.is_equal))
+        quant("qse", 0, 128, T.sele[:], ["sele0", "sele1", "sele2", "sele3"], "qse")
+        op("v", ["k01e0", "k01e1"], ["k01e0", "k01e1"], lambda: vec.memset(T.k01e[96:128, :], 0.0))
+
     node_terms()
     for t in range(R):
-        x, nx, qa, qo, yb, off = "x%d" % t, "x%d" % (t + 1), "qa%d" % t, "qo%d" % t, "yb%d" % t, T["off%d" % t]
+        x, nx, qa, qo, off = "x%d" % t, "x%d" % (t + 1), "qa%d" % t, "qo%d" % t, T["off%d" % t]
         last = t == R - 1
         if t > 0:
             px = "x%d" % (t - 1)
@@ -316,9 +386,13 @@ def rank_program(g, core, T, topo):
             for b in range(4):
                 mm("pz", b, E, "qe", 128 * b, "qe%d" % b, qa, E * j, "%s_%d" % (qa, j), False, j == 2)
         if t == 0:
-            for b in range(4):
+            for b in (2, 3):
                 quant("qn", 128 * b, 128 * b + 128, T.ezn[:, 3 - b:515 - b], ["ezn"], "qn%d" % b)
             minus_held(0)
+        elif last:
+            edge_tiles()
+        else:
+            quant("qw", 0, 128 * O, T.wt[:], ["wt"], "qw")
         to_tile("zt", "pz", 0.25)
         quant(x, CA, CA + E, T.zt[:], ["zt0", "zt1", "zt2", "zt3"], x + "c")
         if not last:
@@ -327,75 +401,75 @@ def rank_program(g, core, T, topo):
         for b in range(4):
             mm("py", b, E, "qe", 128 * b, "qe%d" % b, x, CA, x + "c", False, True)
         if t == 0:
-            quant("qu", 0, 128, T.ub[:], ["ub0", "ub1", "ub2", "ub3"], "qu")
-            for s in range(2):
-                op("v", ["krow", "krow0", "krow1", "krow2", "pf"], ["kk%d" % s],
-                   ts(T.kk[:, NT * s:NT * s + NT], T.krow[:], -4.0 * s, g16, A.add, A.is_equal))
-        to_tile("yt", "py", 1.0)
-        quant("qy", 0, E, T.yt[:], ["yt0", "yt1", "yt2", "yt3"], "qy")
-        mm("pz", 0, E, "qu", 0, "qu", "qy", 0, "qy", True, True)
-        mm("pz", 1, 128, "qy", 0, "qy", "qu", 0, "qu", True, True)
-        mm("pz", 2, 128, "qy", 64, "qy", "qu", 0, "qu", True, True)
-        if t == 0:
-            op("v", [], ["kk0"], lambda: vec.memset(T.kk[96:128, 0:NT], 0.0))
-            op("v", [], ["kk1"], lambda: vec.memset(T.kk[0:32, NT:2 * NT], 0.0))
-        for s in range(2):
-            op("v", ["pz%d" % (1 + s)], ["nc%d" % s], lambda s=s: vec.tensor_reduce(
-                T.nc[:, s:s + 1], T.pz[:, 512 * (1 + s):512 * (1 + s) + 1], AxisListType.X, A.max, negate=True, apply_absolute_value=True))
-        if t == 0:
+            quant("qu", 0, 176, T.ub[:], ["uba", "ubb", "ub0", "ub1", "ub2", "ub3"], "qu")
             quant("qs", 0, 128, T.sel[:], ["sel0", "sel1", "sel2", "sel3"], "qs")
-        for s in range(2):
-            a = slice(96 * s, 96 * s + 96)
-            op("s", ["pz0"], ["dd%d" % s], act(T.dd[:, a], T.pz[:, a], ACT.Abs))
-            op("s", ["dd%d" % s, "nc%d" % s], ["sg%d" % s], act(T.sg[:, a], T.dd[:, a], ACT.Sign, bias=T.nc[:, s:s + 1]))
-        for s in range(2):
-            a = slice(96 * s, 96 * s + 96)
-            op("v", ["sg%d" % s, "th"], ["gt%d" % s], lambda a=a: vec.tensor_tensor(T.gt[:, a], T.sg[:, a], T.th[:, a], A.is_gt))
-        op("s", ["gt0"], ["cnt0", "sg0"], act(T.sg[:, 0:96], T.gt[:, 0:96], accum_out=T.cnt[:, 0:1]))
-        op("v", ["gt1"], ["cnt1"], lambda: vec.tensor_reduce(T.cnt[:, 1:2], T.gt[:, 96:E], AxisListType.X, A.add))
-        for s in range(2):
-            op("v", ["cnt%d" % s, "kk%d" % s], ["xt%d" % s],
-               ts(T.xt[:, s:4 * NT:4], T.kk[:, NT * s:NT * s + NT], float(CAP), T.cnt[:, s:s + 1], A.mult, A.is_gt))
-        quant("qx", 0, 128, T.xt[:], ["xt0", "xt1", "xtc", "xtc0", "xtc1", "xtc2", "xtc3", "xtc4"], "qx")
-        mm("pz", 3, 128, "qs", 0, "qs", "qx", 0, "qx", True, True)
-        op("v", ["pz3"], ["off%d" % t], lambda off=off: vec.tensor_copy(off[:, 0:NT], T.pz[:, 1536:1536 + NT]))
-        if not last:
-            lo = T["lo%d" % t]
-            send(["off%d" % t], "af%d" % t, True,
-                 [(off[:, 12 + 3 * i:15 + 3 * i], lo[:, 3 * blk(r, h):3 * blk(r, h) + 3]) for i, h in enumerate(others)])
-            landed(["lo%d" % t], "af%d" % t, arriving((True,)))
-            node_terms()
-        pick(nx, MS, MS + E, nx + "m", x, 0, LA, [x + "m", x + "h", x + "c"], off[:, 0:12], ["off%d" % t])
-        pick(qo, 0, E, qo, nx, MS, MS + E, [nx + "m"], T.so[:, 0:12], ["so"])
-        if t == 0:
-            quant("qw", 0, 128 * O, T.wt[:], ["wt"], "qw")
-            op("s", ["ones"], ["wca"], act(T.wc[:, 0:CA], ones[:, 0:CA], scale=0.0))
-            op("s", ["ones"], ["wcb"], act(T.wc[:, CA:LA], ones[:, 0:E]))
-        for o in range(O):
-            mm("py", o, E, "qw", 128 * o, "qw", qo, 0, qo, True, True)
-        if last:
-            store("y", [qo], T.oc[:], T[qo][:, 0:E].bitcast(dt.uint8))
-            for k in range(4):
-                store("y", [qo + "s"], T.osc[4 * k:4 * k + 4, :], T[qo + "s"][32 * k:32 * k + 4, :])
-        flags = T.wc[:, 0:LA].indirect(off[:, 0:12])
-        if t > 0:
-            op("v", ["wca", "wcb", "off%d" % t, "acc"], ["acc"], lambda flags=flags: vec.tensor_tensor(T.acc[:], flags, T.acc[:], A.add))
-        for o in range(O):
-            src, dst = T.py[:, 512 * o:512 * o + E], T[yb][:, E * o:E * o + E]
-            if o == 1 and t != 1:
-                op("v", ["py%d" % o], ["%s_%d" % (yb, o)], lambda src=src, dst=dst: vec.tensor_copy(dst, src))
-            else:
-                op("s", ["py%d" % o], ["%s_%d" % (yb, o)], act(dst, src))
-            if last:
-                store("y", ["%s_%d" % (yb, o)], T.y[:, (t * O + o) * E:(t * O + o + 1) * E], dst)
-        if t == 0:
-            op("v", ["wca", "wcb", "off0"], ["acc"], lambda flags=flags: vec.tensor_copy(T.acc[:], flags))
-        if last:
-            op("v", ["acc", "so"], ["upo"], lambda: vec.tensor_copy(T.upo[:], T.acc[:, 0:E].indirect(T.so[:, 0:12])))
-            store("s", ["upo"], T.up[:], T.upo[0:1, :])
+            table_rows("sele")
         else:
-            store("y", ["%s_%d" % (yb, o) for o in range(O)] + ["lo%d" % t], T.y[:, t * O * E:(t + 1) * O * E], T[yb][:])
-            minus_held(t + 1)
+            products(t - 1)
+        in_edge_order = ("qo%d" % (t - 1), CA, CA + E, "qce", x, CA, CA + E, [x + "c"], T.so[:, 0:12], ["so"])
+        if last:
+            op("s", ["k01e0", "k01e1"], ["kke"], act(T.kke[:], T.k01e[:], ACT.Identity, bias=OFFK, scale=CAP - OFFK))
+            pick_codes(*in_edge_order)
+        to_tile("yt", "py", 1.0)
+        quant("qy", 0, YW, T.yt[:], ["yt0", "yt1", "yt2", "yt3", "ytp"], "qy")
+        if t == 0:
+            edge_columns()
+        else:
+            for o in range(O - 1 if last else O):
+                results(t - 1, o, "s")
+        if last:
+            results(t - 1, O - 1, "v")
+            store_results(t - 1, [])
+        mm("py", 0, 144, "qu", PAIR, "qu", "qy", 0, "qy", True, False)
+        mm("py", 0, 144, "qu", 0, "qu", "qy", PAIR, "qy", False, True)
+        for s in range(2):
+            mm("py", 1 + s, 128, "qy", 96 * s, "qy", "qu", PAIR, "qu", True, True)
+        if not last:
+            node_terms()
+        op("s", ["py0"], ["dd"], act(T.dd[:], T.py[:, 0:144], ACT.Abs))
+        for s in range(2):
+            op("v", ["py%d" % (1 + s)], ["nc%d" % s], lambda s=s: vec.tensor_reduce(
+                T.nc[:, s:s + 1], T.py[:, 512 * (1 + s):512 * (1 + s) + 1], AxisListType.X, A.max, apply_absolute_value=True))
+        for s in range(2):
+            a, d, own = slice(PAIR * s, PAIR * s + PAIR), T.dd[:, 96 * s:96 * s + PAIR], T.nc[:, s:s + 1]
+            op("v", ["dd", "nc%d" % s], ["eq%d" % s], ts(T.eq[:, a], d, own, None, A.is_equal))
+            op("s", ["dd", "nc%d" % s], ["sg%d" % s, "cnt%d" % s], act(T.sg[:, a], d, ACT.Sign, bias=own, scale=-1.0, accum_out=T.cnt[:, s:s + 1]))
+        if last:
+            pick_scales(*in_edge_order)
+            op("s", ["acc", "so"], ["upe"], act(T.upe[:], T.acc[:, 0:E].indirect(T.so[:, 0:12])))
+        for s in range(2):
+            a = slice(PAIR * s, PAIR * s + PAIR)
+            op("v", ["eq%d" % s, "flip"], ["tie%d" % s], scan(T.tie[:, a], T.flip[:], T.eq[:, a], 0.0, A.mult, A.add))
+        kk, nt, qs = ("kke", 12, "qse") if last else ("kk", NT, "qs")
+        for s in range(2):
+            op("v", ["cnt%d" % s, "tie%d" % s, kk], ["xt%d" % s],
+               ts(T.xt[:, s:4 * nt:4], T[kk][:, nt * s:nt * s + nt], T.cnt[:, s:s + 1], T.tie[:, PAIR * s + PAIR - 1:PAIR * s + PAIR], A.subtract, A.is_lt))
+        quant("qx", 0, 128, T.xt[:], ["xt0", "xt1", "xtc", "xtc0", "xtc1", "xtc2", "xtc3", "xtc4"], "qx")
+        mm("py", 3, 128, qs, 0, qs, "qx", 0, "qx", True, True)
+        op("v", ["py3"], ["off%d" % t], lambda off=off, nt=nt: vec.tensor_copy(off[:, 0:nt], T.py[:, 1536:1536 + nt]))
+        if last:
+            break
+        lo = T["lo%d" % t]
+        send(["off%d" % t], "af%d" % t, True,
+             [(off[:, 12 + 3 * i:15 + 3 * i], lo[:, 3 * blk(r, h):3 * blk(r, h) + 3]) for i, h in enumerate(others)])
+        landed(["lo%d" % t], "af%d" % t, arriving((True,)))
+        pick(nx, MS, MS + E, nx + "m", x, 0, LA, [x + "m", x + "h", x + "c"], off[:, 0:12], ["off%d" % t])
+        tally(t)
+        pick(qo, 0, E, qo, nx, MS, MS + E, [nx + "m"], T.so[:, 0:12], ["so"])
+        minus_held(t + 1)
+        if t > 0:
+            store_results(t - 1, ["lo%d" % t])
+    held = "qo%d" % (t - 1)
+    pick(qo, 0, E, qo, held, 0, LA, [held, "qce"], off[:, 0:12], ["off%d" % t])
+    products(t)
+    store("y", [qo], T.oc[:], T[qo][:, 0:E].bitcast(dt.uint8))
+    for k in range(4):
+        store("y", [qo + "s"], T.osc[4 * k:4 * k + 4, :], T[qo + "s"][32 * k:32 * k + 4, :])
+    tally(t)
+    for o in range(O):
+        results(t, o, "v" if o == 1 else "s")
+        store("y", ["yb%d_%d" % (t, o)], T.y[:, (t * O + o) * E:(t * O + o + 1) * E], T["yb%d" % t][:, E * o:E * o + E])
+    store("s", ["upo"], T.up[:], T.upo[0:1, :])
 
     for s in ("cv", "cs", "cp", "cg", "sent", "st"):
         g.wait_ge(T.sem[s], count[s])

@@ -5,8 +5,10 @@ N, V, E, PAIR, CAP, R, O = 4, 48, 192, 48, 16, 3, 3
 X4, U8, BF, F32, I32, U16 = "float8_e4m3fn_x4", "uint8", "bfloat16", "float32", "int32", "uint16"
 MS, HR, CA, LA, XW = 0, 192, 384, 576, 720
 STEP = CA - MS
-BASE = 64
+IW = (2 * N - 1) * E
+YP = (0, E, 4 * E)
 YW = E + 32
+NW = E - 2 * 16
 OFFK = 64.0
 SHIFT = 80
 NT = 21
@@ -24,28 +26,29 @@ def _mx(name, n):
 
 
 for _n, _w, _d in (
-        ("rt", 12, I32), ("mb", 1024, BF), ("ut", 512, BF), ("wt", 1536, BF),
-        ("ones", 516, BF), ("ez", 516, BF), ("ezn", 516, BF), ("seg", E, BF), ("irow", E, BF), ("erow", E, BF),
-        ("diag", E, BF), ("latch", E, BF), ("pcol", 1, I32), ("pi", 4, I32), ("pf", 4, F32), ("gk", 36, F32),
-        ("cj0", 4, F32), ("cj", 4, F32), ("rfo", 36, U16), ("wtab", N * E, BF), ("cum", E, F32), ("occ2", 768, BF),
-        ("cum2", 768, BF), ("k2", 12, I32), ("w12", 12, F32), ("winv", 24, F32), ("ro", 12, U16),
-        ("wrow", E, BF), ("lat", E, F32), ("nh", 24, I32), ("b48", 12, F32), ("f1", 24, F32), ("f2", 12, F32),
-        ("so", 12, U16), ("invb", E, BF), ("invs", E, BF), ("iof", 12, U16),
-        ("b2", 12, I32), ("bo", 12, U16), ("rb", E, BF), ("rf", 3 * E, BF), ("am", 3 * E, BF),
+        ("rt", 12, I32), ("mb", 4 * (E + V), BF), ("ut", 512, BF), ("wt", 1536, BF),
+        ("ones", 516, BF), ("ez", 516, BF), ("ezn", 516, BF), ("irow", E, BF),
+        ("diag", E, BF), ("latch", E, BF), ("pcol", 1, I32), ("pi", 4, I32), ("pf", 4, F32), ("thr", 12, F32),
+        ("c16", 12, F32), ("sp", 12, F32), ("si", 18, I32), ("sj", 36, F32), ("lo3", 36, U16),
+        ("ind", IW, BF), ("cum", N * E, BF), ("occ2", 768, BF),
+        ("cum2", 768, BF), ("k2", 12, I32), ("mk", 48, F32), ("mq", 48, F32), ("ro", 12, U16),
+        ("hit", N * E, BF), ("lat", N * E, BF), ("na", 6 * E, BF), ("nb", 6 * NW, BF), ("nw", 6 * NW, BF), ("ca", 6, F32),
+        ("f1", 24, F32), ("f2", 12, F32), ("so", 12, U16), ("iof", 12, U16),
+        ("b2", 12, I32), ("bo", 12, U16), ("rb", E, BF), ("am", 3 * E, BF),
         ("asc", 3 * E, BF), ("ao", 36, U16), ("ub", 704, BF), ("sel", 512, BF), ("xt", 512, BF), ("flip", PAIR, BF),
         ("krow", NT, F32), ("k01", 2 * NT, F32), ("kk", 2 * NT, F32), ("wc", LA, BF), ("acc", E, F32), ("upo", E, F32),
         ("zt", 4 * E, BF), ("yt", 4 * YW, BF), ("dd", 144, F32), ("nc", 2, F32), ("sg", 96, BF), ("eq", 96, BF),
         ("tie", 96, F32), ("cnt", 2, F32), ("hrow", E, BF), ("lh", 2 * E, BF), ("lhd", 2 * E, BF), ("lhc", 4, F32),
-        ("sele", 512, BF), ("k01e", 24, F32), ("kke", 24, F32), ("upe", E, F32)):
+        ("sele", 512, BF), ("k01e", 24, F32), ("kke", 24, F32), ("yw", IW, F32)):
     _sb(_n, _w, _d)
-for _n, _w in (("qm", 256), ("qe", 512), ("qn", 512), ("qu", 176), ("qw", 384), ("qs", 128), ("qb", E), ("qy", YW),
+for _n, _w in (("qm", E + V), ("qe", 512), ("qn", 512), ("qu", 176), ("qw", 384), ("qs", 128), ("qb", E), ("qy", YW),
                ("qx", 128), ("x0", XW), ("x1", XW), ("x2", LA), ("qo0", E), ("qo1", LA), ("qo2", E), ("qse", 128)):
     _mx(_n, _w)
 for _t in range(R):
     _mx("qa%d" % _t, 3 * E)
-    _sb("yb%d" % _t, O * E, F32)
     _sb("off%d" % _t, 24, U16)
 for _t in range(R - 1):
+    _sb("yb%d" % (2 * _t), O * E, F32)
     _sb("lo%d" % _t, 16, U16)
 SCRATCH["pz"] = ("psum", [128, 2048], F32)
 SCRATCH["py"] = ("psum", [128, 2048], F32)
@@ -122,6 +125,9 @@ def rank_program(g, core, T, topo):
     def tt(out, in0, in1, o):
         return lambda: vec.tensor_tensor(out, in0, in1, o)
 
+    def copy(out, in_):
+        return lambda: vec.tensor_copy(out, in_)
+
     def act(out, in_, func=None, **kw):
         return lambda: sca.activation(out, in_, ACT.Copy if func is None else func, **kw)
 
@@ -190,14 +196,14 @@ def rank_program(g, core, T, topo):
         for k in keys:
             wrote[k] = (sem, n, {})
 
-    for k in range(4):
+    for k in range(2):
         load("y", "ldr", T.rt[32 * k:32 * k + 16, :], T.rev[:])
         load("s", "ldr", T.rt[32 * k + 16:32 * k + 32, :], T.rev[:])
     load("y", "ldm", T.mb[:, 0:4 * E], T.m[:])
     load("s", "ldm", T.mb[:, 4 * E:4 * E + 4 * V], T.b[:])
     load("y", "ldu", T.ut[:], T.u[:])
     load("y", "ldw", T.wt[:], T.w[:])
-    landed(["rt"], "ldr", 128)
+    landed(["rt"], "ldr", 64)
     landed(["mb"], "ldm", 32)
     landed(["ut"], "ldu", 16)
     landed(["wt"], "ldw", 16)
@@ -205,123 +211,180 @@ def rank_program(g, core, T, topo):
     ones = T.ones
     op("g", [], ["pcol"], lambda: g.iota(T.pcol[:], [[0, 1]], 0, 1))
     op("v", [], ["ones"], lambda: vec.memset(ones[:], 1.0))
-    op("v", [], ["seg"], lambda: vec.memset(T.seg[:], 1.0))
+    op("g", [], ["c16"], iota(T.c16[:], [[16, 12]], 0))
     op("g", ["ones"], ["ez"], lambda: g.affine_select(T.ez[:], ones[:], [[1, 516]], A.is_equal, 0.0, -3, -4))
-    for h in range(N):
-        op("s", ["ones"], ["wtab%d" % h], act(T.wtab[:, E * h:E * h + E], ones[:, 0:E], scale=float(BASE ** h)))
-    op("s", ["ones"], ["invb"], act(T.invb[:], ones[:, 0:E]))
-    for i, (s1, o) in enumerate(((15, A.bitwise_and), (3, A.bitwise_and), (12, A.bitwise_and), (4, A.arith_shift_right))):
+    op("g", [], ["irow"], iota(T.irow[:], [[0, 12], [1, 16]], 0))
+    for i, (a, z, v) in enumerate(((576, 768, 1.0), (768, 1152, 0.0), (1152, IW, 0.0))):
+        op("s", ["ones"], ["ind%d" % i], act(T.ind[:, a:z], ones[:, 0:z - a], scale=v))
+    for i, (s1, o) in enumerate(((15, A.bitwise_and), (16, A.bitwise_and), (4, A.arith_shift_right))):
         op("v", ["pcol"], ["pi%d" % i], ts(T.pi[:, i:i + 1], T.pcol[:], s1, None, o))
-    op("v", [], ["seg"], lambda: vec.memset(T.seg[:, 0:E:16], 0.0))
-    op("v", ["ones"], ["erow"], scan(T.erow[:], ones[:, 0:E], ones[:, 0:E], -1.0, A.mult, A.add))
-    op("v", ["pi0", "pi1", "pi2", "pi3"], ["pf"], lambda: vec.tensor_copy(T.pf[:], T.pi[:]))
-    op("v", ["seg"], ["irow"], scan(T.irow[:], T.seg[:], T.seg[:], 0.0, A.mult, A.add))
-    q16, a4, q12, g16 = T.pf[:, 0:1], T.pf[:, 1:2], T.pf[:, 2:3], T.pf[:, 3:4]
-    op("v", ["erow", "pf"], ["cj0"], ts(T.cj0[:], T.erow[:, 0:4], a4, q12, A.is_ge, A.add))
-    op("v", ["irow", "pf"], ["diag"], ts(T.diag[:], T.irow[:], q16, None, A.is_equal))
-    op("v", ["cj0", "erow"], ["cj"], tt(T.cj[:], T.cj0[:], T.erow[:, 0:4], A.add))
-    op("v", ["diag"], ["latch"], ts(T.latch[:], T.diag[:], 2.0 ** 27, -2.0 ** 26, A.mult, A.add))
+    op("v", [], ["ind3"], lambda: vec.memset(T.ind[:, 0:576], 0.0))
+    op("v", ["pi0", "pi1", "pi2"], ["pf"], copy(T.pf[:, 0:3], T.pi[:, 0:3]))
+    op("v", [], ["occ2b"], lambda: vec.memset(T.occ2[:, 384:768], 0.0))
+    q16, odd16, g16, even16 = T.pf[:, 0:1], T.pf[:, 1:2], T.pf[:, 2:3], T.pf[:, 3:4]
+    op("v", ["c16", "pf"], ["thr"], ts(T.thr[:], T.c16[:], q16, -0.5, A.add, A.add))
+    op("s", ["pf"], ["pfe"], act(even16, odd16, ACT.Identity, bias=16.0, scale=-1.0))
 
-    op("v", ["rt"], ["ro"], lambda: vec.tensor_copy(T.ro[:], T.rt[:]))
-    op("s", ["ro"] + ["wtab%d" % h for h in range(N)], ["wrow"], act(T.wrow[:], T.wtab[:, 0:N * E].indirect(T.ro[:, 0:12])))
-
-    op("s", ["ones"], ["mbp"], act(T.mb[:, 4 * (E + V):1024], ones[:, 0:1024 - 4 * (E + V)], scale=0.0))
-    op("s", ["ones"], ["xt0", "xt1", "xtc"], act(T.xt[:], ones[:, 0:512], scale=0.0))
+    ro = ["ro0", "ro1"]
+    for k in range(2):
+        op("v", ["rt"], [ro[k]], copy(T.ro[64 * k:64 * k + 64, :], T.rt[0:64, :]))
+    for h in range(N):
+        out, win = T.hit[:, E * h:E * h + E], T.ind[:, E * (N - 1 - h):E * (2 * N - 1 - h)].indirect(T.ro[:, 0:12])
+        op("v" if h < 2 else "s", ro + ["ind%d" % i for i in range(4)], ["hit%d" % h], copy(out, win) if h < 2 else act(out, win))
+    for h in (0, 2, 1, 3):
+        a = slice(E * h, E * h + E)
+        op("v", ["hit%d" % h, "ones"], ["cum%d" % h], scan(T.cum[:, a], ones[:, 0:E], T.hit[:, a], PAIR * h - 1.0, A.mult, A.add))
+    for c in range(6):
+        h, a = c // 3, 16 if c % 3 == 1 else 0
+        op("s", ["cum%d" % h, "thr"], ["ca%d" % c], act(T.na[:, E * c + a:E * c + E - a], T.cum[:, E * h + a:E * h + E - a], ACT.Sign,
+                                                      bias=T.thr[:, c:c + 1], scale=-1.0, accum_out=T.ca[:, c:c + 1]))
+    for c in range(6):
+        a = E * (2 + c // 3) + 16 * (c % 3)
+        op("v", ["cum%d" % (2 + c // 3), "thr"], ["nb%d" % c], ts(T.nb[:, NW * c:NW * c + NW], T.cum[:, a:a + NW], T.thr[:, 6 + c:7 + c], None, A.is_lt))
+    for c in range(6):
+        a = slice(NW * c, NW * c + NW)
+        op("v", ["nb%d" % c, "ones"], ["nw%d" % c], scan(T.nw[:, a], ones[:, 0:NW], T.nb[:, a], 16.0 * (c % 3), A.mult, A.add))
+    quant("qm", 0, E + V, T.mb[:], ["mb"], "qm")
+    op("v", ["nw%d" % c for c in range(6)], ["iof1"], copy(T.iof[:, 6:12], T.nw[:, NW - 1:6 * NW:NW]))
+    op("v", ["ca%d" % c for c in range(6)], ["iof0"], ts(T.iof[:, 0:6], T.ca[:], 0.5, E / 2.0, A.mult, A.add))
+    iof = ["iof0", "iof1"]
     op("s", ["ones"], ["occ2a"], act(T.occ2[:, 0:384], ones[:, 0:384], scale=0.0))
-    op("s", ["ones"], ["occ2b"], act(T.occ2[:, 384:768], ones[:, 0:384], scale=0.0))
-    op("s", ["ez"], ["ezn"], act(T.ezn[:], T.ez[:], scale=-1.0))
-    for t in range(2):
-        op("s", ["diag"], ["sel%d" % t], act(T.sel[:, t:512:4], T.diag[:, 0:128], scale=float(STEP)))
+    pick("x0", MS, MS + E, "x0m", "qm", 0, E + V, ["qm"], T.iof[:, 0:12], iof)
 
     def table_rows(name):
         op("s", ["irow"], [name + "2"], act(T[name][:, 2:512:4], T.irow[:, 0:128]))
         op("s", ["ones"], [name + "3"], act(T[name][:, 3:512:4], ones[:, 0:128]))
 
-    table_rows("sel")
     op("g", [], ["krow"], iota(T.krow[:, 0:12], [[1, 12]], 0))
     for i, h in enumerate(others):
         op("g", [], ["krow%d" % i], iota(T.krow[:, 12 + 3 * i:15 + 3 * i], [[1, 3]], 3 * h))
     op("g", [], ["hrow"], iota(T.hrow[:], [[1, 12], [0, 16]], 0))
-    op("g", ["xtc"], ["xtc3"], iota(T.xt[0:1, 2:4 * NT:4], [[0, NT]], 1))
-    op("g", ["xtc"], ["xtc4"], iota(T.xt[0:1, 3:48:4], [[16, 12]], 0))
-    for i, h in enumerate(others):
-        op("g", ["xtc"], ["xtc%d" % i], iota(T.xt[0:1, 51 + 12 * i:60 + 12 * i:4], [[16, 3]], PAIR * blk(r, h)))
-
-    for k in range(3):
-        op("v", ["rt"], ["gk%d" % k], ts(T.gk[:, 12 * k:12 * k + 12], T.rt[:], float(E * (k + 1)), 1.0 / BASE, A.is_lt, A.max))
-    op("v", ["rt"], ["k2"], ts(T.k2[:], T.rt[:], -(E - 1) / 2.0, 1.0 / E, A.add, A.mult))
-    op("v", ["gk0", "gk1"], ["w12"], tt(T.w12[:], T.gk[:, 0:12], T.gk[:, 12:24], A.mult))
-    op("v", ["k2"], ["b48"], ts(T.b48[:], T.k2[:], float(PAIR), PAIR / 2.0 - 1, A.mult, A.add))
-    op("v", ["w12", "gk2"], ["winv0"], tt(T.winv[:, 0:12], T.w12[:], T.gk[:, 24:36], A.mult))
-    op("v", ["wrow", "ones"], ["cum"], scan(T.cum[:], ones[:, 0:E], T.wrow[:], -PAIR / 2.0 * sum(BASE ** h for h in range(N)), A.mult, A.add))
-    op("v", ["winv0"], ["winv1"], ts(T.winv[:, 12:24], T.winv[:, 0:12], 1.0 / BASE, None, A.mult))
-    op("v", ["cum", "latch"], ["lat"], scan(T.lat[:], T.latch[:], T.cum[:], 0.0, A.max, A.min))
-
-    def rfo(j):
-        op("v", ["erow", "cj"], ["rfo%d" % j], ts(T.rfo[:, 12 * j:12 * j + 12], T.erow[:, 0:E:16], T.cj[:, j:j + 1], None, A.add))
 
     def k01(s):
         op("v", ["krow", "krow0", "krow1", "krow2", "pf"], ["k01%d" % s],
            ts(T.k01[:, NT * s:NT * s + NT], T.krow[:], -6.0 * s, g16, A.add, A.is_equal))
 
-    rfo(0)
-    for i in range(2):
-        op("v", ["lat", "winv%d" % i], ["nh%d" % i], tt(T.nh[:, 12 * i:12 * i + 12], T.lat[:, 15:E:16], T.winv[:, 12 * i:12 * i + 12], A.mult))
-    op("v", ["nh0", "b48"], ["f10"], tt(T.f1[:, 0:12], T.nh[:, 0:12], T.b48[:], A.add))
-    op("v", ["nh1"], ["f11"], ts(T.f1[:, 12:24], T.nh[:, 12:24], -float(BASE), None, A.mult))
-    rfo(1)
-    op("v", ["f10", "f11"], ["f2"], tt(T.f2[:], T.f1[:, 0:12], T.f1[:, 12:24], A.add))
-    rfo(2)
-    op("v", ["f2"], ["so"], lambda: vec.tensor_copy(T.so[:], T.f2[:]))
-    quant("qm", 0, 128, T.mb[:, 0:512], ["mb"], "qm0")
-    op("v", ["so", "erow"], ["invb"], lambda: vec.tensor_copy(T.invb[:, 0:E].indirect(T.so[:, 0:12]), T.erow[:]))
-    quant("qm", 128, 256, T.mb[:, 512:1024], ["mb", "mbp"], "qm1")
-    op("v", ["invb", "latch"], ["invs"], scan(T.invs[:], T.latch[:], T.invb[:], 0.0, A.max, A.min))
-    k01(0)
-    op("v", ["invs"], ["iof"], lambda: vec.tensor_copy(T.iof[:], T.invs[:, 15:E:16]))
-    op("v", ["invs"], ["b2"], ts(T.b2[:], T.invs[:, 15:E:16], 0.25, E - 0.375, A.mult, A.add))
-    pick("x0", MS, MS + E, "x0m", "qm", 0, 256, ["qm0", "qm1"], T.iof[:, 0:12], ["iof"])
     send_block("x0", MS, HR, "x0m", "ad0")
     landed(["x0h", "x0hs"], "ad0", arriving((True, False)))
 
-    op("v", ["ro", "ones"], ["occ2a", "occ2b"], lambda: vec.tensor_copy(T.occ2[:, 0:768].indirect(T.ro[:, 0:12]), ones[:, 0:E]))
-    op("v", ["b2"], ["bo"], lambda: vec.tensor_copy(T.bo[:], T.b2[:]))
-    k01(1)
-    op("v", ["k010"], ["k010"], lambda: vec.memset(T.k01[96:128, 0:NT], 0.0))
-    for h in range(N):
+    def unpack_tile(b):
+        quant("qe", 128 * b, 128 * b + 128, T.ez[:, 3 - b:515 - b], ["ez"], "qe%d" % b)
+
+    def minus_tile(b):
+        quant("qn", 128 * b, 128 * b + 128, T.ezn[:, 3 - b:515 - b], ["ezn"], "qn%d" % b)
+
+    def places(h):
         first = (MS + PAIR * h if h == r else HR + PAIR * blk(h, r)) - SHIFT - 1
         op("v", ["occ2a", "occ2b", "ones"], ["cum2%d" % h],
            scan(T.cum2[:, E * h:E * h + E], ones[:, 0:E], T.occ2[:, E * h:E * h + E], float(first), A.mult, A.add))
-    for i, row in enumerate(("irow", "hrow")):
-        op("s", [row, "iof"], ["lh%d" % i], act(T.lh[:, E * i:E * i + E], T[row][:, 0:E].indirect(T.iof[:, 0:12])))
-        for s in range(2):
-            a = slice(E * i + 96 * s, E * i + 96 * s + 96)
-            op("g", ["lh%d" % i], ["lhd%d%d" % (i, s)], lambda a=a: g.affine_select(T.lhd[:, a], T.lh[:, a], [[1, 96]], A.is_equal, 0.0, 0, -1))
-    nodes = ("qb", 0, E, "qb", "qm", 0, 256, ["qm0", "qm1"], T.bo[:, 0:12], ["bo"])
-    pick_scales(*nodes)
-    op("s", ["cum2%d" % h for h in range(N)] + ["ro"], ["rb"], act(T.rb[:], T.cum2[:, 0:768].indirect(T.ro[:, 0:12])))
+
+    op("v", iof + ["pfe"], ["sp0"], ts(T.sp[:, 0:6], T.iof[:, 0:12:2], even16, 1.0 / 16, A.mult, A.mult))
+    op("v", iof + ["pf"], ["sp1"], ts(T.sp[:, 6:12], T.iof[:, 1:12:2], odd16, 1.0 / 16, A.mult, A.mult))
+    op("v", iof, ["b2"], ts(T.b2[:], T.iof[:], 0.25, E - 0.375, A.mult, A.add))
+    unpack_tile(0)
+    op("v", ["sp0", "sp1"], ["si0"], tt(T.si[:, 0:6], T.sp[:, 0:6], T.sp[:, 6:12], A.add))
+    op("v", ro + ["ones"], ["occ2a", "occ2b"], copy(T.occ2[:, 0:768].indirect(T.ro[:, 0:12]), ones[:, 0:E]))
+    op("v", ["si0"], ["si1"], ts(T.si[:, 6:12], T.si[:, 0:6], 3, None, A.bitwise_and))
+    op("v", ["si0"], ["si2"], ts(T.si[:, 12:18], T.si[:, 0:6], 252, None, A.bitwise_and))
+    op("v", ["b2"], ["bo"], copy(T.bo[:], T.b2[:]))
+    places(0)
     for j in range(3):
-        op("s", ["rb", "rfo%d" % j], ["rf%d" % j], act(T.rf[:, E * j:E * j + E], T.rb[:, 0:E].indirect(T.rfo[:, 12 * j:12 * j + 12])))
-    op("s", ["k010", "k011"], ["kk"], act(T.kk[:], T.k01[:], ACT.Identity, bias=OFFK, scale=CAP - OFFK))
-    op("s", ["ones"], ["ytp"], act(T.yt[:, 4 * E:4 * YW], ones[:, 0:4 * (YW - E)], scale=0.0))
-    op("s", ["ones"], ["uba"], act(T.ub[:, 0:192], ones[:, 0:192], scale=0.0))
-    op("s", ["ones"], ["ubb"], act(T.ub[:, 384:704], ones[:, 0:320], scale=0.0))
-    for t in range(4):
-        op("s", ["ut", "ones"], ["ub%d" % t], act(T.ub[:, 192 + t:384:4], ones[:, 0:PAIR], ACT.Identity, bias=T.ut[:, t:t + 1], scale=0.0))
+        op("v", ["si1"], ["sj%d" % j], ts(T.sj[:, 6 * j:6 * j + 6], T.si[:, 6:12], float(j), float(j), A.is_le, A.add))
+    for h in range(1, N):
+        places(h)
+    for j in range(3):
+        op("v", ["sj%d" % j, "si2"], ["sk%d" % j], tt(T.sj[:, 18 + 6 * j:24 + 6 * j], T.sj[:, 6 * j:6 * j + 6], T.si[:, 12:18], A.add))
+    unpack_tile(1)
+    for k in range(2):
+        op("v", ["sk0", "sk1", "sk2"], ["lo3%d" % k], copy(T.lo3[:, k:36:2], T.sj[:, 18:36]))
+    op("s", ["ez"], ["ezn"], act(T.ezn[:], T.ez[:], scale=-1.0))
+    op("s", ["ones"], ["xt0", "xt1", "xtc"], act(T.xt[:], ones[:, 0:512], scale=0.0))
+    op("g", ["xtc"], ["xtc3"], iota(T.xt[0:1, 2:4 * NT:4], [[0, NT]], 1))
+    op("g", ["xtc"], ["xtc4"], iota(T.xt[0:1, 3:48:4], [[16, 12]], 0))
+    for i, h in enumerate(others):
+        op("g", ["xtc"], ["xtc%d" % i], iota(T.xt[0:1, 51 + 12 * i:60 + 12 * i:4], [[16, 3]], PAIR * blk(r, h)))
+    nodes = ("qb", 0, E, "qb", "qm", 0, E + V, ["qm"], T.bo[:, 0:12], ["bo"])
+    pick_scales(*nodes)
+    op("s", ["cum2%d" % h for h in range(N)] + ro, ["rb"], act(T.rb[:], T.cum2[:, 0:768].indirect(T.ro[:, 0:12])))
+    pick_codes(*nodes)
+
+    def gather_list(j):
+        out, win = T.am[:, E * j:E * j + E], T.rb[:, 0:E].indirect(T.lo3[:, 12 * j:12 * j + 12])
+        op("s" if j else "v", ["rb", "lo30", "lo31"], ["am%d" % j], act(out, win) if j else copy(out, win))
+
+    def turn_list(j):
+        op("v", ["am%d" % j], ["asc%d" % j], lambda: vec.transpose(T.asc[:, E * j:E * j + E], T.am[:, E * j:E * j + E]))
+
+    def cut_list(j):
+        op("v", ["asc%d" % j], ["ao%d" % j], ts(T.ao[:, 12 * j:12 * j + 12], T.asc[:, E * j:E * j + E:16], float(SHIFT), None, A.add))
+
+    for j in range(3):
+        gather_list(j)
     op("g", ["ones"], ["flip"], lambda: g.affine_select(T.flip[:], ones[:, 0:PAIR], [[1, PAIR]], A.not_equal, -1.0, 0, -1))
     op("g", ["flip"], ["flip"], lambda: g.affine_select(T.flip[:], T.flip[:], [[1, PAIR]], A.not_equal, -1.0, PAIR, -1))
-    op("g", [], ["wc"], iota(T.wc[:], [[1, 2], [0, LA // 2]], 0))
-    pick_codes(*nodes)
-    for b in range(4):
-        quant("qe", 128 * b, 128 * b + 128, T.ez[:, 3 - b:515 - b], ["ez"], "qe%d" % b)
-    for j in range(3):
-        op("v", ["rf%d" % j, "iof", "diag"], ["am%d" % j],
-           tt(T.am[:, E * j:E * j + E], T.rf[:, E * j:E * j + E].indirect(T.iof[:, 0:12]), T.diag[:], A.mult))
-    for j in range(3):
-        op("v", ["am%d" % j, "seg"], ["asc%d" % j], scan(T.asc[:, E * j:E * j + E], T.seg[:], T.am[:, E * j:E * j + E], 0.0, A.mult, A.add))
-    quant("qn", 0, 128, T.ezn[:, 3:515], ["ezn"], "qn0")
-    op("v", ["asc0", "asc1", "asc2"], ["ao"], ts(T.ao[:], T.asc[:, 15:3 * E:16], float(SHIFT), None, A.add))
-    quant("qn", 128, 256, T.ezn[:, 2:514], ["ezn"], "qn1")
+    op("g", [], ["uba"], iota(T.ub[:, 0:192], [[0, 192]], 0))
+    op("g", [], ["ubb"], iota(T.ub[:, 384:704], [[0, 320]], 0))
+    op("g", [], ["ytp"], iota(T.yt[:, 4 * E:4 * YW], [[0, 4 * (YW - E)]], 0))
+    unpack_tile(2)
+    turn_list(0)
+    turn_list(1)
+    unpack_tile(3)
+    cut_list(0)
+    turn_list(2)
+    cut_list(1)
+    minus_tile(0)
+
+    def sizes_tile():
+        for t in range(4):
+            op("s", ["ut", "ones"], ["ub%d" % t], act(T.ub[:, 192 + t:384:4], ones[:, 0:PAIR], ACT.Identity, bias=T.ut[:, t:t + 1], scale=0.0))
+
+    def edge_numbers(i):
+        row = ("irow", "hrow")[i]
+        op("s", [row] + iof, ["lh%d" % i], act(T.lh[:, E * i:E * i + E], T[row][:, 0:E].indirect(T.iof[:, 0:12])))
+
+    def edge_select():
+        for i in range(2):
+            for s in range(2):
+                a = slice(E * i + 96 * s, E * i + 96 * s + 96)
+                op("g", ["lh%d" % i], ["lhd%d%d" % (i, s)], lambda a=a: g.affine_select(T.lhd[:, a], T.lh[:, a], [[1, 96]], A.is_equal, 0.0, 0, -1))
+
+    def edge_columns():
+        for i in (1, 0):
+            for s in range(2):
+                a = slice(E * i + 96 * s, E * i + 96 * s + 96)
+                op("s", ["lhd%d%d" % (i, s)], ["lhd%d%d" % (i, s), "lhc%d%d" % (i, s)],
+                   act(T.lhd[:, a], T.lhd[:, a], accum_out=T.lhc[:, 2 * i + s:2 * i + s + 1]))
+
+    def edge_tiles(step):
+        if step == 0:
+            for s in range(2):
+                op("v", ["irow", "lhc0%d" % s], ["sele%d" % s], ts(T.sele[:, s:512:4], T.irow[:, 0:128], T.lhc[:, s:s + 1], float(STEP), A.is_equal, A.mult))
+        elif step == 1:
+            for s in range(2):
+                op("v", ["krow", "lhc1%d" % s], ["k01e%d" % s], ts(T.k01e[:, 12 * s:12 * s + 12], T.krow[:, 0:12], T.lhc[:, 2 + s:3 + s], None, A.is_equal))
+        else:
+            quant("qse", 0, 128, T.sele[:], ["sele0", "sele1", "sele2", "sele3"], "qse")
+            op("v", ["k01e0", "k01e1"], ["k01e0", "k01e1"], lambda: vec.memset(T.k01e[96:128, :], 0.0))
+
+    def slots(step):
+        if step == 0:
+            op("v", ["diag"], ["latch"], ts(T.latch[:], T.diag[:], 512.0, -256.0, A.mult, A.add))
+            op("v", ro, ["k2"], ts(T.k2[:], T.ro[:], -(E - 1) / 2.0, 1.0 / E, A.add, A.mult))
+        elif step <= N:
+            h = step - 1
+            op("v", ["k2"], ["mk%d" % h], ts(T.mk[:, 12 * h:12 * h + 12], T.k2[:], float(h), None, A.is_equal))
+        elif step == 5:
+            for h in range(N):
+                a = slice(E * h, E * h + E)
+                op("v", ["cum%d" % h, "latch"], ["lat%d" % h], scan(T.lat[:, a], T.latch[:], T.cum[:, a], 0.0, A.max, A.min))
+        elif step == 6:
+            op("v", ["lat%d" % h for h in range(N)] + ["mk%d" % h for h in range(N)], ["mq"], tt(T.mq[:], T.lat[:, 15:N * E:16], T.mk[:], A.mult))
+        elif step == 7:
+            op("v", ["mq"], ["f1"], tt(T.f1[:], T.mq[:, 0:24], T.mq[:, 24:48], A.add))
+        elif step == 8:
+            op("v", ["f1"], ["f2"], tt(T.f2[:], T.f1[:, 0:12], T.f1[:, 12:24], A.add))
+        else:
+            op("v", ["f2"], ["so"], copy(T.so[:], T.f2[:]))
 
     def node_terms():
         for b in range(4):
@@ -339,60 +402,56 @@ def rank_program(g, core, T, topo):
             else:
                 op("v", ["%s%d" % (bank, b)], ["%s%d" % (tile, b)], ts(dst, src, scale, None, A.mult))
 
-    def products(t):
+    def products(name, a, key):
         for o in range(O):
-            mm("pz", o, E, "qw", 128 * o, "qw", "qo%d" % t, 0, "qo%d" % t, True, True)
+            mm("pz", o, E, "qw", 128 * o, "qw", name, a, key, True, True)
 
-    def results(t, o, q):
-        src, dst = T.pz[:, 512 * o:512 * o + E], T["yb%d" % t][:, E * o:E * o + E]
-        op(q, ["pz%d" % o], ["yb%d_%d" % (t, o)], act(dst, src) if q == "s" else (lambda: vec.tensor_copy(dst, src)))
+    def results(name, a, o, q):
+        src, dst = T.pz[:, 512 * o:512 * o + E], T[name][:, a:a + E]
+        op(q, ["pz%d" % o], ["%s_%d" % (name, a)], act(dst, src) if q == "s" else copy(dst, src))
 
-    def store_results(t, after):
-        store("y", ["yb%d_%d" % (t, o) for o in range(O)] + after, T.y[:, t * O * E:(t + 1) * O * E], T["yb%d" % t][:])
+    def store_results(c, name, a, n, after):
+        store("y", ["%s_%d" % (name, a + E * i) for i in range(n)] + after, T.y[:, c * E:(c + n) * E], T[name][:, a:a + n * E])
+
+    upe = T.yw[:, 5 * E:6 * E]
 
     def tally(t):
         flags = T.wc[:, 0:LA].indirect(T["off%d" % t][:, 0:12])
         if t == 0:
-            op("v", ["wc", "off0"], ["acc"], lambda: vec.tensor_copy(T.acc[:], flags))
+            op("v", ["wc", "off0"], ["acc"], copy(T.acc[:], flags))
         elif t < R - 1:
             op("v", ["wc", "off%d" % t, "acc"], ["acc"], tt(T.acc[:], flags, T.acc[:], A.add))
         else:
-            op("v", ["wc", "off%d" % t, "upe"], ["upo"], tt(T.upo[:], flags, T.upe[:], A.add))
-
-    def edge_columns():
-        for i in range(2):
-            for s in range(2):
-                a = slice(E * i + 96 * s, E * i + 96 * s + 96)
-                op("s", ["lhd%d%d" % (i, s)], ["lhd%d%d" % (i, s), "lhc%d%d" % (i, s)],
-                   act(T.lhd[:, a], T.lhd[:, a], accum_out=T.lhc[:, 2 * i + s:2 * i + s + 1]))
-
-    def edge_tiles():
-        for s in range(2):
-            op("v", ["irow", "lhc0%d" % s], ["sele%d" % s], ts(T.sele[:, s:512:4], T.irow[:, 0:128], T.lhc[:, s:s + 1], float(STEP), A.is_equal, A.mult))
-        for s in range(2):
-            op("v", ["krow", "lhc1%d" % s], ["k01e%d" % s], ts(T.k01e[:, 12 * s:12 * s + 12], T.krow[:, 0:12], T.lhc[:, 2 + s:3 + s], None, A.is_equal))
-        quant("qse", 0, 128, T.sele[:], ["sele0", "sele1", "sele2", "sele3"], "qse")
-        op("v", ["k01e0", "k01e1"], ["k01e0", "k01e1"], lambda: vec.memset(T.k01e[96:128, :], 0.0))
+            op("v", ["wc", "off%d" % t, "upe"], ["upo"], tt(T.upo[:], flags, upe, A.add))
 
     node_terms()
     for t in range(R):
         x, nx, qa, qo, off = "x%d" % t, "x%d" % (t + 1), "qa%d" % t, "qo%d" % t, T["off%d" % t]
         last = t == R - 1
+        held = "qo%d" % (t - 1)
         if t > 0:
             px = "x%d" % (t - 1)
+            if t == 1:
+                slots(6)
             pick(x, HR, HR + 3 * PAIR, x + "h", px, HR, XW, [px + "h", px + "c", px + "l"], T["lo%d" % (t - 1)][:, 0:9], ["lo%d" % (t - 1)])
         for j in range(3):
-            pick(qa, E * j, E * j + E, "%s_%d" % (qa, j), x, 0, HR + 3 * PAIR, [x + "m", x + "h"], T.ao[:, 12 * j:12 * j + 12], ["ao"])
+            if t == 1:
+                slots(7 + j)
+            if t == 0 and j == 1:
+                cut_list(2)
+            pick(qa, E * j, E * j + E, "%s_%d" % (qa, j), x, 0, HR + 3 * PAIR, [x + "m", x + "h"], T.ao[:, 12 * j:12 * j + 12], ["ao%d" % j])
             for b in range(4):
                 mm("pz", b, E, "qe", 128 * b, "qe%d" % b, qa, E * j, "%s_%d" % (qa, j), False, j == 2)
         if t == 0:
-            for b in (2, 3):
-                quant("qn", 128 * b, 128 * b + 128, T.ezn[:, 3 - b:515 - b], ["ezn"], "qn%d" % b)
+            for b in range(1, 4):
+                minus_tile(b)
+            op("v", ["irow", "pf"], ["diag"], ts(T.diag[:], T.irow[:], q16, None, A.is_equal))
             minus_held(0)
-        elif last:
-            edge_tiles()
+            sizes_tile()
         else:
-            quant("qw", 0, 128 * O, T.wt[:], ["wt"], "qw")
+            pick(held, 0, E, held, x, MS, MS + E, [x + "m"], T.so[:, 0:12], ["so"])
+            if last:
+                edge_tiles(2)
         to_tile("zt", "pz", 0.25)
         quant(x, CA, CA + E, T.zt[:], ["zt0", "zt1", "zt2", "zt3"], x + "c")
         if not last:
@@ -401,30 +460,46 @@ def rank_program(g, core, T, topo):
         for b in range(4):
             mm("py", b, E, "qe", 128 * b, "qe%d" % b, x, CA, x + "c", False, True)
         if t == 0:
+            for s in range(2):
+                op("s", ["diag"], ["sel%d" % s], act(T.sel[:, s:512:4], T.diag[:, 0:128], scale=float(STEP)))
+            table_rows("sel")
             quant("qu", 0, 176, T.ub[:], ["uba", "ubb", "ub0", "ub1", "ub2", "ub3"], "qu")
-            quant("qs", 0, 128, T.sel[:], ["sel0", "sel1", "sel2", "sel3"], "qs")
-            table_rows("sele")
+            k01(0)
+            k01(1)
+            op("g", [], ["wc"], iota(T.wc[:], [[1, 2], [0, LA // 2]], 0))
+            op("v", ["k010"], ["k010"], lambda: vec.memset(T.k01[96:128, 0:NT], 0.0))
         else:
-            products(t - 1)
-        in_edge_order = ("qo%d" % (t - 1), CA, CA + E, "qce", x, CA, CA + E, [x + "c"], T.so[:, 0:12], ["so"])
+            if not last:
+                quant("qw", 0, 128 * O, T.wt[:], ["wt"], "qw")
+            products(held, 0, held)
+        if t == 1:
+            edge_numbers(1)
+            edge_select()
         if last:
-            op("s", ["k01e0", "k01e1"], ["kke"], act(T.kke[:], T.k01e[:], ACT.Identity, bias=OFFK, scale=CAP - OFFK))
-            pick_codes(*in_edge_order)
+            pick(held, CA, CA + E, "qce", x, CA, CA + E, [x + "c"], T.so[:, 0:12], ["so"])
         to_tile("yt", "py", 1.0)
         quant("qy", 0, YW, T.yt[:], ["yt0", "yt1", "yt2", "yt3", "ytp"], "qy")
         if t == 0:
-            edge_columns()
+            op("s", ["k010", "k011"], ["kk"], act(T.kk[:], T.k01[:], ACT.Identity, bias=OFFK, scale=CAP - OFFK))
+            quant("qs", 0, 128, T.sel[:], ["sel0", "sel1", "sel2", "sel3"], "qs")
+            slots(0)
+        elif not last:
+            for o in range(O):
+                results("yb0", E * o, o, "s")
+            tally(0)
         else:
-            for o in range(O - 1 if last else O):
-                results(t - 1, o, "s")
-        if last:
-            results(t - 1, O - 1, "v")
-            store_results(t - 1, [])
+            op("s", ["k01e0", "k01e1"], ["kke"], act(T.kke[:], T.k01e[:], ACT.Identity, bias=OFFK, scale=CAP - OFFK))
+            for o in range(O):
+                results("yw", YP[o], o, "v" if o == 1 else "s")
+            store_results(O, "yw", YP[0], 2, [])
+            store_results(O + 2, "yw", YP[2], 1, [])
         mm("py", 0, 144, "qu", PAIR, "qu", "qy", 0, "qy", True, False)
         mm("py", 0, 144, "qu", 0, "qu", "qy", PAIR, "qy", False, True)
         for s in range(2):
             mm("py", 1 + s, 128, "qy", 96 * s, "qy", "qu", PAIR, "qu", True, True)
-        if not last:
+        if last:
+            products(held, CA, "qce")
+        else:
             node_terms()
         op("s", ["py0"], ["dd"], act(T.dd[:], T.py[:, 0:144], ACT.Abs))
         for s in range(2):
@@ -434,19 +509,32 @@ def rank_program(g, core, T, topo):
             a, d, own = slice(PAIR * s, PAIR * s + PAIR), T.dd[:, 96 * s:96 * s + PAIR], T.nc[:, s:s + 1]
             op("v", ["dd", "nc%d" % s], ["eq%d" % s], ts(T.eq[:, a], d, own, None, A.is_equal))
             op("s", ["dd", "nc%d" % s], ["sg%d" % s, "cnt%d" % s], act(T.sg[:, a], d, ACT.Sign, bias=own, scale=-1.0, accum_out=T.cnt[:, s:s + 1]))
+        if t == 0:
+            slots(1)
         if last:
-            pick_scales(*in_edge_order)
-            op("s", ["acc", "so"], ["upe"], act(T.upe[:], T.acc[:, 0:E].indirect(T.so[:, 0:12])))
+            for o in range(O):
+                results("yw", YP[o] + STEP, o, "s")
+            op("s", ["acc", "so"], ["upe"], act(upe, T.acc[:, 0:E].indirect(T.so[:, 0:12])))
         for s in range(2):
             a = slice(PAIR * s, PAIR * s + PAIR)
             op("v", ["eq%d" % s, "flip"], ["tie%d" % s], scan(T.tie[:, a], T.flip[:], T.eq[:, a], 0.0, A.mult, A.add))
+        if t == 0:
+            slots(2)
         kk, nt, qs = ("kke", 12, "qse") if last else ("kk", NT, "qs")
         for s in range(2):
             op("v", ["cnt%d" % s, "tie%d" % s, kk], ["xt%d" % s],
                ts(T.xt[:, s:4 * nt:4], T[kk][:, nt * s:nt * s + nt], T.cnt[:, s:s + 1], T.tie[:, PAIR * s + PAIR - 1:PAIR * s + PAIR], A.subtract, A.is_lt))
+        if t == 0:
+            slots(3)
         quant("qx", 0, 128, T.xt[:], ["xt0", "xt1", "xtc", "xtc0", "xtc1", "xtc2", "xtc3", "xtc4"], "qx")
+        if t == 0:
+            slots(4)
+        if t == 1:
+            edge_columns()
+            table_rows("sele")
+            edge_tiles(1)
         mm("py", 3, 128, qs, 0, qs, "qx", 0, "qx", True, True)
-        op("v", ["py3"], ["off%d" % t], lambda off=off, nt=nt: vec.tensor_copy(off[:, 0:nt], T.py[:, 1536:1536 + nt]))
+        op("v", ["py3"], ["off%d" % t], copy(off[:, 0:nt], T.py[:, 1536:1536 + nt]))
         if last:
             break
         lo = T["lo%d" % t]
@@ -454,22 +542,29 @@ def rank_program(g, core, T, topo):
              [(off[:, 12 + 3 * i:15 + 3 * i], lo[:, 3 * blk(r, h):3 * blk(r, h) + 3]) for i, h in enumerate(others)])
         landed(["lo%d" % t], "af%d" % t, arriving((True,)))
         pick(nx, MS, MS + E, nx + "m", x, 0, LA, [x + "m", x + "h", x + "c"], off[:, 0:12], ["off%d" % t])
-        tally(t)
-        pick(qo, 0, E, qo, nx, MS, MS + E, [nx + "m"], T.so[:, 0:12], ["so"])
+        if t == 0:
+            edge_numbers(0)
+            slots(5)
+        else:
+            tally(t)
+            edge_tiles(0)
         minus_held(t + 1)
         if t > 0:
-            store_results(t - 1, ["lo%d" % t])
-    held = "qo%d" % (t - 1)
-    pick(qo, 0, E, qo, held, 0, LA, [held, "qce"], off[:, 0:12], ["off%d" % t])
-    products(t)
-    store("y", [qo], T.oc[:], T[qo][:, 0:E].bitcast(dt.uint8))
-    for k in range(4):
-        store("y", [qo + "s"], T.osc[4 * k:4 * k + 4, :], T[qo + "s"][32 * k:32 * k + 4, :])
-    tally(t)
+            store_results(0, "yb0", 0, O, ["lo%d" % t])
+
+    both = ["yw_%d" % (a + d) for a in YP for d in (0, STEP)] + ["upe", "off%d" % t]
     for o in range(O):
-        results(t, o, "v" if o == 1 else "s")
-        store("y", ["yb%d_%d" % (t, o)], T.y[:, (t * O + o) * E:(t * O + o + 1) * E], T["yb%d" % t][:, E * o:E * o + E])
-    store("s", ["upo"], T.up[:], T.upo[0:1, :])
+        out, win = T.yb2[:, E * o:E * o + E], T.yw[:, YP[o]:YP[o] + LA].indirect(off[:, 0:12])
+        op("s" if o else "v", both, ["yb2_%d" % (E * o)], act(out, win) if o else copy(out, win))
+    pick(qo, 0, E, qo, held, 0, LA, [held, "qce"], off[:, 0:12], ["off%d" % t])
+    tally(t)
+    store_results(t * O, "yb2", 0, 1, [])
+    store_results(t * O + 1, "yb2", E, 1, [])
+    store("y", [qo], T.oc[:], T[qo][:, 0:E].bitcast(dt.uint8))
+    store_results(t * O + 2, "yb2", 2 * E, 1, [])
+    store("y", ["upo"], T.up[:], T.upo[0:1, :])
+    for k in range(4):
+        store("s" if k % 2 else "y", [qo + "s"], T.osc[4 * k:4 * k + 4, :], T[qo + "s"][32 * k:32 * k + 4, :])
 
     for s in ("cv", "cs", "cp", "cg", "sent", "st"):
         g.wait_ge(T.sem[s], count[s])

@@ -3,15 +3,35 @@ from concourse.mybir import dt, AluOpType, AxisListType, ActivationFunctionType
 
 N, V, E, PAIR, CAP, R, O = 4, 48, 192, 48, 16, 3, 3
 X4, U8, BF, F32, I32, U16 = "float8_e4m3fn_x4", "uint8", "bfloat16", "float32", "int32", "uint16"
-MS, HR, CA, LA, XW = 0, 192, 384, 576, 720
-STEP = CA - MS
-IW = (2 * N - 1) * E
-YP = (0, E, 4 * E)
-YW = E + 32
+FAR = (N - 1) * PAIR
+STEP, HSTEP = 512, 896
+HR, CA, LA, XW = E, STEP, E + STEP, E + HSTEP
+TW = 128
+LAST = E - 128
+YP = (0, E, STEP + 2 * E)
 NW = E - 2 * 16
-OFFK = 64.0
-SHIFT = 80
-NT = 21
+OFFK = 128.0
+NT, NE = 21, 36
+UNIT = 136.0
+
+ORDER = [int(_i) for _i in """
+0 1 5 19 17 13 3 11 16 15 14 9 21 25 18 10 22 20 12 28 27 26 2 4 29 30 24 80 23 68 32 33 31 35 69 38 39 37 36 40 34 41
+55 47 57 58 56 59 61 63 60 62 64 65 71 84 77 85 66 81 90 52 78 43 51 72 67 82 42 86 7 50 83 93 75 6 74 76 73 48 8 53 91
+88 70 87 94 89 45 46 95 97 112 106 117 116 79 96 107 99 102 98 92 100 108 101 105 118 125 111 103 115 119 120 160 114
+113 126 54 127 109 123 139 132 121 134 133 122 124 128 110 141 151 129 131 140 130 138 135 104 137 136 142 148 144 147
+168 149 146 145 150 171 143 172 173 162 152 154 156 155 163 183 215 153 159 229 161 164 157 167 166 187 165 169 177 170
+180 174 179 175 178 176 195 185 182 193 49 44 184 181 250 194 192 188 245 189 236 191 186 190 256 249 198 199 201 197
+203 196 202 200 158 247 209 210 206 207 204 213 208 211 248 205 217 246 216 364 220 222 214 238 219 218 224 225 223 237
+227 226 257 212 232 231 233 235 261 234 239 253 240 270 241 243 244 251 259 260 252 221 228 262 263 264 265 271 273 272
+266 279 280 267 268 269 286 275 287 274 277 284 242 282 281 276 283 292 293 290 294 289 314 278 291 288 301 315 295 285
+298 299 297 300 307 302 310 311 312 313 254 317 323 320 324 321 325 322 326 318 304 255 319 362 316 327 309 329 328 305
+330 230 333 334 335 336 337 341 303 340 346 339 347 338 348 296 342 343 344 349 350 345 351 352 370 258 372 353 357 354
+371 355 358 356 392 359 385 360 361 365 366 367 368 369 376 332 374 375 308 377 382 378 381 306 373 386 379 384 380 383
+390 387 389 393 396 401 400 388 399 398 331 397 402 403 394 408 409 395 405 414 407 415 404 406 413 424 425 411 410 416
+412 363 419 431 418 426 417 421 429 428 427 437 432 422 423 420 430 433 440 434 435 436 449 442 439 443 438 444 445 450
+441 446 447 455 456 457 458 459 462 463 452 464 391 465 466 467 468 448 451 461 472 473 471 453 460 474 454 475 470 476
+469 477 478 481 482 483 484 487 486 489 488 490 479 485 492 480 495 496 491 497 494 493
+""".split()]
 
 SCRATCH = {}
 
@@ -28,25 +48,26 @@ def _mx(name, n):
 for _n, _w, _d in (
         ("rt", 12, I32), ("mb", 4 * (E + V), BF), ("ut", 512, BF), ("wt", 1536, BF),
         ("ones", 516, BF), ("ez", 516, BF), ("ezn", 516, BF), ("irow", E, BF),
-        ("diag", E, BF), ("latch", E, BF), ("pcol", 1, I32), ("pi", 4, I32), ("pf", 4, F32), ("thr", 12, F32),
-        ("c16", 12, F32), ("sp", 12, F32), ("si", 18, I32), ("sj", 36, F32), ("lo3", 36, U16),
-        ("ind", IW, BF), ("cum", N * E, BF), ("occ2", 768, BF),
-        ("cum2", 768, BF), ("k2", 12, I32), ("mk", 48, F32), ("mq", 48, F32), ("ro", 12, U16),
-        ("hit", N * E, BF), ("lat", N * E, BF), ("na", 6 * E, BF), ("nb", 6 * NW, BF), ("nw", 6 * NW, BF), ("ca", 6, F32),
-        ("f1", 24, F32), ("f2", 12, F32), ("so", 12, U16), ("iof", 12, U16),
-        ("b2", 12, I32), ("bo", 12, U16), ("rb", E, BF), ("am", 3 * E, BF),
-        ("asc", 3 * E, BF), ("ao", 36, U16), ("ub", 704, BF), ("sel", 512, BF), ("xt", 512, BF), ("flip", PAIR, BF),
-        ("krow", NT, F32), ("k01", 2 * NT, F32), ("kk", 2 * NT, F32), ("wc", LA, BF), ("acc", E, F32), ("upo", E, F32),
-        ("zt", 4 * E, BF), ("yt", 4 * YW, BF), ("dd", 144, F32), ("nc", 2, F32), ("sg", 96, BF), ("eq", 96, BF),
-        ("tie", 96, F32), ("cnt", 2, F32), ("hrow", E, BF), ("lh", 2 * E, BF), ("lhd", 2 * E, BF), ("lhc", 4, F32),
-        ("sele", 512, BF), ("k01e", 24, F32), ("kke", 24, F32), ("yw", IW, F32)):
+        ("latch", E, BF), ("pi", 6, I32), ("pf", 17, F32), ("thr", 6, F32),
+        ("iff", 16, F32), ("five", 96, BF), ("fl", 108, BF), ("sj", 96, F32), ("lo3", 48, U16),
+        ("ind", (N + 1) * E, BF), ("cum", 2 * E, BF), ("occ2", N * E, BF),
+        ("cum2", N * E, BF), ("k2", 12, I32), ("mk", 24, F32), ("mq", 24, F32), ("ro", 12, U16),
+        ("hit", 2 * E, BF), ("lat", 2 * E, BF), ("na", 4 * E, BF), ("nb", 2 * NW, BF), ("ca", 6 * NW, F32),
+        ("f1", 36, F32), ("so", 14, U16), ("iof", 12, U16), ("bo", 12, U16), ("rb", E, BF), ("am", 3 * E, BF),
+        ("asc", 3 * E, BF), ("ao", 46, U16), ("ub", 704, BF), ("sel", 512, BF), ("xt", 512, BF), ("flip", PAIR, BF),
+        ("krow", NE, F32), ("kk", 2 * NT, F32),
+        ("zt", 4 * E, BF), ("yt", 4 * (PAIR + E), BF), ("dd", 144, F32), ("dh", 50, F32), ("nc", 2, F32),
+        ("sg", 3 * PAIR, BF), ("eq", 3 * PAIR, BF), ("tie", 3 * PAIR, F32), ("cnt", 3, F32), ("hrow", E, BF),
+        ("lh", 2 * E, BF), ("lhd", 2 * E, BF), ("lhc", 4, F32), ("sele", 512, BF),
+        ("kke", 2 * NE, F32), ("yw", YP[2] + STEP + E, F32), ("was", 6, F32), ("wj", 24, BF), ("upt", 48, F32)):
     _sb(_n, _w, _d)
-for _n, _w in (("qm", E + V), ("qe", 512), ("qn", 512), ("qu", 176), ("qw", 384), ("qs", 128), ("qb", E), ("qy", YW),
-               ("qx", 128), ("x0", XW), ("x1", XW), ("x2", LA), ("qo0", E), ("qo1", LA), ("qo2", E), ("qse", 128)):
+for _n, _w in (("qm", E + V), ("qe", 512), ("qn", 512), ("qu", 176), ("qw", 384), ("qs", 128), ("qb", 2 * E),
+               ("qh", 128), ("qx", 128), ("x0", XW), ("x1", XW), ("x2", CA + E), ("qo0", E), ("qo1", CA + E), ("qo2", E),
+               ("qse", 128)):
     _mx(_n, _w)
 for _t in range(R):
     _mx("qa%d" % _t, 3 * E)
-    _sb("off%d" % _t, 24, U16)
+    _sb("off%d" % _t, 22, U16)
 for _t in range(R - 1):
     _sb("yb%d" % (2 * _t), O * E, F32)
     _sb("lo%d" % _t, 16, U16)
@@ -54,6 +75,12 @@ SCRATCH["pz"] = ("psum", [128, 2048], F32)
 SCRATCH["py"] = ("psum", [128, 2048], F32)
 
 SEMAPHORES = ["cv", "cs", "cp", "cg", "ldr", "ldm", "ldu", "ldw", "st", "sent", "ad0", "ad1", "ad2", "af0", "af1"]
+
+
+def heads(r):
+    near = r + 1 - 2 * (r % 2)
+    rest = [h for h in range(N) if h not in (r, near)]
+    return (rest[::-1] if near > r else rest) + [near, r]
 
 
 def rank_program(g, core, T, topo):
@@ -65,7 +92,7 @@ def rank_program(g, core, T, topo):
     SEM = {"v": "cv", "s": "cs", "p": "cp", "g": "cg"}
     count = {"cv": 0, "cs": 0, "cp": 0, "cg": 0, "st": 0, "sent": 0}
     known = {q: {} for q in Q}
-    wrote, readers = {}, {}
+    wrote, readers, plan = {}, {}, []
 
     def settle(q, reads, writes):
         need = []
@@ -101,6 +128,11 @@ def rank_program(g, core, T, topo):
 
     def op(q, reads, writes, call):
         writes = list(writes) + [k for k in reads if k[:2] in ("pz", "py")]
+        if q == "g" and "gq" not in writes:
+            reads = list(reads) + ["gq"]
+        plan.append((q, list(reads), writes, lambda: compute(q, reads, writes, call)))
+
+    def compute(q, reads, writes, call):
         settle(q, reads, writes)
         s = SEM[q]
         count[s] += 1
@@ -111,9 +143,11 @@ def rank_program(g, core, T, topo):
         Q[q].dma_start(out, in_).then_inc(T.sem[sem], 16)
 
     def store(q, reads, out, in_):
-        settle(q, reads, [])
-        count["st"] += 16
-        Q[q].dma_start(out, in_).then_inc(T.sem.st, 16)
+        def call():
+            settle(q, reads, [])
+            count["st"] += 16
+            Q[q].dma_start(out, in_).then_inc(T.sem.st, 16)
+        plan.append((q, list(reads), [], call))
 
     vec, sca, pe = g.vector, g.scalar, g.tensor
 
@@ -131,6 +165,9 @@ def rank_program(g, core, T, topo):
     def act(out, in_, func=None, **kw):
         return lambda: sca.activation(out, in_, ACT.Copy if func is None else func, **kw)
 
+    def line(out, in_, scale, bias):
+        return act(out, in_, ACT.Identity, bias=bias, scale=scale)
+
     def scan(out, d0, d1, first, op0, op1):
         return lambda: vec.tensor_tensor_scan(out, d0, d1, first, op0, op1)
 
@@ -140,26 +177,29 @@ def rank_program(g, core, T, topo):
     def quant(name, a, b, tile, reads, key):
         op("v", reads, [key, key + "s"], lambda: vec.quantize_mx(T[name][:, a:b], T[name + "s"][:, a:b], tile))
 
-    def pick_codes(dst, c, d, dkey, src, a, b, skeys, off, okeys):
-        op("v", skeys + okeys, [dkey], lambda: vec.tensor_copy(
+    def pick_codes(dst, c, d, dkeys, src, a, b, skeys, off, okeys):
+        op("v", skeys + okeys, dkeys, lambda: vec.tensor_copy(
             T[dst][:, c:d].bitcast(dt.uint32), T[src][:, a:b].bitcast(dt.uint32).indirect(off)))
 
-    def pick_scales(dst, c, d, dkey, src, a, b, skeys, off, okeys):
-        op("s", [k + "s" for k in skeys] + okeys, [dkey + "s"], act(T[dst + "s"][:, c:d], T[src + "s"][:, a:b].indirect(off)))
+    def pick_scales(dst, c, d, dkeys, src, a, b, skeys, off, okeys):
+        op("s", [k + "s" for k in skeys] + okeys, [k + "s" for k in dkeys],
+           act(T[dst + "s"][:, c:d], T[src + "s"][:, a:b].indirect(off)))
 
     def pick(*a):
         pick_codes(*a)
         pick_scales(*a)
 
-    def mm(bank, b, n, lname, la, lkey, rname, ra, rkey, start, stop):
-        op("p", [lkey, lkey + "s", rkey, rkey + "s"], ["%s%d" % (bank, b)], lambda: pe.matmul_mx(
+    def mm(bank, b, n, lname, la, lkey, rname, ra, rkeys, start, stop):
+        keys = [lkey] + rkeys
+        op("p", keys + [k + "s" for k in keys], ["%s%d" % (bank, b)], lambda: pe.matmul_mx(
             T[bank][:, 512 * b:512 * b + n], T[lname][:, la:la + 128], T[lname + "s"][:, la:la + 128],
             T[rname][:, ra:ra + n], T[rname + "s"][:, ra:ra + n], start, stop))
 
-    others = [(r + d) % N for d in range(1, N)]
+    hd = heads(r)
+    others = hd[:N - 1]
 
     def blk(src, dst):
-        return src if src < dst else src - 1
+        return heads(src).index(dst)
 
     def dest(h):
         rid, pid, _ = topo.addr(T.cores[h])
@@ -167,34 +207,38 @@ def rank_program(g, core, T, topo):
 
     def masks(src, first):
         out = []
-        for i in range(N - 1):
-            eng = topo.engines(T.cores[src], T.cores[(src + 1 + i) % N])
+        for i, h in enumerate(heads(src)[:N - 1]):
+            eng = topo.engines(T.cores[src], T.cores[h])
             n = len(eng)
             part = [eng[:n // 2], eng[n // 2:3 * n // 4], eng[3 * n // 4:]] if first else \
                    [eng[n // 2:], eng[:n // 4], eng[n // 4:n // 2]]
             out.append(part[i])
         return out
 
-    def send(reads, sem, first, pairs):
-        settle("g", reads, [])
+    def send(reads, sem, first, pairs, lands):
         ms = masks(r, first)
-        count["sent"] += sum(len(m) for m in ms)
-        g.remote_dma_fused([RemoteDMATransfer(dst_ids=[dest(h)], dma_engine_mask=sum(1 << e for e in ms[i]),
-                                              remote_sem=T.sem[sem], src=pairs[i][0], dst=pairs[i][1])
-                            for i, h in enumerate(others)], local_sem=T.sem.sent)
+
+        def call():
+            settle("g", reads, [])
+            count["sent"] += sum(len(m) for m in ms)
+            g.remote_dma_fused([RemoteDMATransfer(dst_ids=[dest(h)], dma_engine_mask=sum(1 << e for e in ms[i]),
+                                                  remote_sem=T.sem[sem], src=pairs[i][0], dst=pairs[i][1])
+                                for i, h in enumerate(others)], local_sem=T.sem.sent)
+        plan.append(("g", list(reads), ["out"] + lands, call))
 
     def arriving(firsts):
-        return sum(len(masks(s, f)[(r - s - 1) % N]) for s in others for f in firsts)
-
-    def send_block(name, a, z, key, sem):
-        c, s = T[name], T[name + "s"]
-        at = [(a + PAIR * h, z + PAIR * blk(r, h)) for h in others]
-        send([key], sem, True, [(c[:, i:i + PAIR].bitcast(dt.uint8), c[:, j:j + PAIR].bitcast(dt.uint8)) for i, j in at])
-        send([key + "s"], sem, False, [(s[:, i:i + PAIR], s[:, j:j + PAIR]) for i, j in at])
+        return sum(len(masks(s, f)[blk(s, r)]) for s in others for f in firsts)
 
     def landed(keys, sem, n):
         for k in keys:
             wrote[k] = (sem, n, {})
+
+    def send_block(name, a, z, key, sem, lands):
+        c, s = T[name], T[name + "s"]
+        at = [(a + PAIR * i, z + PAIR * i) for i in range(N - 1)]
+        send([key], sem, True, [(c[:, i:i + PAIR].bitcast(dt.uint8), c[:, j:j + PAIR].bitcast(dt.uint8)) for i, j in at], [])
+        send([key + "s"], sem, False, [(s[:, i:i + PAIR], s[:, j:j + PAIR]) for i, j in at], [lands, lands + "s"])
+        landed([lands, lands + "s"], sem, arriving((True, False)))
 
     for k in range(2):
         load("y", "ldr", T.rt[32 * k:32 * k + 16, :], T.rev[:])
@@ -208,64 +252,40 @@ def rank_program(g, core, T, topo):
     landed(["ut"], "ldu", 16)
     landed(["wt"], "ldw", 16)
 
-    ones = T.ones
-    op("g", [], ["pcol"], lambda: g.iota(T.pcol[:], [[0, 1]], 0, 1))
+    ones, pf = T.ones, T.pf
+    q16, odd, g16, half, pcol = (pf[:, i:i + 1] for i in range(5))
+    steps, spare = pf[:, 13:14], pf[:, 14:15]
+    op("g", [], ["pi4"], lambda: g.iota(T.pi[:, 4:5], [[0, 1]], 0, 1))
     op("v", [], ["ones"], lambda: vec.memset(ones[:], 1.0))
-    op("g", [], ["c16"], iota(T.c16[:], [[16, 12]], 0))
+    op("g", [], ["c16"], iota(T.thr[:, 3:6], [[16, 3]], 0))
     op("g", ["ones"], ["ez"], lambda: g.affine_select(T.ez[:], ones[:], [[1, 516]], A.is_equal, 0.0, -3, -4))
     op("g", [], ["irow"], iota(T.irow[:], [[0, 12], [1, 16]], 0))
-    for i, (a, z, v) in enumerate(((576, 768, 1.0), (768, 1152, 0.0), (1152, IW, 0.0))):
-        op("s", ["ones"], ["ind%d" % i], act(T.ind[:, a:z], ones[:, 0:z - a], scale=v))
-    for i, (s1, o) in enumerate(((15, A.bitwise_and), (16, A.bitwise_and), (4, A.arith_shift_right))):
-        op("v", ["pcol"], ["pi%d" % i], ts(T.pi[:, i:i + 1], T.pcol[:], s1, None, o))
-    op("v", [], ["ind3"], lambda: vec.memset(T.ind[:, 0:576], 0.0))
-    op("v", ["pi0", "pi1", "pi2"], ["pf"], copy(T.pf[:, 0:3], T.pi[:, 0:3]))
-    op("v", [], ["occ2b"], lambda: vec.memset(T.occ2[:, 384:768], 0.0))
-    q16, odd16, g16, even16 = T.pf[:, 0:1], T.pf[:, 1:2], T.pf[:, 2:3], T.pf[:, 3:4]
-    op("v", ["c16", "pf"], ["thr"], ts(T.thr[:], T.c16[:], q16, -0.5, A.add, A.add))
-    op("s", ["pf"], ["pfe"], act(even16, odd16, ACT.Identity, bias=16.0, scale=-1.0))
-
-    ro = ["ro0", "ro1"]
-    for k in range(2):
-        op("v", ["rt"], [ro[k]], copy(T.ro[64 * k:64 * k + 64, :], T.rt[0:64, :]))
-    for h in range(N):
-        out, win = T.hit[:, E * h:E * h + E], T.ind[:, E * (N - 1 - h):E * (2 * N - 1 - h)].indirect(T.ro[:, 0:12])
-        op("v" if h < 2 else "s", ro + ["ind%d" % i for i in range(4)], ["hit%d" % h], copy(out, win) if h < 2 else act(out, win))
-    for h in (0, 2, 1, 3):
-        a = slice(E * h, E * h + E)
-        op("v", ["hit%d" % h, "ones"], ["cum%d" % h], scan(T.cum[:, a], ones[:, 0:E], T.hit[:, a], PAIR * h - 1.0, A.mult, A.add))
-    for c in range(6):
-        h, a = c // 3, 16 if c % 3 == 1 else 0
-        op("s", ["cum%d" % h, "thr"], ["ca%d" % c], act(T.na[:, E * c + a:E * c + E - a], T.cum[:, E * h + a:E * h + E - a], ACT.Sign,
-                                                      bias=T.thr[:, c:c + 1], scale=-1.0, accum_out=T.ca[:, c:c + 1]))
-    for c in range(6):
-        a = E * (2 + c // 3) + 16 * (c % 3)
-        op("v", ["cum%d" % (2 + c // 3), "thr"], ["nb%d" % c], ts(T.nb[:, NW * c:NW * c + NW], T.cum[:, a:a + NW], T.thr[:, 6 + c:7 + c], None, A.is_lt))
-    for c in range(6):
-        a = slice(NW * c, NW * c + NW)
-        op("v", ["nb%d" % c, "ones"], ["nw%d" % c], scan(T.nw[:, a], ones[:, 0:NW], T.nb[:, a], 16.0 * (c % 3), A.mult, A.add))
-    quant("qm", 0, E + V, T.mb[:], ["mb"], "qm")
-    op("v", ["nw%d" % c for c in range(6)], ["iof1"], copy(T.iof[:, 6:12], T.nw[:, NW - 1:6 * NW:NW]))
-    op("v", ["ca%d" % c for c in range(6)], ["iof0"], ts(T.iof[:, 0:6], T.ca[:], 0.5, E / 2.0, A.mult, A.add))
-    iof = ["iof0", "iof1"]
-    op("s", ["ones"], ["occ2a"], act(T.occ2[:, 0:384], ones[:, 0:384], scale=0.0))
-    pick("x0", MS, MS + E, "x0m", "qm", 0, E + V, ["qm"], T.iof[:, 0:12], iof)
-
-    def table_rows(name):
-        op("s", ["irow"], [name + "2"], act(T[name][:, 2:512:4], T.irow[:, 0:128]))
-        op("s", ["ones"], [name + "3"], act(T[name][:, 3:512:4], ones[:, 0:128]))
-
-    op("g", [], ["krow"], iota(T.krow[:, 0:12], [[1, 12]], 0))
-    for i, h in enumerate(others):
-        op("g", [], ["krow%d" % i], iota(T.krow[:, 12 + 3 * i:15 + 3 * i], [[1, 3]], 3 * h))
-    op("g", [], ["hrow"], iota(T.hrow[:], [[1, 12], [0, 16]], 0))
-
-    def k01(s):
-        op("v", ["krow", "krow0", "krow1", "krow2", "pf"], ["k01%d" % s],
-           ts(T.k01[:, NT * s:NT * s + NT], T.krow[:], -6.0 * s, g16, A.add, A.is_equal))
-
-    send_block("x0", MS, HR, "x0m", "ad0")
-    landed(["x0h", "x0hs"], "ad0", arriving((True, False)))
+    op("g", [], ["five"], iota(T.five[:], [[0, 48], [5, 2]], 0))
+    op("g", [], ["krow"], iota(T.krow[:], [[0, 3], [1, 12]], 0))
+    op("g", ["ones"], ["flip"], lambda: g.affine_select(T.flip[:], ones[:, 0:PAIR], [[1, PAIR]], A.not_equal, -1.0, 0, -1))
+    op("g", ["flip"], ["flip"], lambda: g.affine_select(T.flip[:], T.flip[:], [[1, PAIR]], A.not_equal, -1.0, PAIR, -1))
+    win = [E if hd[1] > hd[0] else 0, E if hd[0] > hd[1] else 0]
+    at = [win[0] // E + hd[0], win[0] // E + hd[2]]
+    for k in range(N + 1):
+        if k not in at:
+            op("s", ["ones"], ["ind%d" % k], act(T.ind[:, E * k:E * k + E], ones[:, 0:E], scale=0.0))
+    op("s", ["ones"], ["occ2b"], act(T.occ2[:, 2 * E:N * E], ones[:, 0:2 * E], scale=0.0))
+    op("v", ["pi4"], ["pi0"], ts(T.pi[:, 0:1], T.pi[:, 4:5], 15, None, A.bitwise_and))
+    op("v", ["pi4"], ["pi1"], ts(T.pi[:, 1:2], T.pi[:, 4:5], 4, 1, A.arith_shift_right, A.bitwise_and))
+    op("v", ["pi4"], ["pi2"], ts(T.pi[:, 2:3], T.pi[:, 4:5], 4, None, A.arith_shift_right))
+    op("v", ["pi4"], ["pi3"], ts(T.pi[:, 3:4], T.pi[:, 4:5], 6, None, A.arith_shift_right))
+    op("v", ["pi4"], ["pi5"], ts(T.pi[:, 5:6], T.pi[:, 4:5], 14, None, A.bitwise_and))
+    ind = ["ind%d" % k for k in range(N + 1) if k not in at]
+    for i in range(2):
+        for k in range(2):
+            ind.append("ind%d%d" % (i, k))
+            op("v", [], [ind[-1]], lambda i=i, k=k: vec.memset(T.ind[64 * k:64 * k + 64, E * at[i]:E * at[i] + E], float(i == k)))
+        if i == 0:
+            op("v", ["pi%d" % i for i in range(5)], ["pf"], copy(pf[:, 0:5], T.pi[:, 0:5]))
+    op("v", ["c16", "pf"], ["thr"], ts(T.thr[:, 0:3], T.thr[:, 3:6], q16, -0.5, A.add, A.add))
+    op("v", ["pi5", "pf"], ["twice"], ts(T.so[:, 12:13], T.pi[:, 5:6], odd, None, A.add))
+    op("v", [], ["iffp"], lambda: vec.memset(T.iff[:, 12:16], 0.0))
+    op("v", [], ["occ2a"], lambda: vec.memset(T.occ2[:, 0:2 * E], 0.0))
 
     def unpack_tile(b):
         quant("qe", 128 * b, 128 * b + 128, T.ez[:, 3 - b:515 - b], ["ez"], "qe%d" % b)
@@ -273,87 +293,138 @@ def rank_program(g, core, T, topo):
     def minus_tile(b):
         quant("qn", 128 * b, 128 * b + 128, T.ezn[:, 3 - b:515 - b], ["ezn"], "qn%d" % b)
 
+    ro = ["ro0", "ro1"]
+
+    def mark(k):
+        op("v", ro + ["ones"], ["occ2a", "occ2b"], copy(T.occ2[:, 0:N * E].indirect(T.ro[:, 4 * k:4 * k + 4]), ones[:, 0:64]))
+
     def places(h):
-        first = (MS + PAIR * h if h == r else HR + PAIR * blk(h, r)) - SHIFT - 1
+        first = (FAR if h == r else HR + PAIR * blk(h, r)) - TW - 1
         op("v", ["occ2a", "occ2b", "ones"], ["cum2%d" % h],
            scan(T.cum2[:, E * h:E * h + E], ones[:, 0:E], T.occ2[:, E * h:E * h + E], float(first), A.mult, A.add))
 
-    op("v", iof + ["pfe"], ["sp0"], ts(T.sp[:, 0:6], T.iof[:, 0:12:2], even16, 1.0 / 16, A.mult, A.mult))
-    op("v", iof + ["pf"], ["sp1"], ts(T.sp[:, 6:12], T.iof[:, 1:12:2], odd16, 1.0 / 16, A.mult, A.mult))
-    op("v", iof, ["b2"], ts(T.b2[:], T.iof[:], 0.25, E - 0.375, A.mult, A.add))
-    unpack_tile(0)
-    op("v", ["sp0", "sp1"], ["si0"], tt(T.si[:, 0:6], T.sp[:, 0:6], T.sp[:, 6:12], A.add))
-    op("v", ro + ["ones"], ["occ2a", "occ2b"], copy(T.occ2[:, 0:768].indirect(T.ro[:, 0:12]), ones[:, 0:E]))
-    op("v", ["si0"], ["si1"], ts(T.si[:, 6:12], T.si[:, 0:6], 3, None, A.bitwise_and))
-    op("v", ["si0"], ["si2"], ts(T.si[:, 12:18], T.si[:, 0:6], 252, None, A.bitwise_and))
-    op("v", ["b2"], ["bo"], copy(T.bo[:], T.b2[:]))
-    places(0)
-    for j in range(3):
-        op("v", ["si1"], ["sj%d" % j], ts(T.sj[:, 6 * j:6 * j + 6], T.si[:, 6:12], float(j), float(j), A.is_le, A.add))
-    for h in range(1, N):
-        places(h)
-    for j in range(3):
-        op("v", ["sj%d" % j, "si2"], ["sk%d" % j], tt(T.sj[:, 18 + 6 * j:24 + 6 * j], T.sj[:, 6 * j:6 * j + 6], T.si[:, 12:18], A.add))
-    unpack_tile(1)
     for k in range(2):
-        op("v", ["sk0", "sk1", "sk2"], ["lo3%d" % k], copy(T.lo3[:, k:36:2], T.sj[:, 18:36]))
-    op("s", ["ez"], ["ezn"], act(T.ezn[:], T.ez[:], scale=-1.0))
-    op("s", ["ones"], ["xt0", "xt1", "xtc"], act(T.xt[:], ones[:, 0:512], scale=0.0))
-    op("g", ["xtc"], ["xtc3"], iota(T.xt[0:1, 2:4 * NT:4], [[0, NT]], 1))
-    op("g", ["xtc"], ["xtc4"], iota(T.xt[0:1, 3:48:4], [[16, 12]], 0))
-    for i, h in enumerate(others):
-        op("g", ["xtc"], ["xtc%d" % i], iota(T.xt[0:1, 51 + 12 * i:60 + 12 * i:4], [[16, 3]], PAIR * blk(r, h)))
-    nodes = ("qb", 0, E, "qb", "qm", 0, E + V, ["qm"], T.bo[:, 0:12], ["bo"])
-    pick_scales(*nodes)
-    op("s", ["cum2%d" % h for h in range(N)] + ro, ["rb"], act(T.rb[:], T.cum2[:, 0:768].indirect(T.ro[:, 0:12])))
-    pick_codes(*nodes)
+        op("v", ["rt"], [ro[k]], copy(T.ro[64 * k:64 * k + 64, :], T.rt[0:64, :]))
+    for k in range(2):
+        out, w = T.hit[:, E * k:E * k + E], T.ind[:, win[k]:win[k] + N * E].indirect(T.ro[:, 0:12])
+        op("s" if k else "v", ro + ind, ["hit%d" % k], act(out, w) if k else copy(out, w))
+    mark(0)
+    for k in range(2):
+        a = slice(E * k, E * k + E)
+        op("v", ["hit%d" % k, "ones"], ["cum%d" % k], scan(T.cum[:, a], ones[:, 0:E], T.hit[:, a], -1.0, A.mult, A.add))
+    for i, c in enumerate((1, 0, 2, 4)):
+        k, a = c // 3, 16 if c % 3 == 1 else 0
+        op("s", ["cum%d" % k, "thr"], ["ca%d" % c], act(T.na[:, E * i + a:E * i + E - a], T.cum[:, E * k + a:E * k + E - a], ACT.Sign,
+                                                      bias=T.thr[:, c % 3:c % 3 + 1], scale=-1.0, accum_out=T.ca[:, NW * c + NW - 1:NW * c + NW]))
+    for i in range(2):
+        a = E + 32 * i
+        op("v", ["cum1", "thr"], ["nb%d" % i], ts(T.nb[:, NW * i:NW * i + NW], T.cum[:, a:a + NW], T.thr[:, 2 * i:2 * i + 1], 2.0, A.is_lt, A.mult))
+    for i in range(2):
+        c = 3 + 2 * i
+        op("v", ["nb%d" % i, "ones"], ["ca%d" % c], scan(T.ca[:, NW * c:NW * c + NW], ones[:, 0:NW], T.nb[:, NW * i:NW * i + NW], 64.0 * i - E, A.mult, A.add))
+    op("s", ["pf"], ["st0"], act(pf[:, 12:13], pcol, ACT.Sign, bias=0.5 - PAIR))
+    op("s", ["pf"], ["gs"], act(spare, pcol, ACT.Relu, bias=1.0 - 2 * PAIR))
+    op("s", ["pf"], ["gs1"], line(pf[:, 16:17], g16, 1.0, 6.0))
+    op("s", ["st0"], ["st1"], line(steps, pf[:, 12:13], (HSTEP - STEP) / 2.0, (HSTEP + STEP) / 2.0))
+    op("s", ["gs"], ["gs0"], line(pf[:, 15:16], spare, 16.0, g16))
+    for k in range(2):
+        op("s", ["pf"], ["hc%d" % k], line(pf[:, 10 + k:11 + k], half, float(hd[2 + k] - hd[k]), float(hd[k])))
+        op("s", ["pf"], ["ci%d" % k], line(pf[:, 8 + k:9 + k], half, 2.0 * PAIR, float(PAIR * k)))
+    for t in range(4):
+        op("s", ["ut", "ones"], ["ub%d" % t], line(T.ub[:, 192 + t:384:4], ones[:, 0:PAIR], 0.0, T.ut[:, t:t + 1]))
+    quant("qm", 0, E + V, T.mb[:], ["mb"], "qm")
 
-    def gather_list(j):
-        out, win = T.am[:, E * j:E * j + E], T.rb[:, 0:E].indirect(T.lo3[:, 12 * j:12 * j + 12])
-        op("s" if j else "v", ["rb", "lo30", "lo31"], ["am%d" % j], act(out, win) if j else copy(out, win))
+    def both_halves(name):
+        keys = []
+        for src in range(2):
+            for dst in range(2):
+                keys.append("%s%d%d" % (name, src, dst))
+                op("v", ["ca%d" % c for c in range(6)], [keys[-1]],
+                   ts(T[name][64 * dst:64 * dst + 64, 6 * src:6 * src + 6], T.ca[64 * src:64 * src + 64, NW - 1:6 * NW:NW], 0.5, E / 2.0, A.mult, A.add))
+        return keys
+
+    iof = both_halves("iof")
+    iff = both_halves("iff")
+    pick("x0", 0, E, ["x0m", "x0o"], "qm", 0, E + V, ["qm"], T.iof[:, 0:12], iof)
+    send_block("x0", 0, HR, "x0m", "ad0", "x0h")
+
+    op("g", [], ["uba"], iota(T.ub[:, 0:192], [[0, 192]], 0))
+    op("g", [], ["ubb"], iota(T.ub[:, 384:704], [[0, 320]], 0))
+    op("g", [], ["ytp"], iota(T.yt[:, 0:4 * PAIR], [[0, 4 * PAIR]], 0))
+
+    mark(1)
+    mark(2)
+    for h in range(N):
+        places(h)
+    op("s", iff, ["fb"], line(T.fl[:, 96:108], T.iff[:, 0:12], 0.25, UNIT - 0.375))
+    op("v", ["fb"], ["bo"], ts(T.bo[:], T.fl[:, 96:108], E - UNIT, None, A.add))
+    unpack_tile(0)
+    nodes = ("qb", E, 2 * E, ["qb"], "qm", 0, E + V, ["qm"], T.bo[:, 0:12], ["bo"])
+    op("s", ["ones"], ["xt0", "xt1", "xt2", "xt3", "xtc"], act(T.xt[:], ones[:, 0:512], scale=0.0))
+    chosen = T.iff[:, 0:16].indirect(T.so[:, 12:13])
+    for j, (d, c) in enumerate(((-1, 0), (2, 2), (1, 3))):
+        op("s", iff + ["iffp", "twice"], ["fa%d" % j], line(T.fl[:, 32 * j:32 * j + 32:2], chosen, 0.25, UNIT - 0.375))
+        op("s", iff + ["iffp", "twice"], ["fj%d" % j], line(T.fl[:, 32 * j + 1:32 * j + 32:2], chosen, -0.25, c + 0.375 - d / 4.0 - UNIT))
+    op("s", ["cum2%d" % h for h in range(N)] + ro, ["rb"], act(T.rb[:], T.cum2[:, 0:N * E].indirect(T.ro[:, 0:12])))
+    pick_codes(*nodes)
+    unpack_tile(1)
+    unpack_tile(2)
+    op("v", ["five"] + ["f%s%d" % (k, j) for k in "aj" for j in range(3)], ["sk"], scan(T.sj[:], T.five[:], T.fl[:, 0:96], 0.0, A.mult, A.add))
+    unpack_tile(3)
+    pick_scales(*nodes)
+    op("v", ["sk"], ["lo3"], ts(T.lo3[:], T.sj[:, 1:96:2], -4 * UNIT, None, A.add))
+
+    def gather_list(j, q):
+        out, w = T.am[:, E * j:E * j + E], T.rb[:, 0:E].indirect(T.lo3[:, 16 * j:16 * j + 12])
+        op(q, ["rb", "lo3"], ["am%d" % j], act(out, w) if q == "s" else copy(out, w))
 
     def turn_list(j):
         op("v", ["am%d" % j], ["asc%d" % j], lambda: vec.transpose(T.asc[:, E * j:E * j + E], T.am[:, E * j:E * j + E]))
 
     def cut_list(j):
-        op("v", ["asc%d" % j], ["ao%d" % j], ts(T.ao[:, 12 * j:12 * j + 12], T.asc[:, E * j:E * j + E:16], float(SHIFT), None, A.add))
+        op("v", ["asc%d" % j], ["ao%d" % j], ts(T.ao[:, 12 * j:12 * j + 12], T.asc[:, E * j:E * j + E:16], 0.0, None, A.add))
 
-    for j in range(3):
-        gather_list(j)
-    op("g", ["ones"], ["flip"], lambda: g.affine_select(T.flip[:], ones[:, 0:PAIR], [[1, PAIR]], A.not_equal, -1.0, 0, -1))
-    op("g", ["flip"], ["flip"], lambda: g.affine_select(T.flip[:], T.flip[:], [[1, PAIR]], A.not_equal, -1.0, PAIR, -1))
-    op("g", [], ["uba"], iota(T.ub[:, 0:192], [[0, 192]], 0))
-    op("g", [], ["ubb"], iota(T.ub[:, 384:704], [[0, 320]], 0))
-    op("g", [], ["ytp"], iota(T.yt[:, 4 * E:4 * YW], [[0, 4 * (YW - E)]], 0))
-    unpack_tile(2)
+    def cut_home(j):
+        op("v", ["asc%d" % j], ["ah%d" % j], ts(T.ao[:, 36 + 3 * j:39 + 3 * j], T.asc[:, E * j + FAR:E * j + E:16], 0.0, None, A.add))
+
+    gather_list(0, "v")
+    gather_list(1, "s")
+    gather_list(2, "s")
+    op("s", ["ez"], ["ezn"], act(T.ezn[:], T.ez[:], scale=-1.0))
     turn_list(0)
     turn_list(1)
-    unpack_tile(3)
     cut_list(0)
     turn_list(2)
     cut_list(1)
     minus_tile(0)
+    cut_list(2)
+    op("g", ["xtc"], ["xtc0", "gq"], iota(T.xt[96:97, 2:4 * NT:4], [[0, NT]], 1))
+    op("g", ["xtc"], ["xtc1", "gq"], iota(T.xt[96:97, 3:4 * 24:4], [[0, 2], [16, 12]], 0))
+    op("g", ["xtc"], ["xtc2", "gq"], iota(T.xt[64:65, 51:4 * NT:4], [[0, 9]], HR))
+    op("g", [], ["sel2"], iota(T.sel[:, 2:512:4], [[0, 8], [1, 16]], 0))
+    op("g", [], ["sel3"], iota(T.sel[:, 3:512:4], [[0, 128]], 1))
+    xt_keys = ["xt0", "xt1", "xt2", "xt3", "xtc", "xtc0", "xtc1", "xtc2"]
 
-    def sizes_tile():
-        for t in range(4):
-            op("s", ["ut", "ones"], ["ub%d" % t], act(T.ub[:, 192 + t:384:4], ones[:, 0:PAIR], ACT.Identity, bias=T.ut[:, t:t + 1], scale=0.0))
+    def limits(s):
+        op("v", ["krow", "gs%d" % s], ["kk%d" % s], ts(T.kk[:, NT * s:NT * s + NT], T.krow[:, 0:NT], pf[:, 15 + s:16 + s], OFFK, A.not_equal, A.mult))
+
+    def select_tile(s):
+        op("v", ["irow", "pf", "st1"], ["sel%d" % s], ts(T.sel[:, s:512:4], T.irow[:, 0:128], q16, steps if s else float(STEP), A.is_equal, A.mult))
 
     def edge_numbers(i):
         row = ("irow", "hrow")[i]
         op("s", [row] + iof, ["lh%d" % i], act(T.lh[:, E * i:E * i + E], T[row][:, 0:E].indirect(T.iof[:, 0:12])))
 
-    def edge_select():
-        for i in range(2):
-            for s in range(2):
-                a = slice(E * i + 96 * s, E * i + 96 * s + 96)
-                op("g", ["lh%d" % i], ["lhd%d%d" % (i, s)], lambda a=a: g.affine_select(T.lhd[:, a], T.lh[:, a], [[1, 96]], A.is_equal, 0.0, 0, -1))
+    def edge_select(i):
+        for s in range(2):
+            a = slice(E * i + 96 * s, E * i + 96 * s + 96)
+            op("g", ["lh%d" % i], ["lhd%d%d" % (i, s)], lambda a=a: g.affine_select(T.lhd[:, a], T.lh[:, a], [[1, 96]], A.is_equal, 0.0, 0, -1))
 
-    def edge_columns():
-        for i in (1, 0):
-            for s in range(2):
-                a = slice(E * i + 96 * s, E * i + 96 * s + 96)
-                op("s", ["lhd%d%d" % (i, s)], ["lhd%d%d" % (i, s), "lhc%d%d" % (i, s)],
-                   act(T.lhd[:, a], T.lhd[:, a], accum_out=T.lhc[:, 2 * i + s:2 * i + s + 1]))
+    def edge_columns(i):
+        for s in range(2):
+            a = slice(E * i + 96 * s, E * i + 96 * s + 96)
+            op("s", ["lhd%d%d" % (i, s), "gs"], ["lhd%d%d" % (i, s), "lhc%d%d" % (i, s)],
+               act(T.lhd[:, a], T.lhd[:, a], ACT.Identity, bias=spare, accum_out=T.lhc[:, 2 * i + s:2 * i + s + 1]))
 
     def edge_tiles(step):
         if step == 0:
@@ -361,210 +432,305 @@ def rank_program(g, core, T, topo):
                 op("v", ["irow", "lhc0%d" % s], ["sele%d" % s], ts(T.sele[:, s:512:4], T.irow[:, 0:128], T.lhc[:, s:s + 1], float(STEP), A.is_equal, A.mult))
         elif step == 1:
             for s in range(2):
-                op("v", ["krow", "lhc1%d" % s], ["k01e%d" % s], ts(T.k01e[:, 12 * s:12 * s + 12], T.krow[:, 0:12], T.lhc[:, 2 + s:3 + s], None, A.is_equal))
+                op("g", ["sele%d" % s], ["sele%d" % (2 + s)], lambda s=s: g.affine_select(
+                    T.sele[0:96, 2 + s:512:4], T.sele[0:96, s:512:4], [[0, 128]], A.is_ge, 0.0, 0, 0))
+        elif step == 2:
+            op("g", [], ["sele4", "gq"], iota(T.sele[96:128, 2:512:4], [[0, 8], [1, 16]], 0))
+            op("g", [], ["sele5", "gq"], iota(T.sele[96:128, 3:512:4], [[0, 128]], 1))
+        elif step == 3:
+            for s in range(2):
+                op("v", ["krow", "lhc1%d" % s], ["kke%d" % s], ts(T.kke[:, NE * s:NE * s + NE], T.krow[:], T.lhc[:, 2 + s:3 + s], OFFK, A.not_equal, A.mult))
         else:
-            quant("qse", 0, 128, T.sele[:], ["sele0", "sele1", "sele2", "sele3"], "qse")
-            op("v", ["k01e0", "k01e1"], ["k01e0", "k01e1"], lambda: vec.memset(T.k01e[96:128, :], 0.0))
+            quant("qse", 0, 128, T.sele[:], ["sele%d" % i for i in range(6)], "qse")
 
-    def slots(step):
+    def slots(step, k=0):
         if step == 0:
-            op("v", ["diag"], ["latch"], ts(T.latch[:], T.diag[:], 512.0, -256.0, A.mult, A.add))
+            op("v", ["irow", "pf"], ["latch"], ts(T.latch[:], T.irow[:], q16, 256.0, A.is_equal, A.mult))
+        elif step == 1:
             op("v", ro, ["k2"], ts(T.k2[:], T.ro[:], -(E - 1) / 2.0, 1.0 / E, A.add, A.mult))
-        elif step <= N:
-            h = step - 1
-            op("v", ["k2"], ["mk%d" % h], ts(T.mk[:, 12 * h:12 * h + 12], T.k2[:], float(h), None, A.is_equal))
+        elif step == 2:
+            op("v", ["k2", "hc%d" % k], ["mk%d" % k], ts(T.mk[:, 12 * k:12 * k + 12], T.k2[:], pf[:, 10 + k:11 + k], None, A.is_equal))
+        elif step == 3:
+            a = slice(E * k, E * k + E)
+            op("v", ["cum%d" % k, "latch"], ["lat%d" % k], scan(T.lat[:, a], T.latch[:], T.cum[:, a], 0.0, A.max, A.min))
+            op("s", ["lat%d" % k, "ci%d" % k], ["la%d" % k], line(T.mq[:, 12 * k:12 * k + 12], T.lat[:, E * k + 15:E * k + E:16], 1.0, pf[:, 8 + k:9 + k]))
+        elif step == 4:
+            op("v", ["la0", "la1", "mk0", "mk1"], ["mq"], tt(T.mq[:], T.mq[:], T.mk[:], A.mult))
         elif step == 5:
-            for h in range(N):
-                a = slice(E * h, E * h + E)
-                op("v", ["cum%d" % h, "latch"], ["lat%d" % h], scan(T.lat[:, a], T.latch[:], T.cum[:, a], 0.0, A.max, A.min))
+            op("v", ["mq"], ["f1"], tt(T.f1[:, 0:12], T.mq[:, 0:12], T.mq[:, 12:24], A.add))
         elif step == 6:
-            op("v", ["lat%d" % h for h in range(N)] + ["mk%d" % h for h in range(N)], ["mq"], tt(T.mq[:], T.lat[:, 15:N * E:16], T.mk[:], A.mult))
+            for k in range(2):
+                op("v", ["f1"], ["f2%d" % k], copy(T.f1[64 * k:64 * k + 64, 12:24], T.f1[64 - 64 * k:128 - 64 * k, 0:12]))
         elif step == 7:
-            op("v", ["mq"], ["f1"], tt(T.f1[:], T.mq[:, 0:24], T.mq[:, 24:48], A.add))
-        elif step == 8:
-            op("v", ["f1"], ["f2"], tt(T.f2[:], T.f1[:, 0:12], T.f1[:, 12:24], A.add))
+            op("v", ["f1", "f20", "f21"], ["f3"], tt(T.f1[:, 24:36], T.f1[:, 0:12], T.f1[:, 12:24], A.add))
         else:
-            op("v", ["f2"], ["so"], copy(T.so[:], T.f2[:]))
+            op("v", ["f3"], ["so"], copy(T.so[:, 0:12], T.f1[:, 24:36]))
 
-    def node_terms():
-        for b in range(4):
-            mm("pz", b, E, "qe", 128 * b, "qe%d" % b, "qb", 0, "qb", True, False)
+    def node_terms(n, banks=range(4)):
+        for b in banks:
+            mm("pz", b, n, "qe", 128 * b, "qe%d" % b, "qb", E, ["qb"], True, False)
 
-    def minus_held(t):
+    def minus_held(bank, t, n):
+        x = "x%d" % t
         for b in range(4):
-            mm("py", b, E, "qn", 128 * b, "qn%d" % b, "x%d" % t, MS, "x%dm" % t, True, False)
+            mm(bank, b, n, "qn", 128 * b, "qn%d" % b, x, 0, [x + "m", x + "o"], True, False)
 
-    def to_tile(tile, bank, scale):
-        for b in range(4):
-            src, dst = T[bank][:, 512 * b:512 * b + E], T[tile][:, b:4 * E:4]
-            if b % 2 == 0:
-                op("s", ["%s%d" % (bank, b)], ["%s%d" % (tile, b)], act(dst, src, scale=scale))
+    def to_tile(tile, at, key, bank, first, n, scale, queues, banks=range(4)):
+        for b in banks:
+            src, dst = T[bank][:, 512 * b + first:512 * b + first + n], T[tile][:, 4 * at + b:4 * (at + n):4]
+            keys = ["%s%d" % (k, b) for k in key]
+            if queues[b] == "s":
+                op("s", ["%s%d" % (bank, b)], keys, act(dst, src, scale=scale))
             else:
-                op("v", ["%s%d" % (bank, b)], ["%s%d" % (tile, b)], ts(dst, src, scale, None, A.mult))
+                op("v", ["%s%d" % (bank, b)], keys, ts(dst, src, scale, None, A.mult))
+
+    def four(*keys):
+        return ["%s%d" % (k, b) for k in keys for b in range(4)]
+
+    def weights(o):
+        quant("qw", 128 * o, 128 * o + 128, T.wt[:, 512 * o:512 * o + 512], ["wt"], "qw%d" % o)
 
     def products(name, a, key):
         for o in range(O):
-            mm("pz", o, E, "qw", 128 * o, "qw", name, a, key, True, True)
+            mm("pz", o, E, "qw", 128 * o, "qw%d" % o, name, a, [key], True, True)
 
-    def results(name, a, o, q):
-        src, dst = T.pz[:, 512 * o:512 * o + E], T[name][:, a:a + E]
-        op(q, ["pz%d" % o], ["%s_%d" % (name, a)], act(dst, src) if q == "s" else copy(dst, src))
+    def results(name, a, o):
+        op("s", ["pz%d" % o], ["%s_%d" % (name, a)], act(T[name][:, a:a + E], T.pz[:, 512 * o:512 * o + E]))
 
     def store_results(c, name, a, n, after):
         store("y", ["%s_%d" % (name, a + E * i) for i in range(n)] + after, T.y[:, c * E:(c + n) * E], T[name][:, a:a + n * E])
 
-    upe = T.yw[:, 5 * E:6 * E]
+    def compare(s, d, own, keys):
+        a = slice(PAIR * s, PAIR * s + PAIR)
+        op("v", keys, ["eq%d" % s], ts(T.eq[:, a], d, own, None, A.is_equal))
+        op("s", keys, ["sg%d" % s, "cnt%d" % s], act(T.sg[:, a], d, ACT.Sign, bias=own, scale=-1.0, accum_out=T.cnt[:, s:s + 1]))
 
-    def tally(t):
-        flags = T.wc[:, 0:LA].indirect(T["off%d" % t][:, 0:12])
-        if t == 0:
-            op("v", ["wc", "off0"], ["acc"], copy(T.acc[:], flags))
-        elif t < R - 1:
-            op("v", ["wc", "off%d" % t, "acc"], ["acc"], tt(T.acc[:], flags, T.acc[:], A.add))
-        else:
-            op("v", ["wc", "off%d" % t, "upe"], ["upo"], tt(T.upo[:], flags, upe, A.add))
+    def ties(s):
+        a = slice(PAIR * s, PAIR * s + PAIR)
+        op("v", ["eq%d" % s, "flip"], ["tie%d" % s], scan(T.tie[:, a], T.flip[:], T.eq[:, a], float(CAP), A.mult, A.add))
 
-    node_terms()
-    for t in range(R):
-        x, nx, qa, qo, off = "x%d" % t, "x%d" % (t + 1), "qa%d" % t, "qo%d" % t, T["off%d" % t]
-        last = t == R - 1
-        held = "qo%d" % (t - 1)
-        if t > 0:
-            px = "x%d" % (t - 1)
-            if t == 1:
-                slots(6)
-            pick(x, HR, HR + 3 * PAIR, x + "h", px, HR, XW, [px + "h", px + "c", px + "l"], T["lo%d" % (t - 1)][:, 0:9], ["lo%d" % (t - 1)])
+    def flags(s, out, key, kk, kkey):
+        op("v", ["cnt%d" % s, "tie%d" % s, kkey], [key],
+           ts(out, kk, T.cnt[:, s:s + 1], T.tie[:, PAIR * s + PAIR - 1:PAIR * s + PAIR], A.subtract, A.is_lt))
+
+    def taken(t, s):
+        op("s", ["xt%d" % s], ["was%d%d" % (t, s), "wj%d" % s], act(T.wj[:, 12 * s:12 * s + 12], T.xt[:, s:48:4], accum_out=T.was[:, 2 * t + s:2 * t + s + 1]))
+
+    def taken_before(step):
+        for s in range(2):
+            if step == 0:
+                op("s", ["was0%d" % s, "was1%d" % s], ["was%d" % s], line(T.was[:, 4 + s:5 + s], T.was[:, s:s + 1], 1.0, T.was[:, 2 + s:3 + s]))
+            else:
+                op("v", ["was%d" % s, "krow", "lhc1%d" % s], ["xt%d" % (2 + s)],
+                   ts(T.xt[:, 98 + s:4 * NE:4], T.krow[:, 0:12], T.lhc[:, 2 + s:3 + s], T.was[:, 4 + s:5 + s], A.is_equal, A.mult))
+
+    def sizes(bank, n):
+        a = E - n
+        mm(bank, 0, FAR, "qu", PAIR, "qu", "qb", a, ["qy"], True, False)
+        mm(bank, 0, max(n - PAIR, 128), "qu", 0, "qu", "qb", a + PAIR, ["qy", "qb"], False, True)
+        for s in range(2):
+            mm(bank, 1 + s, 128, "qb", a + 96 * s, "qy", "qu", PAIR, ["qu", "qb"], True, True)
+
+    def ranks(bank):
+        op("s", [bank + "0"], ["dd"], act(T.dd[:], T[bank][:, 0:144], ACT.Abs))
+        for s in range(2):
+            op("v", ["%s%d" % (bank, 1 + s)], ["nc%d" % s], lambda s=s: vec.tensor_reduce(
+                T.nc[:, s:s + 1], T[bank][:, 512 * (1 + s):512 * (1 + s) + 1], AxisListType.X, A.max, apply_absolute_value=True))
+        for s in range(2):
+            compare(s, T.dd[:, 96 * s:96 * s + PAIR], T.nc[:, s:s + 1], ["dd", "nc%d" % s])
+
+    def table_codes():
+        quant("qx", 0, 128, T.xt[:], xt_keys, "qx")
+
+    def table(bank, b, qs):
+        mm(bank, b, 128, qs, 0, qs, "qx", 0, ["qx"], True, True)
+
+    def terms(t, n, between):
+        x, qa = "x%d" % t, "qa%d" % t
         for j in range(3):
-            if t == 1:
-                slots(7 + j)
-            if t == 0 and j == 1:
-                cut_list(2)
-            pick(qa, E * j, E * j + E, "%s_%d" % (qa, j), x, 0, HR + 3 * PAIR, [x + "m", x + "h"], T.ao[:, 12 * j:12 * j + 12], ["ao%d" % j])
+            key = "%s_%d" % (qa, j)
+            pick(qa, n * j, n * j + n, [key], x, TW, HR + FAR, [x + k for k in "oh"], T.ao[:, 12 * j:12 * j + n // 16], ["ao%d" % j])
             for b in range(4):
-                mm("pz", b, E, "qe", 128 * b, "qe%d" % b, qa, E * j, "%s_%d" % (qa, j), False, j == 2)
-        if t == 0:
-            for b in range(1, 4):
-                minus_tile(b)
-            op("v", ["irow", "pf"], ["diag"], ts(T.diag[:], T.irow[:], q16, None, A.is_equal))
-            minus_held(0)
-            sizes_tile()
-        else:
-            pick(held, 0, E, held, x, MS, MS + E, [x + "m"], T.so[:, 0:12], ["so"])
-            if last:
-                edge_tiles(2)
-        to_tile("zt", "pz", 0.25)
-        quant(x, CA, CA + E, T.zt[:], ["zt0", "zt1", "zt2", "zt3"], x + "c")
-        if not last:
-            send_block(x, CA, LA, x + "c", "ad%d" % (t + 1))
-            landed([x + "l", x + "ls"], "ad%d" % (t + 1), arriving((True, False)))
-        for b in range(4):
-            mm("py", b, E, "qe", 128 * b, "qe%d" % b, x, CA, x + "c", False, True)
-        if t == 0:
-            for s in range(2):
-                op("s", ["diag"], ["sel%d" % s], act(T.sel[:, s:512:4], T.diag[:, 0:128], scale=float(STEP)))
-            table_rows("sel")
-            quant("qu", 0, 176, T.ub[:], ["uba", "ubb", "ub0", "ub1", "ub2", "ub3"], "qu")
-            k01(0)
-            k01(1)
-            op("g", [], ["wc"], iota(T.wc[:], [[1, 2], [0, LA // 2]], 0))
-            op("v", ["k010"], ["k010"], lambda: vec.memset(T.k01[96:128, 0:NT], 0.0))
-        else:
-            if not last:
-                quant("qw", 0, 128 * O, T.wt[:], ["wt"], "qw")
-            products(held, 0, held)
-        if t == 1:
-            edge_numbers(1)
-            edge_select()
-        if last:
-            pick(held, CA, CA + E, "qce", x, CA, CA + E, [x + "c"], T.so[:, 0:12], ["so"])
-        to_tile("yt", "py", 1.0)
-        quant("qy", 0, YW, T.yt[:], ["yt0", "yt1", "yt2", "yt3", "ytp"], "qy")
-        if t == 0:
-            op("s", ["k010", "k011"], ["kk"], act(T.kk[:], T.k01[:], ACT.Identity, bias=OFFK, scale=CAP - OFFK))
-            quant("qs", 0, 128, T.sel[:], ["sel0", "sel1", "sel2", "sel3"], "qs")
-            slots(0)
-        elif not last:
-            for o in range(O):
-                results("yb0", E * o, o, "s")
-            tally(0)
-        else:
-            op("s", ["k01e0", "k01e1"], ["kke"], act(T.kke[:], T.k01e[:], ACT.Identity, bias=OFFK, scale=CAP - OFFK))
-            for o in range(O):
-                results("yw", YP[o], o, "v" if o == 1 else "s")
-            store_results(O, "yw", YP[0], 2, [])
-            store_results(O + 2, "yw", YP[2], 1, [])
-        mm("py", 0, 144, "qu", PAIR, "qu", "qy", 0, "qy", True, False)
-        mm("py", 0, 144, "qu", 0, "qu", "qy", PAIR, "qy", False, True)
-        for s in range(2):
-            mm("py", 1 + s, 128, "qy", 96 * s, "qy", "qu", PAIR, "qu", True, True)
-        if last:
-            products(held, CA, "qce")
-        else:
-            node_terms()
-        op("s", ["py0"], ["dd"], act(T.dd[:], T.py[:, 0:144], ACT.Abs))
-        for s in range(2):
-            op("v", ["py%d" % (1 + s)], ["nc%d" % s], lambda s=s: vec.tensor_reduce(
-                T.nc[:, s:s + 1], T.py[:, 512 * (1 + s):512 * (1 + s) + 1], AxisListType.X, A.max, apply_absolute_value=True))
-        for s in range(2):
-            a, d, own = slice(PAIR * s, PAIR * s + PAIR), T.dd[:, 96 * s:96 * s + PAIR], T.nc[:, s:s + 1]
-            op("v", ["dd", "nc%d" % s], ["eq%d" % s], ts(T.eq[:, a], d, own, None, A.is_equal))
-            op("s", ["dd", "nc%d" % s], ["sg%d" % s, "cnt%d" % s], act(T.sg[:, a], d, ACT.Sign, bias=own, scale=-1.0, accum_out=T.cnt[:, s:s + 1]))
-        if t == 0:
-            slots(1)
-        if last:
-            for o in range(O):
-                results("yw", YP[o] + STEP, o, "s")
-            op("s", ["acc", "so"], ["upe"], act(upe, T.acc[:, 0:E].indirect(T.so[:, 0:12])))
-        for s in range(2):
-            a = slice(PAIR * s, PAIR * s + PAIR)
-            op("v", ["eq%d" % s, "flip"], ["tie%d" % s], scan(T.tie[:, a], T.flip[:], T.eq[:, a], 0.0, A.mult, A.add))
-        if t == 0:
-            slots(2)
-        kk, nt, qs = ("kke", 12, "qse") if last else ("kk", NT, "qs")
-        for s in range(2):
-            op("v", ["cnt%d" % s, "tie%d" % s, kk], ["xt%d" % s],
-               ts(T.xt[:, s:4 * nt:4], T[kk][:, nt * s:nt * s + nt], T.cnt[:, s:s + 1], T.tie[:, PAIR * s + PAIR - 1:PAIR * s + PAIR], A.subtract, A.is_lt))
-        if t == 0:
-            slots(3)
-        quant("qx", 0, 128, T.xt[:], ["xt0", "xt1", "xtc", "xtc0", "xtc1", "xtc2", "xtc3", "xtc4"], "qx")
-        if t == 0:
-            slots(4)
-        if t == 1:
-            edge_columns()
-            table_rows("sele")
-            edge_tiles(1)
-        mm("py", 3, 128, qs, 0, qs, "qx", 0, "qx", True, True)
-        op("v", ["py3"], ["off%d" % t], copy(off[:, 0:nt], T.py[:, 1536:1536 + nt]))
-        if last:
-            break
-        lo = T["lo%d" % t]
-        send(["off%d" % t], "af%d" % t, True,
-             [(off[:, 12 + 3 * i:15 + 3 * i], lo[:, 3 * blk(r, h):3 * blk(r, h) + 3]) for i, h in enumerate(others)])
-        landed(["lo%d" % t], "af%d" % t, arriving((True,)))
-        pick(nx, MS, MS + E, nx + "m", x, 0, LA, [x + "m", x + "h", x + "c"], off[:, 0:12], ["off%d" % t])
-        if t == 0:
-            edge_numbers(0)
-            slots(5)
-        else:
-            tally(t)
-            edge_tiles(0)
-        minus_held(t + 1)
-        if t > 0:
-            store_results(0, "yb0", 0, O, ["lo%d" % t])
+                mm("pz", b, n, "qe", 128 * b, "qe%d" % b, qa, n * j, [key], False, j == 2)
+            between(j)
 
-    both = ["yw_%d" % (a + d) for a in YP for d in (0, STEP)] + ["upe", "off%d" % t]
+    def home_sums(t, banks):
+        qa = "qa%d" % t
+        for b in banks:
+            for j in range(3):
+                mm("py", b, 128, "qe", 128 * b, "qe%d" % b, qa, 3 * FAR + PAIR * (j + 1) - 128, [qa + "_2", qa + "_h"], False, j == 2)
+
+    def home_nodes(banks):
+        for b in banks:
+            mm("py", b, 128, "qe", 128 * b, "qe%d" % b, "qb", E + LAST, ["qb"], True, False)
+
+    node_terms(FAR)
+    home_nodes(range(4))
+    for t in range(R - 1):
+        x, nx, qa, off, lo = "x%d" % t, "x%d" % (t + 1), "qa%d" % t, T["off%d" % t], T["lo%d" % t]
+        edge_order = ("qo0", 0, E, ["qo0"], x, 0, E, [x + "m", x + "o"], T.so[:, 0:12], ["so"])
+        terms(t, FAR, cut_home if t == 0 else lambda j: slots(6 + j))
+        pick(qa, 3 * FAR, 4 * FAR, [qa + "_h"], x, TW, HR + FAR, [x + k for k in "oh"], T.ao[:, 36:45], ["ah0", "ah1", "ah2"])
+        if t == 0:
+            minus_tile(1)
+            minus_tile(2)
+        else:
+            weights(1)
+        to_tile("zt", 0, ["zt"], "pz", 0, FAR, 0.25, "svsv")
+        home_sums(t, (0,))
+        if t == 0:
+            minus_tile(3)
+        else:
+            weights(2)
+        quant(x, CA, CA + FAR, T.zt[:, 0:4 * FAR], four("zt"), x + "c")
+        minus_held("pz", t, FAR)
+        send_block(x, CA, LA, x + "c", "ad%d" % (t + 1), x + "l")
+        to_tile("zt", FAR, ["zh"], "py", 128 - PAIR, PAIR, 0.25, "ssss", (0,))
+        if t == 0:
+            op("g", [], ["hrow"], iota(T.hrow[:], [[1, 12], [0, 16]], 0))
+            quant("qu", 0, 176, T.ub[:], ["uba", "ubb", "ub0", "ub1", "ub2", "ub3"], "qu")
+            select_tile(0)
+            select_tile(1)
+        else:
+            edge_tiles(2)
+            pick_codes(*edge_order)
+            edge_columns(0)
+        for b in range(4):
+            mm("pz", b, FAR, "qe", 128 * b, "qe%d" % b, x, CA, [x + "c"], False, True)
+        home_sums(t, (1, 2, 3))
+        to_tile("yt", 2 * PAIR, ["yt"], "pz", 0, FAR, 1.0, "svsv")
+        quant("qb", E - FAR, E, T.yt[:, 8 * PAIR:4 * (PAIR + E)], four("yt"), "qy")
+        to_tile("zt", FAR, ["zh"], "py", 128 - PAIR, PAIR, 0.25, "ssss", (1, 2, 3))
+        if t == 0:
+            limits(0)
+            limits(1)
+            quant("qs", 0, 128, T.sel[:], four("sel"), "qs")
+        else:
+            edge_tiles(0)
+        sizes("pz", FAR)
+        quant(x, XW - 128, XW, T.zt[:, 4 * LAST:4 * E], four("zt", "zh"), x + "d")
+        for b in range(4):
+            mm("py", b, 128, "qn", 128 * b, "qn%d" % b, x, LAST, [x + "m", x + "o"], True, False)
+        for b in range(4):
+            mm("py", b, 128, "qe", 128 * b, "qe%d" % b, x, XW - 128, [x + "d"], False, True)
+        ranks("pz")
+        to_tile("yt", PAIR, ["yh"], "py", 128 - PAIR, PAIR, 1.0, "ssss")
+        if t == 0:
+            node_terms(FAR, range(3))
+            slots(0)
+        for s in range(2):
+            ties(s)
+        for s in range(2):
+            flags(s, T.xt[:, s:4 * NT:4], "xt%d" % s, T.kk[:, NT * s:NT * s + NT], "kk%d" % s)
+        quant("qh", 0, 128, T.yt[:, 0:512], four("yt", "yh") + ["ytp"], "qh")
+        if t == 0:
+            home_nodes((2, 3))
+        else:
+            pick_scales(*edge_order)
+            edge_columns(1)
+        table_codes()
+        mm("pz", 3, 128, "qu", 0, "qu", "qh", 0, ["qh"], True, False)
+        mm("pz", 3, 128, "qh", 0, "qh", "qu", PAIR, ["qu"], False, True)
+        table("py", 0, "qs")
+        op("s", ["pz3"], ["dh"], act(T.dh[:, 0:PAIR + 1], T.pz[:, 1536 + PAIR - 1:1536 + 2 * PAIR], ACT.Abs))
+        if t > 0:
+            products("qo0", 0, "qo0")
+        else:
+            node_terms(FAR, (3,))
+            slots(1)
+        taken(t, 0)
+        compare(2, T.dh[:, 1:PAIR + 1], T.dh[:, 0:1], ["dh"])
+        op("v", ["py0"], ["off%d" % t], copy(off[:, 0:NT], T.py[:, 0:NT]))
+        send(["off%d" % t], "af%d" % t, True, [(off[:, 12 + 3 * i:15 + 3 * i], lo[:, 3 * i:3 * i + 3]) for i in range(N - 1)], ["lo%d" % t])
+        landed(["lo%d" % t], "af%d" % t, arriving((True,)))
+        ties(2)
+        if t == 0:
+            slots(2, 0)
+            slots(2, 1)
+            edge_numbers(0)
+        flags(2, T.xt[:, 37:48:4], "xt1", T.kk[:, NT + 9:NT + 12], "kk1")
+        table_codes()
+        pick(nx, 0, TW, [nx + "m"], x, 0, CA + TW, [x + k for k in "mohc"], off[:, 0:8], ["off%d" % t])
+        table("py", 1, "qs")
+        if t == 0:
+            home_nodes((0,))
+            slots(3, 0)
+            slots(3, 1)
+            weights(0)
+            edge_numbers(1)
+        else:
+            for o in range(O):
+                results("yb0", E * o, o)
+            node_terms(E)
+            edge_tiles(3)
+        op("v", ["py1", "off%d" % t], ["ofh%d" % t], copy(off[:, 9:12], T.py[:, 512 + 9:512 + 12]))
+        if t == 0:
+            home_nodes((1,))
+            edge_select(0)
+            edge_select(1)
+            slots(4)
+        else:
+            edge_tiles(1)
+            store_results(0, "yb0", 0, O, ["lo%d" % t])
+        taken(t, 1)
+        pick(nx, TW, E, [nx + "o"], x, 0, XW, [x + k for k in "mohcld"], off[:, 8:12], ["off%d" % t, "ofh%d" % t])
+        if t == 0:
+            slots(5)
+        pick(nx, HR, HR + FAR, [nx + "h"], x, 0, LA + FAR, [x + k for k in "mohcl"], lo[:, 0:9], ["lo%d" % t])
+
+    t = R - 1
+    x, held, qo, off = "x%d" % t, "qo%d" % (t - 1), "qo%d" % t, T["off%d" % t]
+    terms(t, E, lambda j: None)
+    minus_held("py", t, E)
+    pick(held, 0, E, [held], x, 0, E, [x + "m", x + "o"], T.so[:, 0:12], ["so"])
+    to_tile("zt", 0, ["zt", "zh"], "pz", 0, E, 0.25, "svsv")
+    quant(x, CA, CA + E, T.zt[:], four("zt"), x + "c")
+    taken_before(0)
+    for b in range(4):
+        mm("py", b, E, "qe", 128 * b, "qe%d" % b, x, CA, [x + "c"], False, True)
+    products(held, 0, held)
+    pick(held, CA, CA + E, ["qce"], x, CA, CA + E, [x + "c"], T.so[:, 0:12], ["so"])
+    to_tile("yt", PAIR, ["yt", "yh"], "py", 0, E, 1.0, "svsv")
+    quant("qb", 0, E, T.yt[:, 4 * PAIR:4 * (PAIR + E)], four("yt"), "qy")
+    edge_tiles(4)
+    taken_before(1)
     for o in range(O):
-        out, win = T.yb2[:, E * o:E * o + E], T.yw[:, YP[o]:YP[o] + LA].indirect(off[:, 0:12])
-        op("s" if o else "v", both, ["yb2_%d" % (E * o)], act(out, win) if o else copy(out, win))
-    pick(qo, 0, E, qo, held, 0, LA, [held, "qce"], off[:, 0:12], ["off%d" % t])
-    tally(t)
-    store_results(t * O, "yb2", 0, 1, [])
-    store_results(t * O + 1, "yb2", E, 1, [])
+        results("yw", YP[o], o)
+    store_results(O, "yw", YP[0], 2, [])
+    store_results(O + 2, "yw", YP[2], 1, [])
+    sizes("py", E)
+    products(held, CA, "qce")
+    ranks("py")
+    for o in range(O):
+        results("yw", YP[o] + STEP, o)
+    for s in range(2):
+        ties(s)
+    for s in range(2):
+        flags(s, T.xt[:, s:4 * NE:4], "xt%d" % s, T.kke[:, NE * s:NE * s + NE], "kke%d" % s)
+    table_codes()
+    table("py", 3, "qse")
+    op("v", ["py3"], ["off%d" % t], copy(off[:, 0:12], T.py[:, 1536:1536 + 12]))
+
+    both = ["yw_%d" % (a + d) for a in YP for d in (0, STEP)] + ["off%d" % t]
+
+    def final(q, o, a, z, key):
+        out, w = T.yb2[:, E * o + 16 * a:E * o + 16 * z], T.yw[:, YP[o]:YP[o] + STEP + E].indirect(off[:, a:z])
+        op(q, both, [key], act(out, w) if q == "s" else copy(out, w))
+
+    op("v", ["py3"], ["upt"], lambda: vec.transpose(T.upt[0:32, 0:32], T.py[0:32, 1536 + 24:1536 + 56]))
+    op("v", ["upt"], ["upo"], ts(T.upt[0:12, 32:48], T.upt[0:12, 0:16], 1.0 / STEP, None, A.mult))
+    for o in range(O):
+        final("v", o, 0, 6, "yb2_part%d" % o)
+        final("s", o, 6, 12, "yb2_%d" % (E * o))
+    pick(qo, 0, E, [qo], held, 0, CA + E, [held, "qce"], off[:, 0:12], ["off%d" % t])
+    for o in range(O):
+        store_results(t * O + o, "yb2", E * o, 1, ["yb2_part%d" % o])
     store("y", [qo], T.oc[:], T[qo][:, 0:E].bitcast(dt.uint8))
-    store_results(t * O + 2, "yb2", 2 * E, 1, [])
-    store("y", ["upo"], T.up[:], T.upo[0:1, :])
+    store("y", ["upo"], T.up[:], T.upt[0:12, 32:48])
     for k in range(4):
         store("s" if k % 2 else "y", [qo + "s"], T.osc[4 * k:4 * k + 4, :], T[qo + "s"][32 * k:32 * k + 4, :])
 
+    for i in ORDER:
+        plan[i][3]()
     for s in ("cv", "cs", "cp", "cg", "sent", "st"):
         g.wait_ge(T.sem[s], count[s])

from concourse.bass import DstId, RemoteDMATransfer
from concourse.mybir import dt, AluOpType, AxisListType, ActivationFunctionType

N, V, E, PAIR, CAP, R, O = 4, 48, 192, 48, 16, 3, 3
X4, U8, BF, F32, I32, U16 = "float8_e4m3fn_x4", "uint8", "bfloat16", "float32", "int32", "uint16"
FAR = (N - 1) * PAIR
STEP, HSTEP = 512, 896
HR, CA, LA, XW = E, STEP, E + STEP, E + HSTEP
TW = 128
LAST = E - 128
YP = (0, E, STEP + 2 * E)
NW = E - 2 * 16
OFFK = 128.0
NT, NE = 21, 36
UNIT = 136.0

ORDER = [int(_i) for _i in """
0 1 5 19 17 13 3 11 16 15 14 9 21 25 18 10 22 20 12 28 27 26 2 4 29 30 24 80 23 68 32 33 31 35 69 38 39 37 36 40 34 41
55 47 57 58 56 59 61 63 60 62 64 65 71 84 77 85 66 81 90 52 78 43 51 72 67 82 42 86 7 50 83 93 75 6 74 76 73 48 8 53 91
88 70 87 94 89 45 46 95 97 112 106 117 116 79 96 107 99 102 98 92 100 108 101 105 118 125 111 103 115 119 120 160 114
113 126 54 127 109 123 139 132 121 134 133 122 124 128 110 141 151 129 131 140 130 138 135 104 137 136 142 148 144 147
168 149 146 145 150 171 143 172 173 162 152 154 156 155 163 183 215 153 159 229 161 164 157 167 166 187 165 169 177 170
180 174 179 175 178 176 195 185 182 193 49 44 184 181 250 194 192 188 245 189 236 191 186 190 256 249 198 199 201 197
203 196 202 200 158 247 209 210 206 207 204 213 208 211 248 205 217 246 216 364 220 222 214 238 219 218 224 225 223 237
227 226 257 212 232 231 233 235 261 234 239 253 240 270 241 243 244 251 259 260 252 221 228 262 263 264 265 271 273 272
266 279 280 267 268 269 286 275 287 274 277 284 242 282 281 276 283 292 293 290 294 289 314 278 291 288 301 315 295 285
298 299 297 300 307 302 310 311 312 313 254 317 323 320 324 321 325 322 326 318 304 255 319 362 316 327 309 329 328 305
330 230 333 334 335 336 337 341 303 340 346 339 347 338 348 296 342 343 344 349 350 345 351 352 370 258 372 353 357 354
371 355 358 356 392 359 385 360 361 365 366 367 368 369 376 332 374 375 308 377 382 378 381 306 373 386 379 384 380 383
390 387 389 393 396 401 400 388 399 398 331 397 402 403 394 408 409 395 405 414 407 415 404 406 413 424 425 411 410 416
412 363 419 431 418 426 417 421 429 428 427 437 432 422 423 420 430 433 440 434 435 436 449 442 439 443 438 444 445 450
441 446 447 455 456 457 458 459 462 463 452 464 391 465 466 467 468 448 451 461 472 473 471 453 460 474 454 475 470 476
469 477 478 481 482 483 484 487 486 489 488 490 479 485 492 480 495 496 491 497 494 493
""".split()]

SCRATCH = {}


def _sb(name, n, d):
    SCRATCH[name] = ("sbuf", [128, n], d)


def _mx(name, n):
    _sb(name, n, X4)
    _sb(name + "s", n, U8)


for _n, _w, _d in (
        ("rt", 12, I32), ("mb", 4 * (E + V), BF), ("ut", 512, BF), ("wt", 1536, BF),
        ("ones", 516, BF), ("ez", 516, BF), ("ezn", 516, BF), ("irow", E, BF),
        ("latch", E, BF), ("pi", 6, I32), ("pf", 17, F32), ("thr", 6, F32),
        ("iff", 16, F32), ("five", 96, BF), ("fl", 108, BF), ("sj", 96, F32), ("lo3", 48, U16),
        ("ind", (N + 1) * E, BF), ("cum", 2 * E, BF), ("occ2", N * E, BF),
        ("cum2", N * E, BF), ("k2", 12, I32), ("mk", 24, F32), ("mq", 24, F32), ("ro", 12, U16),
        ("hit", 2 * E, BF), ("lat", 2 * E, BF), ("na", 4 * E, BF), ("nb", 2 * NW, BF), ("ca", 6 * NW, F32),
        ("f1", 36, F32), ("so", 14, U16), ("iof", 12, U16), ("bo", 12, U16), ("rb", E, BF), ("am", 3 * E, BF),
        ("asc", 3 * E, BF), ("ao", 46, U16), ("ub", 704, BF), ("sel", 512, BF), ("xt", 512, BF), ("flip", PAIR, BF),
        ("krow", NE, F32), ("kk", 2 * NT, F32),
        ("zt", 4 * E, BF), ("yt", 4 * (PAIR + E), BF), ("dd", 144, F32), ("dh", 50, F32), ("nc", 2, F32),
        ("sg", 3 * PAIR, BF), ("eq", 3 * PAIR, BF), ("tie", 3 * PAIR, F32), ("cnt", 3, F32), ("hrow", E, BF),
        ("lh", 2 * E, BF), ("lhd", 2 * E, BF), ("lhc", 4, F32), ("sele", 512, BF),
        ("kke", 2 * NE, F32), ("yw", YP[2] + STEP + E, F32), ("was", 6, F32), ("wj", 24, BF), ("upt", 48, F32)):
    _sb(_n, _w, _d)
for _n, _w in (("qm", E + V), ("qe", 512), ("qn", 512), ("qu", 176), ("qw", 384), ("qs", 128), ("qb", 2 * E),
               ("qh", 128), ("qx", 128), ("x0", XW), ("x1", XW), ("x2", CA + E), ("qo0", E), ("qo1", CA + E), ("qo2", E),
               ("qse", 128)):
    _mx(_n, _w)
for _t in range(R):
    _mx("qa%d" % _t, 3 * E)
    _sb("off%d" % _t, 22, U16)
for _t in range(R - 1):
    _sb("yb%d" % (2 * _t), O * E, F32)
    _sb("lo%d" % _t, 16, U16)
SCRATCH["pz"] = ("psum", [128, 2048], F32)
SCRATCH["py"] = ("psum", [128, 2048], F32)

SEMAPHORES = ["cv", "cs", "cp", "cg", "ldr", "ldm", "ldu", "ldw", "st", "sent", "ad0", "ad1", "ad2", "af0", "af1"]


def heads(r):
    near = r + 1 - 2 * (r % 2)
    rest = [h for h in range(N) if h not in (r, near)]
    return (rest[::-1] if near > r else rest) + [near, r]


def rank_program(g, core, T, topo):
    r = T.rank_of(core)
    if r is None:
        return
    A, ACT = AluOpType, ActivationFunctionType
    Q = {"v": g.vector, "s": g.scalar, "p": g.tensor, "g": g, "y": g.sync}
    SEM = {"v": "cv", "s": "cs", "p": "cp", "g": "cg"}
    count = {"cv": 0, "cs": 0, "cp": 0, "cg": 0, "st": 0, "sent": 0}
    known = {q: {} for q in Q}
    wrote, readers, plan = {}, {}, []

    def settle(q, reads, writes):
        need = []
        for k in reads:
            if k in wrote:
                need.append(wrote[k])
        for k in writes:
            bank = k[:2] in ("pz", "py")
            for tok in ([wrote[k]] if k in wrote else []) + readers.get(k, []):
                if not (bank and q == "p" and tok[0] == "cp"):
                    need.append(tok)
        need = [t for t in need if known[q].get(t[0], 0) < t[1]]
        top = {}
        for t in need:
            if t[0] not in top or top[t[0]][1] < t[1]:
                top[t[0]] = t
        for s in sorted(top):
            t = top[s]
            if any(o[2].get(s, 0) >= t[1] for o in top.values() if o is not t):
                continue
            Q[q].wait_ge(T.sem[s], t[1])
        for t in top.values():
            for s, c in list(t[2].items()) + [(t[0], t[1])]:
                if known[q].get(s, 0) < c:
                    known[q][s] = c

    def note(tok, reads, writes):
        for k in reads:
            readers.setdefault(k, []).append(tok)
        for k in writes:
            wrote[k] = tok
            readers[k] = []

    def op(q, reads, writes, call):
        writes = list(writes) + [k for k in reads if k[:2] in ("pz", "py")]
        if q == "g" and "gq" not in writes:
            reads = list(reads) + ["gq"]
        plan.append((q, list(reads), writes, lambda: compute(q, reads, writes, call)))

    def compute(q, reads, writes, call):
        settle(q, reads, writes)
        s = SEM[q]
        count[s] += 1
        call().then_inc(T.sem[s], 1)
        note((s, count[s], dict(known[q])), reads, writes)

    def load(q, sem, out, in_):
        Q[q].dma_start(out, in_).then_inc(T.sem[sem], 16)

    def store(q, reads, out, in_):
        def call():
            settle(q, reads, [])
            count["st"] += 16
            Q[q].dma_start(out, in_).then_inc(T.sem.st, 16)
        plan.append((q, list(reads), [], call))

    vec, sca, pe = g.vector, g.scalar, g.tensor

    def ts(out, in0, s1, s2, op0, op1=None):
        if op1 is None:
            return lambda: vec.tensor_scalar(out, in0, s1, None, op0)
        return lambda: vec.tensor_scalar(out, in0, s1, s2, op0, op1)

    def tt(out, in0, in1, o):
        return lambda: vec.tensor_tensor(out, in0, in1, o)

    def copy(out, in_):
        return lambda: vec.tensor_copy(out, in_)

    def act(out, in_, func=None, **kw):
        return lambda: sca.activation(out, in_, ACT.Copy if func is None else func, **kw)

    def line(out, in_, scale, bias):
        return act(out, in_, ACT.Identity, bias=bias, scale=scale)

    def scan(out, d0, d1, first, op0, op1):
        return lambda: vec.tensor_tensor_scan(out, d0, d1, first, op0, op1)

    def iota(out, pattern, base):
        return lambda: g.iota(out, pattern, base, 0, allow_small_or_imprecise_dtypes=True)

    def quant(name, a, b, tile, reads, key):
        op("v", reads, [key, key + "s"], lambda: vec.quantize_mx(T[name][:, a:b], T[name + "s"][:, a:b], tile))

    def pick_codes(dst, c, d, dkeys, src, a, b, skeys, off, okeys):
        op("v", skeys + okeys, dkeys, lambda: vec.tensor_copy(
            T[dst][:, c:d].bitcast(dt.uint32), T[src][:, a:b].bitcast(dt.uint32).indirect(off)))

    def pick_scales(dst, c, d, dkeys, src, a, b, skeys, off, okeys):
        op("s", [k + "s" for k in skeys] + okeys, [k + "s" for k in dkeys],
           act(T[dst + "s"][:, c:d], T[src + "s"][:, a:b].indirect(off)))

    def pick(*a):
        pick_codes(*a)
        pick_scales(*a)

    def mm(bank, b, n, lname, la, lkey, rname, ra, rkeys, start, stop):
        keys = [lkey] + rkeys
        op("p", keys + [k + "s" for k in keys], ["%s%d" % (bank, b)], lambda: pe.matmul_mx(
            T[bank][:, 512 * b:512 * b + n], T[lname][:, la:la + 128], T[lname + "s"][:, la:la + 128],
            T[rname][:, ra:ra + n], T[rname + "s"][:, ra:ra + n], start, stop))

    hd = heads(r)
    others = hd[:N - 1]

    def blk(src, dst):
        return heads(src).index(dst)

    def dest(h):
        rid, pid, _ = topo.addr(T.cores[h])
        return DstId(rid=rid, pnc=pid)

    def masks(src, first):
        out = []
        for i, h in enumerate(heads(src)[:N - 1]):
            eng = topo.engines(T.cores[src], T.cores[h])
            n = len(eng)
            part = [eng[:n // 2], eng[n // 2:3 * n // 4], eng[3 * n // 4:]] if first else \
                   [eng[n // 2:], eng[:n // 4], eng[n // 4:n // 2]]
            out.append(part[i])
        return out

    def send(reads, sem, first, pairs, lands):
        ms = masks(r, first)

        def call():
            settle("g", reads, [])
            count["sent"] += sum(len(m) for m in ms)
            g.remote_dma_fused([RemoteDMATransfer(dst_ids=[dest(h)], dma_engine_mask=sum(1 << e for e in ms[i]),
                                                  remote_sem=T.sem[sem], src=pairs[i][0], dst=pairs[i][1])
                                for i, h in enumerate(others)], local_sem=T.sem.sent)
        plan.append(("g", list(reads), ["out"] + lands, call))

    def arriving(firsts):
        return sum(len(masks(s, f)[blk(s, r)]) for s in others for f in firsts)

    def landed(keys, sem, n):
        for k in keys:
            wrote[k] = (sem, n, {})

    def send_block(name, a, z, key, sem, lands):
        c, s = T[name], T[name + "s"]
        at = [(a + PAIR * i, z + PAIR * i) for i in range(N - 1)]
        send([key], sem, True, [(c[:, i:i + PAIR].bitcast(dt.uint8), c[:, j:j + PAIR].bitcast(dt.uint8)) for i, j in at], [])
        send([key + "s"], sem, False, [(s[:, i:i + PAIR], s[:, j:j + PAIR]) for i, j in at], [lands, lands + "s"])
        landed([lands, lands + "s"], sem, arriving((True, False)))

    for k in range(2):
        load("y", "ldr", T.rt[32 * k:32 * k + 16, :], T.rev[:])
        load("s", "ldr", T.rt[32 * k + 16:32 * k + 32, :], T.rev[:])
    load("y", "ldm", T.mb[:, 0:4 * E], T.m[:])
    load("s", "ldm", T.mb[:, 4 * E:4 * E + 4 * V], T.b[:])
    load("y", "ldu", T.ut[:], T.u[:])
    load("y", "ldw", T.wt[:], T.w[:])
    landed(["rt"], "ldr", 64)
    landed(["mb"], "ldm", 32)
    landed(["ut"], "ldu", 16)
    landed(["wt"], "ldw", 16)

    ones, pf = T.ones, T.pf
    q16, odd, g16, half, pcol = (pf[:, i:i + 1] for i in range(5))
    steps, spare = pf[:, 13:14], pf[:, 14:15]
    op("g", [], ["pi4"], lambda: g.iota(T.pi[:, 4:5], [[0, 1]], 0, 1))
    op("v", [], ["ones"], lambda: vec.memset(ones[:], 1.0))
    op("g", [], ["c16"], iota(T.thr[:, 3:6], [[16, 3]], 0))
    op("g", ["ones"], ["ez"], lambda: g.affine_select(T.ez[:], ones[:], [[1, 516]], A.is_equal, 0.0, -3, -4))
    op("g", [], ["irow"], iota(T.irow[:], [[0, 12], [1, 16]], 0))
    op("g", [], ["five"], iota(T.five[:], [[0, 48], [5, 2]], 0))
    op("g", [], ["krow"], iota(T.krow[:], [[0, 3], [1, 12]], 0))
    op("g", ["ones"], ["flip"], lambda: g.affine_select(T.flip[:], ones[:, 0:PAIR], [[1, PAIR]], A.not_equal, -1.0, 0, -1))
    op("g", ["flip"], ["flip"], lambda: g.affine_select(T.flip[:], T.flip[:], [[1, PAIR]], A.not_equal, -1.0, PAIR, -1))
    win = [E if hd[1] > hd[0] else 0, E if hd[0] > hd[1] else 0]
    at = [win[0] // E + hd[0], win[0] // E + hd[2]]
    for k in range(N + 1):
        if k not in at:
            op("s", ["ones"], ["ind%d" % k], act(T.ind[:, E * k:E * k + E], ones[:, 0:E], scale=0.0))
    op("s", ["ones"], ["occ2b"], act(T.occ2[:, 2 * E:N * E], ones[:, 0:2 * E], scale=0.0))
    op("v", ["pi4"], ["pi0"], ts(T.pi[:, 0:1], T.pi[:, 4:5], 15, None, A.bitwise_and))
    op("v", ["pi4"], ["pi1"], ts(T.pi[:, 1:2], T.pi[:, 4:5], 4, 1, A.arith_shift_right, A.bitwise_and))
    op("v", ["pi4"], ["pi2"], ts(T.pi[:, 2:3], T.pi[:, 4:5], 4, None, A.arith_shift_right))
    op("v", ["pi4"], ["pi3"], ts(T.pi[:, 3:4], T.pi[:, 4:5], 6, None, A.arith_shift_right))
    op("v", ["pi4"], ["pi5"], ts(T.pi[:, 5:6], T.pi[:, 4:5], 14, None, A.bitwise_and))
    ind = ["ind%d" % k for k in range(N + 1) if k not in at]
    for i in range(2):
        for k in range(2):
            ind.append("ind%d%d" % (i, k))
            op("v", [], [ind[-1]], lambda i=i, k=k: vec.memset(T.ind[64 * k:64 * k + 64, E * at[i]:E * at[i] + E], float(i == k)))
        if i == 0:
            op("v", ["pi%d" % i for i in range(5)], ["pf"], copy(pf[:, 0:5], T.pi[:, 0:5]))
    op("v", ["c16", "pf"], ["thr"], ts(T.thr[:, 0:3], T.thr[:, 3:6], q16, -0.5, A.add, A.add))
    op("v", ["pi5", "pf"], ["twice"], ts(T.so[:, 12:13], T.pi[:, 5:6], odd, None, A.add))
    op("v", [], ["iffp"], lambda: vec.memset(T.iff[:, 12:16], 0.0))
    op("v", [], ["occ2a"], lambda: vec.memset(T.occ2[:, 0:2 * E], 0.0))

    def unpack_tile(b):
        quant("qe", 128 * b, 128 * b + 128, T.ez[:, 3 - b:515 - b], ["ez"], "qe%d" % b)

    def minus_tile(b):
        quant("qn", 128 * b, 128 * b + 128, T.ezn[:, 3 - b:515 - b], ["ezn"], "qn%d" % b)

    ro = ["ro0", "ro1"]

    def mark(k):
        op("v", ro + ["ones"], ["occ2a", "occ2b"], copy(T.occ2[:, 0:N * E].indirect(T.ro[:, 4 * k:4 * k + 4]), ones[:, 0:64]))

    def places(h):
        first = (FAR if h == r else HR + PAIR * blk(h, r)) - TW - 1
        op("v", ["occ2a", "occ2b", "ones"], ["cum2%d" % h],
           scan(T.cum2[:, E * h:E * h + E], ones[:, 0:E], T.occ2[:, E * h:E * h + E], float(first), A.mult, A.add))

    for k in range(2):
        op("v", ["rt"], [ro[k]], copy(T.ro[64 * k:64 * k + 64, :], T.rt[0:64, :]))
    for k in range(2):
        out, w = T.hit[:, E * k:E * k + E], T.ind[:, win[k]:win[k] + N * E].indirect(T.ro[:, 0:12])
        op("s" if k else "v", ro + ind, ["hit%d" % k], act(out, w) if k else copy(out, w))
    mark(0)
    for k in range(2):
        a = slice(E * k, E * k + E)
        op("v", ["hit%d" % k, "ones"], ["cum%d" % k], scan(T.cum[:, a], ones[:, 0:E], T.hit[:, a], -1.0, A.mult, A.add))
    for i, c in enumerate((1, 0, 2, 4)):
        k, a = c // 3, 16 if c % 3 == 1 else 0
        op("s", ["cum%d" % k, "thr"], ["ca%d" % c], act(T.na[:, E * i + a:E * i + E - a], T.cum[:, E * k + a:E * k + E - a], ACT.Sign,
                                                      bias=T.thr[:, c % 3:c % 3 + 1], scale=-1.0, accum_out=T.ca[:, NW * c + NW - 1:NW * c + NW]))
    for i in range(2):
        a = E + 32 * i
        op("v", ["cum1", "thr"], ["nb%d" % i], ts(T.nb[:, NW * i:NW * i + NW], T.cum[:, a:a + NW], T.thr[:, 2 * i:2 * i + 1], 2.0, A.is_lt, A.mult))
    for i in range(2):
        c = 3 + 2 * i
        op("v", ["nb%d" % i, "ones"], ["ca%d" % c], scan(T.ca[:, NW * c:NW * c + NW], ones[:, 0:NW], T.nb[:, NW * i:NW * i + NW], 64.0 * i - E, A.mult, A.add))
    op("s", ["pf"], ["st0"], act(pf[:, 12:13], pcol, ACT.Sign, bias=0.5 - PAIR))
    op("s", ["pf"], ["gs"], act(spare, pcol, ACT.Relu, bias=1.0 - 2 * PAIR))
    op("s", ["pf"], ["gs1"], line(pf[:, 16:17], g16, 1.0, 6.0))
    op("s", ["st0"], ["st1"], line(steps, pf[:, 12:13], (HSTEP - STEP) / 2.0, (HSTEP + STEP) / 2.0))
    op("s", ["gs"], ["gs0"], line(pf[:, 15:16], spare, 16.0, g16))
    for k in range(2):
        op("s", ["pf"], ["hc%d" % k], line(pf[:, 10 + k:11 + k], half, float(hd[2 + k] - hd[k]), float(hd[k])))
        op("s", ["pf"], ["ci%d" % k], line(pf[:, 8 + k:9 + k], half, 2.0 * PAIR, float(PAIR * k)))
    for t in range(4):
        op("s", ["ut", "ones"], ["ub%d" % t], line(T.ub[:, 192 + t:384:4], ones[:, 0:PAIR], 0.0, T.ut[:, t:t + 1]))
    quant("qm", 0, E + V, T.mb[:], ["mb"], "qm")

    def both_halves(name):
        keys = []
        for src in range(2):
            for dst in range(2):
                keys.append("%s%d%d" % (name, src, dst))
                op("v", ["ca%d" % c for c in range(6)], [keys[-1]],
                   ts(T[name][64 * dst:64 * dst + 64, 6 * src:6 * src + 6], T.ca[64 * src:64 * src + 64, NW - 1:6 * NW:NW], 0.5, E / 2.0, A.mult, A.add))
        return keys

    iof = both_halves("iof")
    iff = both_halves("iff")
    pick("x0", 0, E, ["x0m", "x0o"], "qm", 0, E + V, ["qm"], T.iof[:, 0:12], iof)
    send_block("x0", 0, HR, "x0m", "ad0", "x0h")

    op("g", [], ["uba"], iota(T.ub[:, 0:192], [[0, 192]], 0))
    op("g", [], ["ubb"], iota(T.ub[:, 384:704], [[0, 320]], 0))
    op("g", [], ["ytp"], iota(T.yt[:, 0:4 * PAIR], [[0, 4 * PAIR]], 0))

    mark(1)
    mark(2)
    for h in range(N):
        places(h)
    op("s", iff, ["fb"], line(T.fl[:, 96:108], T.iff[:, 0:12], 0.25, UNIT - 0.375))
    op("v", ["fb"], ["bo"], ts(T.bo[:], T.fl[:, 96:108], E - UNIT, None, A.add))
    unpack_tile(0)
    nodes = ("qb", E, 2 * E, ["qb"], "qm", 0, E + V, ["qm"], T.bo[:, 0:12], ["bo"])
    op("s", ["ones"], ["xt0", "xt1", "xt2", "xt3", "xtc"], act(T.xt[:], ones[:, 0:512], scale=0.0))
    chosen = T.iff[:, 0:16].indirect(T.so[:, 12:13])
    for j, (d, c) in enumerate(((-1, 0), (2, 2), (1, 3))):
        op("s", iff + ["iffp", "twice"], ["fa%d" % j], line(T.fl[:, 32 * j:32 * j + 32:2], chosen, 0.25, UNIT - 0.375))
        op("s", iff + ["iffp", "twice"], ["fj%d" % j], line(T.fl[:, 32 * j + 1:32 * j + 32:2], chosen, -0.25, c + 0.375 - d / 4.0 - UNIT))
    op("s", ["cum2%d" % h for h in range(N)] + ro, ["rb"], act(T.rb[:], T.cum2[:, 0:N * E].indirect(T.ro[:, 0:12])))
    pick_codes(*nodes)
    unpack_tile(1)
    unpack_tile(2)
    op("v", ["five"] + ["f%s%d" % (k, j) for k in "aj" for j in range(3)], ["sk"], scan(T.sj[:], T.five[:], T.fl[:, 0:96], 0.0, A.mult, A.add))
    unpack_tile(3)
    pick_scales(*nodes)
    op("v", ["sk"], ["lo3"], ts(T.lo3[:], T.sj[:, 1:96:2], -4 * UNIT, None, A.add))

    def gather_list(j, q):
        out, w = T.am[:, E * j:E * j + E], T.rb[:, 0:E].indirect(T.lo3[:, 16 * j:16 * j + 12])
        op(q, ["rb", "lo3"], ["am%d" % j], act(out, w) if q == "s" else copy(out, w))

    def turn_list(j):
        op("v", ["am%d" % j], ["asc%d" % j], lambda: vec.transpose(T.asc[:, E * j:E * j + E], T.am[:, E * j:E * j + E]))

    def cut_list(j):
        op("v", ["asc%d" % j], ["ao%d" % j], ts(T.ao[:, 12 * j:12 * j + 12], T.asc[:, E * j:E * j + E:16], 0.0, None, A.add))

    def cut_home(j):
        op("v", ["asc%d" % j], ["ah%d" % j], ts(T.ao[:, 36 + 3 * j:39 + 3 * j], T.asc[:, E * j + FAR:E * j + E:16], 0.0, None, A.add))

    gather_list(0, "v")
    gather_list(1, "s")
    gather_list(2, "s")
    op("s", ["ez"], ["ezn"], act(T.ezn[:], T.ez[:], scale=-1.0))
    turn_list(0)
    turn_list(1)
    cut_list(0)
    turn_list(2)
    cut_list(1)
    minus_tile(0)
    cut_list(2)
    op("g", ["xtc"], ["xtc0", "gq"], iota(T.xt[96:97, 2:4 * NT:4], [[0, NT]], 1))
    op("g", ["xtc"], ["xtc1", "gq"], iota(T.xt[96:97, 3:4 * 24:4], [[0, 2], [16, 12]], 0))
    op("g", ["xtc"], ["xtc2", "gq"], iota(T.xt[64:65, 51:4 * NT:4], [[0, 9]], HR))
    op("g", [], ["sel2"], iota(T.sel[:, 2:512:4], [[0, 8], [1, 16]], 0))
    op("g", [], ["sel3"], iota(T.sel[:, 3:512:4], [[0, 128]], 1))
    xt_keys = ["xt0", "xt1", "xt2", "xt3", "xtc", "xtc0", "xtc1", "xtc2"]

    def limits(s):
        op("v", ["krow", "gs%d" % s], ["kk%d" % s], ts(T.kk[:, NT * s:NT * s + NT], T.krow[:, 0:NT], pf[:, 15 + s:16 + s], OFFK, A.not_equal, A.mult))

    def select_tile(s):
        op("v", ["irow", "pf", "st1"], ["sel%d" % s], ts(T.sel[:, s:512:4], T.irow[:, 0:128], q16, steps if s else float(STEP), A.is_equal, A.mult))

    def edge_numbers(i):
        row = ("irow", "hrow")[i]
        op("s", [row] + iof, ["lh%d" % i], act(T.lh[:, E * i:E * i + E], T[row][:, 0:E].indirect(T.iof[:, 0:12])))

    def edge_select(i):
        for s in range(2):
            a = slice(E * i + 96 * s, E * i + 96 * s + 96)
            op("g", ["lh%d" % i], ["lhd%d%d" % (i, s)], lambda a=a: g.affine_select(T.lhd[:, a], T.lh[:, a], [[1, 96]], A.is_equal, 0.0, 0, -1))

    def edge_columns(i):
        for s in range(2):
            a = slice(E * i + 96 * s, E * i + 96 * s + 96)
            op("s", ["lhd%d%d" % (i, s), "gs"], ["lhd%d%d" % (i, s), "lhc%d%d" % (i, s)],
               act(T.lhd[:, a], T.lhd[:, a], ACT.Identity, bias=spare, accum_out=T.lhc[:, 2 * i + s:2 * i + s + 1]))

    def edge_tiles(step):
        if step == 0:
            for s in range(2):
                op("v", ["irow", "lhc0%d" % s], ["sele%d" % s], ts(T.sele[:, s:512:4], T.irow[:, 0:128], T.lhc[:, s:s + 1], float(STEP), A.is_equal, A.mult))
        elif step == 1:
            for s in range(2):
                op("g", ["sele%d" % s], ["sele%d" % (2 + s)], lambda s=s: g.affine_select(
                    T.sele[0:96, 2 + s:512:4], T.sele[0:96, s:512:4], [[0, 128]], A.is_ge, 0.0, 0, 0))
        elif step == 2:
            op("g", [], ["sele4", "gq"], iota(T.sele[96:128, 2:512:4], [[0, 8], [1, 16]], 0))
            op("g", [], ["sele5", "gq"], iota(T.sele[96:128, 3:512:4], [[0, 128]], 1))
        elif step == 3:
            for s in range(2):
                op("v", ["krow", "lhc1%d" % s], ["kke%d" % s], ts(T.kke[:, NE * s:NE * s + NE], T.krow[:], T.lhc[:, 2 + s:3 + s], OFFK, A.not_equal, A.mult))
        else:
            quant("qse", 0, 128, T.sele[:], ["sele%d" % i for i in range(6)], "qse")

    def slots(step, k=0):
        if step == 0:
            op("v", ["irow", "pf"], ["latch"], ts(T.latch[:], T.irow[:], q16, 256.0, A.is_equal, A.mult))
        elif step == 1:
            op("v", ro, ["k2"], ts(T.k2[:], T.ro[:], -(E - 1) / 2.0, 1.0 / E, A.add, A.mult))
        elif step == 2:
            op("v", ["k2", "hc%d" % k], ["mk%d" % k], ts(T.mk[:, 12 * k:12 * k + 12], T.k2[:], pf[:, 10 + k:11 + k], None, A.is_equal))
        elif step == 3:
            a = slice(E * k, E * k + E)
            op("v", ["cum%d" % k, "latch"], ["lat%d" % k], scan(T.lat[:, a], T.latch[:], T.cum[:, a], 0.0, A.max, A.min))
            op("s", ["lat%d" % k, "ci%d" % k], ["la%d" % k], line(T.mq[:, 12 * k:12 * k + 12], T.lat[:, E * k + 15:E * k + E:16], 1.0, pf[:, 8 + k:9 + k]))
        elif step == 4:
            op("v", ["la0", "la1", "mk0", "mk1"], ["mq"], tt(T.mq[:], T.mq[:], T.mk[:], A.mult))
        elif step == 5:
            op("v", ["mq"], ["f1"], tt(T.f1[:, 0:12], T.mq[:, 0:12], T.mq[:, 12:24], A.add))
        elif step == 6:
            for k in range(2):
                op("v", ["f1"], ["f2%d" % k], copy(T.f1[64 * k:64 * k + 64, 12:24], T.f1[64 - 64 * k:128 - 64 * k, 0:12]))
        elif step == 7:
            op("v", ["f1", "f20", "f21"], ["f3"], tt(T.f1[:, 24:36], T.f1[:, 0:12], T.f1[:, 12:24], A.add))
        else:
            op("v", ["f3"], ["so"], copy(T.so[:, 0:12], T.f1[:, 24:36]))

    def node_terms(n, banks=range(4)):
        for b in banks:
            mm("pz", b, n, "qe", 128 * b, "qe%d" % b, "qb", E, ["qb"], True, False)

    def minus_held(bank, t, n):
        x = "x%d" % t
        for b in range(4):
            mm(bank, b, n, "qn", 128 * b, "qn%d" % b, x, 0, [x + "m", x + "o"], True, False)

    def to_tile(tile, at, key, bank, first, n, scale, queues, banks=range(4)):
        for b in banks:
            src, dst = T[bank][:, 512 * b + first:512 * b + first + n], T[tile][:, 4 * at + b:4 * (at + n):4]
            keys = ["%s%d" % (k, b) for k in key]
            if queues[b] == "s":
                op("s", ["%s%d" % (bank, b)], keys, act(dst, src, scale=scale))
            else:
                op("v", ["%s%d" % (bank, b)], keys, ts(dst, src, scale, None, A.mult))

    def four(*keys):
        return ["%s%d" % (k, b) for k in keys for b in range(4)]

    def weights(o):
        quant("qw", 128 * o, 128 * o + 128, T.wt[:, 512 * o:512 * o + 512], ["wt"], "qw%d" % o)

    def products(name, a, key):
        for o in range(O):
            mm("pz", o, E, "qw", 128 * o, "qw%d" % o, name, a, [key], True, True)

    def results(name, a, o):
        op("s", ["pz%d" % o], ["%s_%d" % (name, a)], act(T[name][:, a:a + E], T.pz[:, 512 * o:512 * o + E]))

    def store_results(c, name, a, n, after):
        store("y", ["%s_%d" % (name, a + E * i) for i in range(n)] + after, T.y[:, c * E:(c + n) * E], T[name][:, a:a + n * E])

    def compare(s, d, own, keys):
        a = slice(PAIR * s, PAIR * s + PAIR)
        op("v", keys, ["eq%d" % s], ts(T.eq[:, a], d, own, None, A.is_equal))
        op("s", keys, ["sg%d" % s, "cnt%d" % s], act(T.sg[:, a], d, ACT.Sign, bias=own, scale=-1.0, accum_out=T.cnt[:, s:s + 1]))

    def ties(s):
        a = slice(PAIR * s, PAIR * s + PAIR)
        op("v", ["eq%d" % s, "flip"], ["tie%d" % s], scan(T.tie[:, a], T.flip[:], T.eq[:, a], float(CAP), A.mult, A.add))

    def flags(s, out, key, kk, kkey):
        op("v", ["cnt%d" % s, "tie%d" % s, kkey], [key],
           ts(out, kk, T.cnt[:, s:s + 1], T.tie[:, PAIR * s + PAIR - 1:PAIR * s + PAIR], A.subtract, A.is_lt))

    def taken(t, s):
        op("s", ["xt%d" % s], ["was%d%d" % (t, s), "wj%d" % s], act(T.wj[:, 12 * s:12 * s + 12], T.xt[:, s:48:4], accum_out=T.was[:, 2 * t + s:2 * t + s + 1]))

    def taken_before(step):
        for s in range(2):
            if step == 0:
                op("s", ["was0%d" % s, "was1%d" % s], ["was%d" % s], line(T.was[:, 4 + s:5 + s], T.was[:, s:s + 1], 1.0, T.was[:, 2 + s:3 + s]))
            else:
                op("v", ["was%d" % s, "krow", "lhc1%d" % s], ["xt%d" % (2 + s)],
                   ts(T.xt[:, 98 + s:4 * NE:4], T.krow[:, 0:12], T.lhc[:, 2 + s:3 + s], T.was[:, 4 + s:5 + s], A.is_equal, A.mult))

    def sizes(bank, n):
        a = E - n
        mm(bank, 0, FAR, "qu", PAIR, "qu", "qb", a, ["qy"], True, False)
        mm(bank, 0, max(n - PAIR, 128), "qu", 0, "qu", "qb", a + PAIR, ["qy", "qb"], False, True)
        for s in range(2):
            mm(bank, 1 + s, 128, "qb", a + 96 * s, "qy", "qu", PAIR, ["qu", "qb"], True, True)

    def ranks(bank):
        op("s", [bank + "0"], ["dd"], act(T.dd[:], T[bank][:, 0:144], ACT.Abs))
        for s in range(2):
            op("v", ["%s%d" % (bank, 1 + s)], ["nc%d" % s], lambda s=s: vec.tensor_reduce(
                T.nc[:, s:s + 1], T[bank][:, 512 * (1 + s):512 * (1 + s) + 1], AxisListType.X, A.max, apply_absolute_value=True))
        for s in range(2):
            compare(s, T.dd[:, 96 * s:96 * s + PAIR], T.nc[:, s:s + 1], ["dd", "nc%d" % s])

    def table_codes():
        quant("qx", 0, 128, T.xt[:], xt_keys, "qx")

    def table(bank, b, qs):
        mm(bank, b, 128, qs, 0, qs, "qx", 0, ["qx"], True, True)

    def terms(t, n, between):
        x, qa = "x%d" % t, "qa%d" % t
        for j in range(3):
            key = "%s_%d" % (qa, j)
            pick(qa, n * j, n * j + n, [key], x, TW, HR + FAR, [x + k for k in "oh"], T.ao[:, 12 * j:12 * j + n // 16], ["ao%d" % j])
            for b in range(4):
                mm("pz", b, n, "qe", 128 * b, "qe%d" % b, qa, n * j, [key], False, j == 2)
            between(j)

    def home_sums(t, banks):
        qa = "qa%d" % t
        for b in banks:
            for j in range(3):
                mm("py", b, 128, "qe", 128 * b, "qe%d" % b, qa, 3 * FAR + PAIR * (j + 1) - 128, [qa + "_2", qa + "_h"], False, j == 2)

    def home_nodes(banks):
        for b in banks:
            mm("py", b, 128, "qe", 128 * b, "qe%d" % b, "qb", E + LAST, ["qb"], True, False)

    node_terms(FAR)
    home_nodes(range(4))
    for t in range(R - 1):
        x, nx, qa, off, lo = "x%d" % t, "x%d" % (t + 1), "qa%d" % t, T["off%d" % t], T["lo%d" % t]
        edge_order = ("qo0", 0, E, ["qo0"], x, 0, E, [x + "m", x + "o"], T.so[:, 0:12], ["so"])
        terms(t, FAR, cut_home if t == 0 else lambda j: slots(6 + j))
        pick(qa, 3 * FAR, 4 * FAR, [qa + "_h"], x, TW, HR + FAR, [x + k for k in "oh"], T.ao[:, 36:45], ["ah0", "ah1", "ah2"])
        if t == 0:
            minus_tile(1)
            minus_tile(2)
        else:
            weights(1)
        to_tile("zt", 0, ["zt"], "pz", 0, FAR, 0.25, "svsv")
        home_sums(t, (0,))
        if t == 0:
            minus_tile(3)
        else:
            weights(2)
        quant(x, CA, CA + FAR, T.zt[:, 0:4 * FAR], four("zt"), x + "c")
        minus_held("pz", t, FAR)
        send_block(x, CA, LA, x + "c", "ad%d" % (t + 1), x + "l")
        to_tile("zt", FAR, ["zh"], "py", 128 - PAIR, PAIR, 0.25, "ssss", (0,))
        if t == 0:
            op("g", [], ["hrow"], iota(T.hrow[:], [[1, 12], [0, 16]], 0))
            quant("qu", 0, 176, T.ub[:], ["uba", "ubb", "ub0", "ub1", "ub2", "ub3"], "qu")
            select_tile(0)
            select_tile(1)
        else:
            edge_tiles(2)
            pick_codes(*edge_order)
            edge_columns(0)
        for b in range(4):
            mm("pz", b, FAR, "qe", 128 * b, "qe%d" % b, x, CA, [x + "c"], False, True)
        home_sums(t, (1, 2, 3))
        to_tile("yt", 2 * PAIR, ["yt"], "pz", 0, FAR, 1.0, "svsv")
        quant("qb", E - FAR, E, T.yt[:, 8 * PAIR:4 * (PAIR + E)], four("yt"), "qy")
        to_tile("zt", FAR, ["zh"], "py", 128 - PAIR, PAIR, 0.25, "ssss", (1, 2, 3))
        if t == 0:
            limits(0)
            limits(1)
            quant("qs", 0, 128, T.sel[:], four("sel"), "qs")
        else:
            edge_tiles(0)
        sizes("pz", FAR)
        quant(x, XW - 128, XW, T.zt[:, 4 * LAST:4 * E], four("zt", "zh"), x + "d")
        for b in range(4):
            mm("py", b, 128, "qn", 128 * b, "qn%d" % b, x, LAST, [x + "m", x + "o"], True, False)
        for b in range(4):
            mm("py", b, 128, "qe", 128 * b, "qe%d" % b, x, XW - 128, [x + "d"], False, True)
        ranks("pz")
        to_tile("yt", PAIR, ["yh"], "py", 128 - PAIR, PAIR, 1.0, "ssss")
        if t == 0:
            node_terms(FAR, range(3))
            slots(0)
        for s in range(2):
            ties(s)
        for s in range(2):
            flags(s, T.xt[:, s:4 * NT:4], "xt%d" % s, T.kk[:, NT * s:NT * s + NT], "kk%d" % s)
        quant("qh", 0, 128, T.yt[:, 0:512], four("yt", "yh") + ["ytp"], "qh")
        if t == 0:
            home_nodes((2, 3))
        else:
            pick_scales(*edge_order)
            edge_columns(1)
        table_codes()
        mm("pz", 3, 128, "qu", 0, "qu", "qh", 0, ["qh"], True, False)
        mm("pz", 3, 128, "qh", 0, "qh", "qu", PAIR, ["qu"], False, True)
        table("py", 0, "qs")
        op("s", ["pz3"], ["dh"], act(T.dh[:, 0:PAIR + 1], T.pz[:, 1536 + PAIR - 1:1536 + 2 * PAIR], ACT.Abs))
        if t > 0:
            products("qo0", 0, "qo0")
        else:
            node_terms(FAR, (3,))
            slots(1)
        taken(t, 0)
        compare(2, T.dh[:, 1:PAIR + 1], T.dh[:, 0:1], ["dh"])
        op("v", ["py0"], ["off%d" % t], copy(off[:, 0:NT], T.py[:, 0:NT]))
        send(["off%d" % t], "af%d" % t, True, [(off[:, 12 + 3 * i:15 + 3 * i], lo[:, 3 * i:3 * i + 3]) for i in range(N - 1)], ["lo%d" % t])
        landed(["lo%d" % t], "af%d" % t, arriving((True,)))
        ties(2)
        if t == 0:
            slots(2, 0)
            slots(2, 1)
            edge_numbers(0)
        flags(2, T.xt[:, 37:48:4], "xt1", T.kk[:, NT + 9:NT + 12], "kk1")
        table_codes()
        pick(nx, 0, TW, [nx + "m"], x, 0, CA + TW, [x + k for k in "mohc"], off[:, 0:8], ["off%d" % t])
        table("py", 1, "qs")
        if t == 0:
            home_nodes((0,))
            slots(3, 0)
            slots(3, 1)
            weights(0)
            edge_numbers(1)
        else:
            for o in range(O):
                results("yb0", E * o, o)
            node_terms(E)
            edge_tiles(3)
        op("v", ["py1", "off%d" % t], ["ofh%d" % t], copy(off[:, 9:12], T.py[:, 512 + 9:512 + 12]))
        if t == 0:
            home_nodes((1,))
            edge_select(0)
            edge_select(1)
            slots(4)
        else:
            edge_tiles(1)
            store_results(0, "yb0", 0, O, ["lo%d" % t])
        taken(t, 1)
        pick(nx, TW, E, [nx + "o"], x, 0, XW, [x + k for k in "mohcld"], off[:, 8:12], ["off%d" % t, "ofh%d" % t])
        if t == 0:
            slots(5)
        pick(nx, HR, HR + FAR, [nx + "h"], x, 0, LA + FAR, [x + k for k in "mohcl"], lo[:, 0:9], ["lo%d" % t])

    t = R - 1
    x, held, qo, off = "x%d" % t, "qo%d" % (t - 1), "qo%d" % t, T["off%d" % t]
    terms(t, E, lambda j: None)
    minus_held("py", t, E)
    pick(held, 0, E, [held], x, 0, E, [x + "m", x + "o"], T.so[:, 0:12], ["so"])
    to_tile("zt", 0, ["zt", "zh"], "pz", 0, E, 0.25, "svsv")
    quant(x, CA, CA + E, T.zt[:], four("zt"), x + "c")
    taken_before(0)
    for b in range(4):
        mm("py", b, E, "qe", 128 * b, "qe%d" % b, x, CA, [x + "c"], False, True)
    products(held, 0, held)
    pick(held, CA, CA + E, ["qce"], x, CA, CA + E, [x + "c"], T.so[:, 0:12], ["so"])
    to_tile("yt", PAIR, ["yt", "yh"], "py", 0, E, 1.0, "svsv")
    quant("qb", 0, E, T.yt[:, 4 * PAIR:4 * (PAIR + E)], four("yt"), "qy")
    edge_tiles(4)
    taken_before(1)
    for o in range(O):
        results("yw", YP[o], o)
    store_results(O, "yw", YP[0], 2, [])
    store_results(O + 2, "yw", YP[2], 1, [])
    sizes("py", E)
    products(held, CA, "qce")
    ranks("py")
    for o in range(O):
        results("yw", YP[o] + STEP, o)
    for s in range(2):
        ties(s)
    for s in range(2):
        flags(s, T.xt[:, s:4 * NE:4], "xt%d" % s, T.kke[:, NE * s:NE * s + NE], "kke%d" % s)
    table_codes()
    table("py", 3, "qse")
    op("v", ["py3"], ["off%d" % t], copy(off[:, 0:12], T.py[:, 1536:1536 + 12]))

    both = ["yw_%d" % (a + d) for a in YP for d in (0, STEP)] + ["off%d" % t]

    def final(q, o, a, z, key):
        out, w = T.yb2[:, E * o + 16 * a:E * o + 16 * z], T.yw[:, YP[o]:YP[o] + STEP + E].indirect(off[:, a:z])
        op(q, both, [key], act(out, w) if q == "s" else copy(out, w))

    op("v", ["py3"], ["upt"], lambda: vec.transpose(T.upt[0:32, 0:32], T.py[0:32, 1536 + 24:1536 + 56]))
    op("v", ["upt"], ["upo"], ts(T.upt[0:12, 32:48], T.upt[0:12, 0:16], 1.0 / STEP, None, A.mult))
    for o in range(O):
        final("v", o, 0, 6, "yb2_part%d" % o)
        final("s", o, 6, 12, "yb2_%d" % (E * o))
    pick(qo, 0, E, [qo], held, 0, CA + E, [held, "qce"], off[:, 0:12], ["off%d" % t])
    for o in range(O):
        store_results(t * O + o, "yb2", E * o, 1, ["yb2_part%d" % o])
    store("y", [qo], T.oc[:], T[qo][:, 0:E].bitcast(dt.uint8))
    store("y", ["upo"], T.up[:], T.upt[0:12, 32:48])
    for k in range(4):
        store("s" if k % 2 else "y", [qo + "s"], T.osc[4 * k:4 * k + 4, :], T[qo + "s"][32 * k:32 * k + 4, :])

    for i in ORDER:
        plan[i][3]()
    for s in ("cv", "cs", "cp", "cg", "sent", "st"):
        g.wait_ge(T.sem[s], count[s])
